import numpy as np, ml_dtypes
CORES = [35,38,43,46]
N = 4
BF = ml_dtypes.bfloat16
W, L, S, J, TB, D = 4096, 256, 16, 16, 3, 3
NE = (TB + 1) // 2 * L
def cands(u, k):
    return ((u * u >> 5)[..., None] + (2 * np.arange(J) + 1) * u[..., None] + k) & (W - 1)
def pairs(rng, n, pen):
    s = np.arange(W) % S
    kv = rng.random(W) + pen * ((s < TB) & (s % 2 == 0)); ky = rng.random(W) + pen * ((s < TB) & (s % 2 == 1))
    row = np.full(W, -1, np.int64); row[rng.permutation(np.argsort(kv)[:n])] = np.argsort(ky)[:n]
    return row
def filled(rng, lo, hi):
    return np.stack([np.stack([pairs(rng, int(W * (lo + (hi - lo) * rng.random())), 0.6) for g in range(8)]) for r in range(N)])
def pack(x, a, w):
    b = np.full((N, 8, W), -1, np.int64)
    for r in range(N):
        for g in range(8):
            v = np.flatnonzero(a[r, g] >= 0); b[(r + 1) % N, g, a[r, g, v]] = v
    return {"x": np.ascontiguousarray(x).reshape(N, 128, W).astype(np.float32).astype(BF), "pa": a.astype(np.int32), "pb": b.astype(np.int32), "wt": np.ascontiguousarray(w).reshape(N, 128, 1).astype(np.int32)}
def some(rng, m):
    us = np.flatnonzero(m)
    return int(us[int(rng.integers(0, us.size))]) if us.size else 0
def hashed(z, w, u):
    z = np.array(z); z[:2] = 0; rho = (u - int(np.sum(w * z))) & (W - 1); z[0] = rho & 255; z[1] = rho >> 8
    return z
def firststep(x, a, w, r):
    q = (r + 1) % N; v = S * np.arange(L); z = x[r][:, :, v]; u = np.sum(w[q][:, :, None] * z, axis=1) & (W - 1); c = cands(u, 0)
    col = np.take_along_axis(x[q], c.reshape(8, 1, L * J), 2).reshape(8, 16, L, J); key = np.sum(np.abs(col - z[..., None]), axis=1) * W + c
    y = np.take_along_axis(c, np.argmin(key, axis=2)[..., None], 2)[..., 0]; taken = np.zeros((8, W), bool)
    for g in range(8): taken[g, a[r, g][a[r, g] >= 0]] = True
    return y, (a[r][:, v] < 0) & ~np.take_along_axis(taken, y, 1), taken
def setup_inputs(rng):
    return pack(rng.integers(0, 256, (N, 8, 16, W)), filled(rng, 0.4, 0.85), rng.integers(1, 4096, (N, 8, 16)))
def setup_inputs_spread(rng):
    x = np.minimum(np.exp2(8 * rng.random((N, 8, 1, W))) * rng.random((N, 8, 16, W)) * 1.25, 255).astype(np.int64) * (rng.random((N, 8, 1, W)) > 0.0625)
    w = np.minimum(np.maximum(np.exp2(12 * rng.random((N, 8, 16))).astype(np.int64), 1), 4095)
    return pack(x, filled(rng, 0.05, 0.95), w)
def setup_inputs_ties(rng):
    recs = rng.integers(0, 256, (1, 8, 16, 12)); recs[..., 0] = 0; recs[..., 1] = 0; recs[:, :, 0, 1] = 1
    pick = rng.integers(0, 12, (N, 8, W)); w = rng.integers(1, 4096, (N, 8, 16)); w[:, :, 0] = 2048
    x = np.take_along_axis(np.ascontiguousarray(np.broadcast_to(recs, (N, 8, 16, 12))), pick[:, :, None, :], 3)
    return pack(x, filled(rng, 0.3, 0.9), w)
def setup_inputs_corners(rng):
    x = rng.integers(0, 256, (N, 8, 16, W)); col = rng.random((N, 8, 1, W)); x = np.where(col < 0.06, 0, np.where(col > 0.94, 255, x))
    w = rng.integers(1, 4096, (N, 8, 16)); k = rng.integers(0, 4, (N, 8, 1)); w = np.where(k == 0, 1, np.where(k == 1, 4095, w))
    off = int(rng.integers(0, 8)); a = np.full((N, 8, W), -1, np.int64); s = np.arange(W)
    for r in range(N):
        for g in range(8):
            m = (r + g + off) % 8
            if m == 1: a[r, g] = rng.permutation(W)
            elif m == 2: a[r, g] = pairs(rng, W - NE, 2.0)
            elif m == 3: a[r, g, np.delete(s, W - S)] = rng.permutation(W - 1)
            elif m == 4 or m == 5:
                v = np.flatnonzero(pairs(rng, W // 2 if m == 4 else 3 * W // 4, 0.6) >= 0); a[r, g, v] = v if m == 4 else W - 1 - v
            elif m == 6:
                a[r, g] = pairs(rng, 3 * W // 4, 2.0); rec = rng.integers(0, 256, (16, 1))
                for t in range(0, TB, 2): x[r, g][:, t::S] = rec
    tab = cands(np.arange(W), 0); starter = (s % S < TB) & (s % S % 2 == 0)
    for r in range(N):
        g = (7 - r - off) % 8; q = (r + 1) % N; w[q, g, 0] = 1; w[q, g, 1] = 256
        lanes = np.concatenate([np.arange(0, 32, 2 - r % 2), np.arange(32, 96)]); pl = np.where(lanes < 32, 97 + lanes, 128 + lanes)
        held = a[r - 1, g]; held = held[held >= 0]; held = held[held % S >= TB]; h = rng.permutation(held)[:lanes.size]
        row = np.full(W, -1, np.int64); row[h] = pl[:h.size]; fv = ~starter; fv[h] = False; fy = np.ones(W, bool); fy[96:129] = False; fy[160:224] = False
        row[rng.permutation(np.flatnonzero(fv))[:W // 2]] = rng.permutation(np.flatnonzero(fy))[:W // 2]; a[r, g] = row
        for e in range(h.size):
            k = int(lanes[e]); P = int(pl[e]); z = hashed(rng.integers(0, 256, 16), w[q, g], some(rng, np.any(tab == P, axis=1)))
            if k < 32: there = z; back = np.zeros(16, np.int64)
            else:
                kk = (k - 32) >> 1 if r % 2 == 1 else 2 * ((k - 32) >> 2)
                hit = ((tab + 97 + kk) & (W - 1)) == P; there = hashed(z, w[q, g], some(rng, np.any(hit, axis=1) & ~np.all(hit, axis=1))); back = there
            x[r, g][:, S * k] = z; x[q, g][:, P] = there; x[r, g][:, int(h[e])] = back
    for r in range(0, N, 2):
        g = (7 - r - off) % 8; y, go, taken = firststep(x, a, w, r); n = 0
        for b in range(8): n = n + int(np.unique(y[b][go[b]]).size)
        if n % 2 == 1:
            cnt = np.bincount(y[g][go[g]], minlength=W); one = np.flatnonzero(go[g] & (cnt[y[g]] == 1) & (np.arange(L) >= 96))
            fr = ~taken[g]; fr[y[g]] = False; fr[96:129] = False; fr[160:224] = False; fr = np.flatnonzero(fr)
            if one.size and fr.size: a[r, g, S * int(one[int(rng.integers(0, one.size))])] = int(fr[int(rng.integers(0, fr.size))])
    return pack(x, a, w)
def setup_inputs_ends(rng):
    kind = (7 - np.arange(8)[None, :] + N - 1 - np.arange(N)[:, None]) % 4
    w = np.where(rng.random((N, 8, 16)) < 0.5, 1, 4095); w[kind == 0] = 4095; w[kind == 3] = 1
    x = 255 * (rng.random((N, 8, 16, W)) < rng.choice(np.array([0.0, 0.25, 0.5, 0.75, 1.0]), (N, 8, 1, W))).astype(np.int64)
    pick = rng.random((N, 8, L)) < 0.25; pick[:, :, L - 1] = True; x[:, :, :, ::S] = np.where(pick[:, :, None, :], 255, x[:, :, :, ::S])
    tab = cands(np.arange(W), 0); top = np.max(tab, axis=1); pool = np.flatnonzero(top == np.max(top))
    a = np.full((N, 8, W), -1, np.int64); n = 3 * W // 8
    for r in range(N):
        for g in range(8):
            if kind[r, g] == 1:
                need = int(pool[int(rng.integers(0, pool.size))]) * 3839; i = int(rng.integers(0, 16)); o = (i + 1) % 16; w[r, g, i] = 0
                if (need - int(np.sum(w[r, g]))) & (W - 1) == 0: w[r, g, o] = 4096 - w[r, g, o]
                w[r, g, i] = (need - int(np.sum(w[r, g]))) & (W - 1)
            c = cands(np.array([255 * int(np.sum(w[r, g])) & (W - 1)]), 0)[0]; c = c[c % S != 0]
            if c.size:
                x[r, g][:, c] = 0
                if kind[r, g] == 2: x[r, g][:, int(np.max(c))] = 255
            v = rng.permutation(W); v = v[(v != 0) & (v != W - 1) & (v != W - S)][:n]; y = rng.permutation(W); y = y[(y != 0) & (y != W - 1)][:n]
            a[r, g, v] = y
            if g % 2 == 0: a[r, g, 0] = W - 1; a[r, g, W - 1] = 0
    return pack(x, a, w)
def setup_inputs_paths(rng):
    x = rng.integers(0, 256, (N, 8, 16, W)); w = rng.integers(1, 4096, (N, 8, 16)); w[:, :, 0] = 1; w[:, :, 1] = 256
    tab = cands(np.arange(W), 0); s = np.arange(W); gs = rng.permutation(8); lanes = np.argsort(rng.random((N, 8, L)), axis=-1); cnt = np.zeros((N, 8), np.int64)
    use = np.zeros((N, 8, W), bool); use[:, :, s % S < TB] = True; use[:, :, 1850:1920] = True; use[:, :, 3770:3840] = True
    for o in range(0, W, 1024): use[:, :, o + 96:o + 256] = True
    fv = [[[] for g in range(8)] for r in range(N)]; fy = [[[] for g in range(8)] for r in range(N)]; link = [[[] for g in range(8)] for r in range(N)]
    k0 = np.zeros(N, np.int64); k1 = np.zeros(N, np.int64)
    def start(r, g):
        v = S * int(lanes[r, g, cnt[r, g]]); cnt[r, g] += 1; fv[r][g].append(v)
        return v
    def spot(r, g):
        c = np.flatnonzero(~use[r, g]); p = int(c[int(rng.integers(0, c.size))]); use[r, g, p] = True
        return p
    def reach(r, g, k, v=None, u=0):
        z = rng.integers(0, 256, 16)
        for e in range(40):
            z = rng.integers(0, 256, 16)
            if v is not None: z = hashed(z, v, u)
            c = cands(np.array([int(np.sum(w[r, g] * z)) & (W - 1)]), k)[0]; c = c[~use[r, g, c]]
            if c.size:
                p = int(c[int(rng.integers(0, c.size))]); use[r, g, p] = True
                return z, p
        return z, -1
    def visit(r, g, P, rec, b):
        q = (r + 1) % N; m = np.any(tab == P, axis=1)
        if not np.any(m): return None
        z = hashed(rng.integers(0, 256, 16), w[q, g], some(rng, m)); v = start(r, g)
        if b < 0: b = spot(r, g)
        x[r, g][:, v] = z; x[q, g][:, P] = z; x[r, g][:, b] = rec; link[r][g].append((b, P))
        return z
    for r in range(N):
        q = (r + 1) % N; g = int(gs[0])
        for i in range(L):
            z, p = reach(q, g, 0)
            if p >= 0: x[r, g][:, S * i] = z; x[q, g][:, p] = z; fv[r][g].append(S * i); fy[r][g].append(p); k0[q] += 1
        g = int(gs[1]); xq = x[q, g]
        z = hashed(rng.integers(200, 256, 16), w[q, g], 4095); x[r, g][:, start(r, g)] = z; c = cands(np.array([4095]), 0)[0]
        j = 2 * int(rng.integers(1, J // 2)); xq[:, c] = 0; xq[5, c[j]] = 8; xq[5, c[j - 1]] = 8; fy[r][g].append(int(c[j])); fy[r][g].append(int(c[j - 1]))
        z = hashed(rng.integers(200, 256, 16), w[q, g], 2047); x[r, g][:, start(r, g)] = z; c = cands(np.array([2047]), 0)[0]
        xq[:, c] = 0; xq[6, c] = (int(np.sum(z)) - 4) & 15; xq[5, c[0]] = 1; fy[r][g].append(int(c[0])); k0[q] += 2
    ka = [int(k) & 31 for k in k0]
    for r in range(N):
        q = (r + 1) % N; g = int(gs[2])
        if q % 2 == 1:
            w[q, g, 2] = 0; need = (1024 + 2048 * int(rng.integers(0, 2))) * 3839
            if (need - int(np.sum(w[q, g]))) & (W - 1) == 0: w[q, g, 3] += 1 if w[q, g, 3] < 4095 else -1
            w[q, g, 2] = (need - int(np.sum(w[q, g]))) & (W - 1)
            if visit(r, g, 1024 + 97 + ka[q], np.full(16, 255, np.int64), -1) is not None:
                x[q, g][:, 3072 + 97 + ka[q]] = 0; fy[r][g].append(3072 + 97 + ka[q]); k1[q] += 1
        g = int(gs[4])
        if r % 2 == 1:
            for o in (0, 2048):
                rb, b = reach(r, g, 97 + ka[r], w[q, g], o); z, p = reach(r, g, 0)
                if b >= 0 and p >= 0 and visit(r, g, o + 97 + ka[q], rb, b) is not None:
                    fy[r][g].append(o + 194); v = start(r - 1, g); e = spot(r - 1, g)
                    x[r - 1, g][:, v] = z; x[r, g][:, p] = z; x[r - 1, g][:, e] = rb; link[r - 1][g].append((e, p)); fy[r - 1][g].append(b); k1[r] += 1
    kb = [int(k) & 31 for k in k1]
    for r in range(N):
        q = (r + 1) % N; g = int(gs[3])
        for o in (0, 2048):
            if visit(r, g, o + 97 + ka[q], hashed(rng.integers(0, 256, 16), w[q, g], o), -1) is not None: fy[r][g].append(o + 194 + kb[q])
        g = int(gs[5]); z1, p = reach(q, g, 97 + ka[q])
        if p >= 0:
            z = visit(r, g, 1024 + 194 + kb[q], z1, -1)
            if z is not None:
                z = hashed(z, w[q, g], 1024); b = spot(r, g); x[q, g][:, p] = z1; x[r, g][:, b] = z; link[r][g].append((b, p))
                x[q, g][:, 3072 + 194 + kb[q]] = np.where(z < 128, 255, 0); fy[r][g].append(3072 + 194 + kb[q])
    a = np.full((N, 8, W), -1, np.int64)
    for r in range(N):
        for g in range(8):
            mv = np.ones(W, bool); my = np.ones(W, bool); mv[np.array(fv[r][g], np.int64)] = False; my[np.array(fy[r][g], np.int64)] = False
            for v, y in link[r][g]: mv[v] = False; my[y] = False; a[r, g, v] = y
            vs = np.flatnonzero(mv); vs = np.concatenate([vs[vs % S == 0], rng.permutation(vs[vs % S != 0])[:W // 2]])
            a[r, g, vs] = rng.permutation(np.flatnonzero(my))[:vs.size]
    return pack(x, a, w)
def check_inputs(d):
    bad = []; xx = np.asarray(d["x"]).astype(np.float32)
    if not (np.min(xx) >= 0 and np.max(xx) <= 255): bad.append("range of x")
    if np.any(xx != np.floor(xx)): bad.append("x not whole")
    for k, lo, hi in (("pa", -1, W - 1), ("pb", -1, W - 1), ("wt", 1, 4095)):
        if not (np.min(d[k]) >= lo and np.max(d[k]) <= hi): bad.append("range of " + k)
    own = np.arange(W)[None, :]; off = False
    for r in range(N):
        a = np.asarray(d["pa"])[r].astype(np.int64); b = np.asarray(d["pb"])[(r + 1) % N].astype(np.int64)
        for c, e in ((a, b), (b, a)):
            if np.any((c >= 0) & (np.take_along_axis(e, np.clip(c, 0, W - 1), 1) != own)): off = True
    if off: bad.append("pa and pb not mutual")
    return bad
def reference(x, pa, pb, wt):
    X = x.astype(np.float32).astype(np.int32).reshape(N, 8, 16, W); A = pa.astype(np.int64); B = pb.astype(np.int64); w = wt.astype(np.int64).reshape(N, 8, 16, 1)
    kap = np.zeros(N, np.int64); lane = np.arange(L)
    for t in range(TB):
        q = (np.arange(N) + (1 if t % 2 == 0 else -1)) % N
        near, far = (A, B) if t % 2 == 0 else (B, A)
        v = S * lane + t; x0 = X[:, :, :, v]; z = x0; live = near[:, :, v] < 0; last = np.full((N, 8, L), -1, np.int64)
        for d in range(D):
            u = np.sum(w[q] * z, axis=2) & (W - 1)
            c = cands(u, (97 * d + kap[q])[:, None, None, None])
            col = np.take_along_axis(X[q], c.reshape(N, 8, 1, L * J), 3).reshape(N, 8, 16, L, J)
            dist = np.sum(np.abs(col - z[..., None]), axis=2)
            key = np.where(c == last[..., None], 2 ** 24, dist.astype(np.int64) * W + c)
            y = np.take_along_axis(c, np.argmin(key, axis=3)[..., None], 3)[..., 0]
            go = live & (np.take_along_axis(far[q], y, 2) < 0)
            rr, gg, ii = np.nonzero(go); low = np.full((N, 8, W), L, np.int64); np.minimum.at(low, (rr, gg, y[go]), ii)
            win = go & (np.take_along_axis(low, y, 2) == lane)
            rr, gg, ii = np.nonzero(win); yy = y[win]; qq = q[rr]; vv = S * ii + t
            X[qq, gg, :, yy] = (X[qq, gg, :, yy] + x0[rr, gg, :, ii]) >> 1
            far[qq, gg, yy] = vv; near[rr, gg, vv] = yy
            live = live & ~win; kap = np.bincount(qq, minlength=N).astype(np.int64) & 31; last = y
            p = np.maximum(np.take_along_axis(far[q], y, 2), 0)
            z = np.where(live[:, :, None, :], np.take_along_axis(X, p[:, :, None, :], 3), z)
    return {"yx": X.reshape(N, 128, W).astype(np.float32).astype(BF), "ya": A.astype(np.float32), "yb": B.astype(np.float32)}

@@ -1,0 +1,507 @@
+from concourse.bass import DstId, RemoteDMATransfer
+from concourse.mybir import dt, AluOpType, AxisListType, ActivationFunctionType
+import numpy as np
+
+W = 4096
+WX = 4608
+DEAD = 4096.0
+DUM = 4352
+NB, ND = 3, 3
+BAR = 4095.0 * 4096.0
+
+_B = {}
+
+
+def _sb(name, cols, dtype):
+    _B[name] = ("sbuf", [128, cols], dtype)
+
+
+_sb("X", WX, "bfloat16"); _sb("XC0", WX, "bfloat16"); _sb("XC1", WX, "bfloat16")
+_sb("TA", WX, "float32"); _sb("TB", WX, "float32")
+_sb("PAI", 256, "int32"); _sb("PBI", 256, "int32"); _sb("PF", 512, "float32"); _sb("PG4", 512, "float32")
+_sb("BI", 384, "int32"); _sb("BF", 448, "float32")
+_sb("WI", 8, "int32"); _sb("WF2", 8, "float32")
+_sb("CI5", 512, "int32"); _sb("CT1", 512, "int32"); _sb("CT2", 512, "int32"); _sb("CA", 512, "float32"); _sb("CB", 512, "float32")
+_sb("PI", 8, "int32"); _sb("PT", 16, "int32"); _sb("PC", 16, "float32"); _sb("CF", 512, "float32")
+_sb("MW", 512, "bfloat16"); _sb("WH", 512, "bfloat16"); _sb("WL", 512, "bfloat16")
+_sb("OB", 8, "bfloat16"); _sb("IDF", 128, "float32"); _sb("PEN", 128, "bfloat16"); _sb("ZB", 256, "bfloat16")
+_sb("DIAG", 256, "float32"); _sb("DG2", 256, "float32"); _sb("M1", 128, "float32"); _sb("RS1", 32, "float32")
+_sb("CL", 256, "float32"); _sb("CR", 256, "float32"); _sb("RC", 256, "float32"); _sb("TH2", 256, "float32")
+_sb("RHL", 24, "bfloat16")
+_sb("SRM", 512, "float32")
+_sb("GBH", 128, "bfloat16"); _sb("ONES", 128, "bfloat16")
+_sb("RS8", 256, "float32"); _sb("RS16", 256, "float32")
+_sb("LX1", 8, "uint16"); _sb("LX2", 16, "uint16"); _sb("LX3", 8, "uint16"); _sb("LX4", 16, "uint16"); _sb("LX5", 16, "uint16")
+_sb("LXI", 16, "int32"); _sb("LXJ", 16, "int32")
+_sb("SCOL", 4, "float32"); _sb("ABASE", 4, "float32"); _sb("ACOL", 4, "float32"); _sb("ATMP", 4, "float32")
+_sb("FBC", 16, "float32"); _sb("FB4C", 64, "float32")
+_sb("SSND", 256 * NB, "bfloat16"); _sb("SLAND", 256 * NB, "bfloat16")
+_sb("DSND", 16 * NB, "float32"); _sb("DLAND", 16 * NB, "float32")
+_sb("NSND", 256 * NB * ND, "bfloat16"); _sb("NLAND", 256 * NB * ND, "bfloat16")
+_sb("LSND", 16 * NB * ND, "uint16"); _sb("LLAND", 16 * NB * ND, "uint16")
+_sb("RSND", 16 * NB, "float32"); _sb("RLAND", 16 * NB, "float32")
+_sb("Z", 256, "bfloat16"); _sb("Z4", 1024, "bfloat16"); _sb("SH", 256, "float32")
+_sb("NI", 64, "int32"); _sb("UF", 64, "float32"); _sb("SQ", 256, "float32"); _sb("FI", 256, "int32"); _sb("CI", 256, "int32")
+_sb("OFF", 256, "uint16"); _sb("CFL", 256, "float32"); _sb("EQ", 256, "bfloat16")
+_sb("DF", 4096, "bfloat16"); _sb("AB", 4096, "bfloat16")
+_sb("R", 256, "float32"); _sb("E1", 128, "float32"); _sb("R4", 128, "float32")
+_sb("MN", 16, "float32"); _sb("YI", 16, "int32"); _sb("YA", 16, "int32"); _sb("YQ", 16, "float32"); _sb("YU", 16, "uint16")
+_sb("FB", 16, "float32"); _sb("FB4", 64, "float32"); _sb("L1", 64, "float32"); _sb("L2", 64, "int32"); _sb("LAST", 64, "int32")
+_sb("QL", 256, "bfloat16"); _sb("QR", 256, "bfloat16"); _sb("QE", 256, "bfloat16"); _sb("QO", 256, "bfloat16")
+_sb("TT", 256, "float32"); _sb("T2", 256, "float32"); _sb("FL", 16, "float32"); _sb("JK", 256, "bfloat16")
+_sb("E2", 256, "bfloat16"); _sb("LF", 16, "float32"); _sb("UP", 256, "float32"); _sb("PG", 256, "float32")
+_sb("DM", 256, "float32"); _sb("SC", 256, "float32"); _sb("PU", 16, "uint16"); _sb("E3", 256, "float32"); _sb("E4", 256, "bfloat16")
+_sb("W1", 16, "float32"); _sb("W2", 16, "float32"); _sb("W3", 16, "float32"); _sb("WB", 16, "bfloat16")
+_sb("DEADL", 16, "float32"); _sb("RES", 16, "float32"); _sb("KP", 8, "float32"); _sb("KI", 8, "int32")
+for _n in ["G0", "G1", "G2", "G3", "G4", "G5", "K6", "C7"]:
+    _B[_n] = ("psum", [128, 512], "float32")
+_B["BD"] = ("dram", [14, 128, 32], "float32")
+_B["PD"] = ("dram", [4, 128, 256], "float32")
+SCRATCH = _B
+
+_MSG = []
+for _t in range(NB):
+    _MSG += ["s%d" % _t, "b%d" % _t, "e%d" % _t, "r%d" % _t]
+    for _d in range(ND - 1):
+        _MSG += ["n%d%d" % (_t, _d), "l%d%d" % (_t, _d)]
+SEMAPHORES = ["cv", "cs", "cp", "cg"] + ["rx" + m for m in _MSG] + ["tx" + m for m in _MSG] + ["dm%d" % i for i in range(24)]
+
+
+def rank_program(g, core, T, topo):
+    rank = T.rank_of(core)
+    if rank is None:
+        return
+    A = AluOpType
+    F = ActivationFunctionType
+    RH, RL0, RL1 = T.RHL[:, 0:8], T.RHL[:, 8:16], T.RHL[:, 16:24]
+    GB, SR15, SR14, SRN = [T.SRM[:, 128 * i:128 * i + 128] for i in range(4)]
+    n_ranks = len(T.cores)
+    Q = {"v": g.vector, "s": g.scalar, "p": g.tensor, "g": g, "y": g.sync}
+    cnt = {"v": 0, "s": 0, "p": 0, "g": 0}
+    waited = {q: {} for q in Q}
+    wr = {}
+    rd = {}
+    nd = [0]
+    last = {}
+
+    def need(q, toks):
+        for sem in sorted(toks):
+            if waited[q].get(sem, 0) < toks[sem]:
+                Q[q].wait_ge(T.sem[sem], toks[sem])
+                waited[q][sem] = toks[sem]
+
+    def deps(reads, writes):
+        toks = {}
+        for k in reads:
+            for s, v in wr.get(k, {}).items():
+                toks[s] = max(toks.get(s, 0), v)
+        for k in writes:
+            for m in (wr, rd):
+                for s, v in m.get(k, {}).items():
+                    toks[s] = max(toks.get(s, 0), v)
+        return toks
+
+    def note(reads, writes, sem, val):
+        for k in writes:
+            wr[k] = {sem: val}
+            rd[k] = {}
+        for k in reads:
+            if k not in writes:
+                m = rd.setdefault(k, {})
+                m[sem] = max(m.get(sem, 0), val)
+        last[sem] = max(last.get(sem, 0), val)
+
+    def op(q, fns, reads, writes):
+        need(q, deps(reads, writes))
+        for fn in (fns if isinstance(fns, list) else [fns]):
+            cnt[q] += 1
+            fn().then_inc(T.sem["c" + q], 1)
+        note(reads, writes, "c" + q, cnt[q])
+
+    def dma(q, pieces, reads, writes):
+        need(q, deps(reads, writes))
+        sem = "dm%d" % nd[0]
+        nd[0] += 1
+        for out, in_ in pieces:
+            Q[q].dma_start(out, in_).then_inc(T.sem[sem], 16)
+        note(reads, writes, sem, 16 * len(pieces))
+
+    def engs(src, dst):
+        e = topo.engines(src, dst)
+        m = 0
+        for x in e:
+            m |= 1 << x
+        return m, len(e)
+
+    def send(to, msg, out, in_, reads):
+        need("g", deps(reads, []))
+        dst = T.cores[to]
+        rid, pid, _se = topo.addr(dst)
+        m, n = engs(core, dst)
+        g.remote_dma(out, in_, T.sem["rx" + msg], T.sem["tx" + msg], pid, rid, m)
+        note(reads, [], "tx" + msg, n)
+
+    def landed(frm, msg, keys):
+        n = engs(T.cores[frm], core)[1]
+        note([], keys, "rx" + msg, n)
+
+    def ts(out, in0, s1, o0, r, w, s2=None, o1=None):
+        if o1 is None:
+            op("v", lambda: g.vector.tensor_scalar(out, in0, s1, None, o0), r, w)
+        else:
+            op("v", lambda: g.vector.tensor_scalar(out, in0, s1, s2, o0, o1), r, w)
+
+    def tt(out, a, b, o, r, w):
+        op("v", lambda: g.vector.tensor_tensor(out, a, b, o), r, w)
+
+    def cp(out, a, r, w):
+        op("v", lambda: g.vector.tensor_copy(out, a), r, w)
+
+    def scan(out, d0, d1, o0, o1, r, w):
+        op("v", lambda: g.vector.tensor_tensor_scan(out, d0, d1, 0.0, o0, o1), r, w)
+
+    def ms(ap, c, w):
+        op("v", lambda: g.vector.memset(ap, c), [], w)
+
+    def act(out, in_, f, r, w, **kw):
+        op("s", lambda: g.scalar.activation(out, in_, f, **kw), r, w)
+
+    def mm(out, lhsT, rhs, start, stop):
+        return lambda: g.tensor.matmul(out, lhsT, rhs, start, stop)
+
+    dma("y", [(T.X[:, 0:W], T.x[:])], [], ["X"])
+    dma("s", [(T.WI[:, 0:1], T.wt[:])], [], ["WI"])
+    dma("s", [(T.PBI[:], T.pb[:])], [], ["PBI"])
+    dma("s", [(T.PAI[:], T.pa[:])], [], ["PAI"])
+    op("g", lambda: g.iota(T.PI[:, 0:1], [[0, 1]], 0, 1), [], ["PI"])
+    op("g", lambda: g.iota(T.CI5[:], [[1, 512]], 0, 0), [], ["CI5"])
+    op("g", lambda: g.iota(T.BI[:, 0:32], [[1, 32]], 0, 32), [], ["BI0"])
+    PSH = [(0, "s", 4), (1, "a", 15), (2, "a", 3), (3, "s", 2), (5, "a", 1)]
+    for c, k, v in PSH:
+        ts(T.PT[:, c:c + 1], T.PI[:, 0:1], v, A.arith_shift_right if k == "s" else A.bitwise_and, ["PI"], ["PT%d" % c])
+    ts(T.PT[:, 4:5], T.PI[:, 0:1], 4, A.arith_shift_right, ["PI"], ["PT4"], 1, A.bitwise_and)
+    cp(T.PC[:, 0:4], T.PT[:, 0:4], ["PT0", "PT1", "PT2", "PT3"], ["PC0"])
+    cp(T.PC[:, 4:5], T.PI[:, 0:1], ["PI"], ["PC4"])
+    PGRP, PLOW, PL3, PS2, PP = T.PC[:, 0:1], T.PC[:, 1:2], T.PC[:, 2:3], T.PC[:, 3:4], T.PC[:, 4:5]
+    ts(T.WI[:, 2:3], T.WI[:, 0:1], 3840, A.bitwise_and, ["WI"], ["WI2"])
+    ts(T.WI[:, 3:4], T.WI[:, 0:1], 255, A.bitwise_and, ["WI"], ["WI3"])
+    ts(T.WF2[:, 0:2], T.WI[:, 2:4], 1.0 / 4096, A.mult, ["WI2", "WI3"], ["WF2"])
+    ts(T.CT1[:], T.CI5[:], 4, A.arith_shift_right, ["CI5"], ["CT1"], 7, A.bitwise_and)
+    ts(T.CA[:], T.CT1[:], PGRP, A.is_equal, ["CT1", "PC0"], ["CA"])
+    ts(T.CT1[:], T.CI5[:], 2, A.arith_shift_right, ["CI5"], ["CT1"], 3, A.bitwise_and)
+    ts(T.CT2[:], T.CI5[:], 7, A.arith_shift_right, ["CI5"], ["CT2"])
+    tt(T.CB[:], T.CT1[:], T.CT2[:], A.is_equal, ["CT1", "CT2"], ["CB"])
+    tt(T.MW[:], T.CA[:], T.CB[:], A.mult, ["CA", "CB"], ["MW"])
+    ts(T.WH[:], T.MW[:], T.WF2[:, 0:1], A.mult, ["MW", "WF2"], ["WH"])
+    ts(T.WL[:], T.MW[:], T.WF2[:, 1:2], A.mult, ["MW", "WF2"], ["WL"])
+    nxt, prv = (rank + 1) % n_ranks, (rank - 1) % n_ranks
+
+    def start_batch(t):
+        to = nxt if t % 2 == 0 else prv
+        act(T.SSND[:, 256 * t:256 * t + 256], T.X[:, t:W:16], F.Copy, ["X"], ["SSND%d" % t])
+        send(to, "s%d" % t, T.SLAND[:, 256 * t:256 * t + 256], T.SSND[:, 256 * t:256 * t + 256], ["SSND%d" % t])
+        xc = T.XC0 if t % 2 == 0 else T.XC1
+        send(to, "b%d" % t, xc[:, 0:W], T.X[:, 0:W], ["X"])
+        frm = prv if t % 2 == 0 else nxt
+        landed(frm, "s%d" % t, ["SLAND%d" % t])
+
+    start_batch(0)
+    cp(T.CF[:], T.CI5[:], ["CI5"], ["CF"])
+    ts(T.PT[:, 8:9], T.PT[:, 2:3], 1, A.mult, ["PT2"], ["PT8"])
+    for ch in range(4):
+        ts(T.SCOL[:, ch:ch + 1], PL3, 32.0, A.mult, ["PC0"], ["SCOL"], 128.0 * ch + 16.0, A.add)
+    tt(T.ATMP[:], T.SCOL[:], T.SCOL[:], A.mult, ["SCOL"], ["ATMP"])
+    ts(T.ABASE[:], T.ATMP[:], -1.0, A.mult, ["ATMP"], ["ABASE"], 262144.0 - 12.0, A.add)
+    ts(T.ACOL[:], T.ABASE[:], 0.0, A.add, ["ABASE"], ["ACOL"])
+    ms(T.X[:, W:WX], 0.0, ["Xd"])
+    wr["X"] = deps(["X", "Xd"], [])
+    for f in range(1, 12):
+        ts(T.BI[:, 32 * f:32 * f + 32], T.BI[:, 0:32], f, A.arith_shift_right, ["BI0"], ["BI%d" % f], 1, A.bitwise_and)
+    ts(T.BI[:, 0:32], T.BI[:, 0:32], 1, A.bitwise_and, ["BI0"], ["BI0"])
+    ts(T.BF[:, 0:384], T.BI[:], 2.0, A.mult, ["BI%d" % f for f in range(12)], ["BFA"], -1.0, A.add)
+    ms(T.BF[:, 384:448], 1.0, ["BFB"])
+    dma("y", [(T.BD[f], T.BF[:, 32 * f:32 * f + 32]) for f in range(14)], ["BFA", "BFB"], ["BD"])
+    cp(T.PF[:, 0:256], T.PBI[:], ["PBI"], ["PF0"])
+    ts(T.PG4[:, 0:256], T.PBI[:], 0.0, A.is_ge, ["PBI"], ["PG40"])
+    dma("y", [(T.PD[0], T.PF[:, 0:256]), (T.PD[1], T.PG4[:, 0:256])], ["PF0", "PG40"], ["PD0"])
+    cp(T.PF[:, 256:512], T.PAI[:], ["PAI"], ["PF1"])
+    ts(T.PG4[:, 256:512], T.PAI[:], 0.0, A.is_ge, ["PAI"], ["PG41"])
+    dma("y", [(T.PD[2], T.PF[:, 256:512]), (T.PD[3], T.PG4[:, 256:512])], ["PF1", "PG41"], ["PD1"])
+
+    def fill_table(tab, key, pv, pf, pk):
+        pieces = [(tab[16 * b:16 * b + 14, 0:W], T.BD[:]) for b in range(8)]
+        pieces += [(tab[15:128:16, 0:W], pv), (tab[14:128:16, 0:W], pf)]
+        dma("y", pieces, ["BD", pk], [key])
+
+    fill_table(T.TB, "TBd", T.PD[0], T.PD[1], "PD0")
+    ts(T.OB[:], T.CF[:, 0:8], PGRP, A.is_equal, ["CF", "PC0"], ["OB"], 4096.0, A.mult)
+    ts(T.IDF[:], T.CF[:, 0:128], PP, A.is_equal, ["CF", "PC4"], ["IDF"])
+    ts(T.PEN[:], T.IDF[:], float(2 ** 25), A.mult, ["IDF"], ["PEN"])
+    ms(T.ZB[:], 0.0, ["ZB"])
+    ts(T.CT1[:, 0:256], T.CI5[:, 0:256], 7, A.bitwise_and, ["CI5"], ["CT1"])
+    ts(T.RS8[:], T.CT1[:, 0:256], 0.0, A.is_equal, ["CT1"], ["RS8"], float(2 ** 26), A.mult)
+    ts(T.CT1[:, 0:256], T.CI5[:, 0:256], 15, A.bitwise_and, ["CI5"], ["CT1"])
+    ts(T.RS16[:], T.CT1[:, 0:256], 0.0, A.not_equal, ["CT1"], ["RS16"])
+    ts(T.DIAG[:], T.CT1[:, 0:256], PLOW, A.is_equal, ["CT1", "PC0"], ["DIAG"])
+    ts(T.CT2[:, 0:256], T.CI5[:, 0:256], 4, A.arith_shift_right, ["CI5"], ["CT2"])
+    ts(T.DG2[:], T.CT2[:, 0:256], PLOW, A.is_equal, ["CT2", "PC0"], ["DG2"])
+    ts(T.CT2[:, 0:128], T.CI5[:, 0:128], 2, A.arith_shift_right, ["CI5", "DG2"], ["CT2"], 3, A.bitwise_and)
+    ts(T.M1[:], T.CT2[:, 0:128], PL3, A.is_equal, ["CT2", "PC0"], ["M1"])
+    ts(T.RS1[:], T.CF[:, 0:32], PS2, A.is_equal, ["CF", "PC0"], ["RS1"])
+    op("g", lambda: g.iota(T.LXI[:, 0:8], [[32, 8]], 7, 0), [], ["LXI"])
+    ts(T.LXJ[:, 0:8], T.LXI[:, 0:8], 0, A.add, ["LXI"], ["LXJ"])
+    ts(T.PC[:, 5:6], PL3, 8.0, A.mult, ["PC0"], ["PC5"])
+    ts(T.LX1[:], T.LXI[:, 0:8], T.PC[:, 5:6], A.add, ["LXI", "PC5"], ["LX1"])
+    ts(T.PT[:, 6:7], T.PI[:, 0:1], 2, A.arith_shift_right, ["PI"], ["PT6"], 3, A.bitwise_and)
+    ts(T.PC[:, 6:7], T.PT[:, 6:7], 8.0, A.mult, ["PT6"], ["PC6"])
+    ts(T.LX3[:], T.LXI[:, 0:8], T.PC[:, 6:7], A.add, ["LXI", "PC6"], ["LX3"])
+    ts(T.CT2[:, 0:16], T.CI5[:, 0:16], 7, A.bitwise_and, ["CI5", "M1"], ["CT2"])
+    ts(T.CT1[:, 0:16], T.CI5[:, 0:16], 3, A.arith_shift_right, ["CI5", "DIAG", "RS16"], ["CT1"])
+    ts(T.LXJ[:], T.CT2[:, 0:16], 2.0, A.mult, ["CT2"], ["LXJ"])
+    tt(T.LXI[:], T.LXJ[:], T.CT1[:, 0:16], A.add, ["LXJ", "CT1"], ["LXI"])
+    cp(T.LX2[:], T.LXI[:], ["LXI"], ["LX2"])
+    cp(T.LX4[:], T.CI5[:, 0:16], ["CI5"], ["LX4"])
+    ms(T.CA[:, 0:16], 0.0, ["CA"])
+    ts(T.LX5[:], T.CA[:, 0:16], PLOW, A.add, ["CA", "PC0"], ["LX5"])
+    for i, r in enumerate((12, 13, 14, 15)):
+        ts(T.PC[:, 8 + i:9 + i], PLOW, float(r), A.is_equal, ["PC0"], ["PC%d" % (8 + i)])
+    I12, I13, I14, I15 = [T.PC[:, 8 + i:9 + i] for i in range(4)]
+    ts(T.PC[:, 12:13], PLOW, 12.0, A.is_lt, ["PC0"], ["PC12"])
+    ts(T.CL[:], T.CF[:, 0:256], I13, A.mult, ["CF", "PC9"], ["CL"])
+    ts(T.PC[:, 13:14], T.PC[:, 12:13], 128.0, A.mult, ["PC12"], ["PC13"])
+    ts(T.PC[:, 14:15], I14, 2048.0, A.mult, ["PC10"], ["PC14"])
+    tt(T.PC[:, 13:14], T.PC[:, 13:14], I12, A.add, ["PC13", "PC8"], ["PC13"])
+    ts(T.CL[:], T.CL[:], T.PC[:, 13:14], A.add, ["CL", "PC13", "PC14"], ["CL"], T.PC[:, 14:15], A.add)
+    ts(T.CR[:], T.CF[:, 0:256], I12, A.mult, ["CF", "PC8"], ["CR"], -1.0, A.mult)
+    tt(T.PC[:, 15:16], T.PC[:, 12:13], I13, A.add, ["PC12", "PC9"], ["PC15"])
+    ts(T.CR[:], T.CR[:], T.PC[:, 15:16], A.add, ["CR", "PC15", "PC10"], ["CR"], I14, A.add)
+    ts(T.WF2[:, 4:5], PLOW, 14.0, A.is_lt, ["PC0"], ["WF4"], -2.0, A.mult)
+    tt(T.WF2[:, 4:5], T.WF2[:, 4:5], I14, A.add, ["WF4", "PC10"], ["WF4"])
+    ts(T.RC[:], T.CF[:, 0:256], 16.0, A.mult, ["CF"], ["RC"], I15, A.mult)
+    ts(T.RC[:], T.RC[:], T.WF2[:, 4:5], A.add, ["RC", "WF4"], ["RC"])
+    cp(T.WF2[:, 5:6], T.PT[:, 4:5], ["PT4"], ["WF5"])
+    ts(T.WF2[:, 6:7], T.WF2[:, 5:6], -1.0, A.mult, ["WF5"], ["WF6"], 1.0, A.add)
+    ECOL, OCOL = T.WF2[:, 6:7], T.WF2[:, 5:6]
+    ts(T.CT1[:, 0:256], T.CI5[:, 0:256], 4, A.arith_shift_right, ["CI5", "LXI"], ["CT1"], 7, A.bitwise_and)
+    ts(T.CA[:, 0:256], T.CT1[:, 0:256], 4.0, A.is_lt, ["CT1"], ["CA"], 1536.0, A.mult)
+    ts(T.CB[:, 0:256], T.DIAG[:], 0.0, A.is_equal, ["DIAG"], ["CB"], 1e25, A.mult)
+    tt(T.TH2[:], T.CA[:, 0:256], T.CB[:, 0:256], A.max, ["CA", "CB"], ["TH2"])
+    ts(RH, T.CF[:, 0:8], PGRP, A.is_equal, ["CF", "PC0"], ["RH"], float(DUM), A.mult)
+    ts(RL0, T.CF[:, 0:8], PGRP, A.is_equal, ["CF", "PC0", "PC4"], ["RL0"], PP, A.mult)
+    ts(T.WF2[:, 7:8], PP, 128.0, A.add, ["PC4"], ["WF7"])
+    ts(RL1, T.CF[:, 0:8], PGRP, A.is_equal, ["CF", "PC0", "WF7"], ["RL1"], T.WF2[:, 7:8], A.mult)
+    ts(T.CT1[:, 0:128], T.CI5[:, 0:128], 4, A.arith_shift_right, ["CI5"], ["CT1"])
+    ts(GB, T.CT1[:, 0:128], PGRP, A.is_equal, ["CT1", "PC0"], ["GB"])
+    cp(T.GBH[:], GB, ["GB"], ["GBH"])
+    ts(SR15, GB, I15, A.mult, ["GB", "PC11"], ["SR15"])
+    ts(SR14, GB, I14, A.mult, ["GB", "PC10"], ["SR14"])
+    ts(T.CT2[:, 0:128], T.CI5[:, 0:128], 15, A.bitwise_and, ["CI5", "LXJ"], ["CT2"])
+    ts(T.CA[:, 0:128], T.CT2[:, 0:128], 14.0, A.is_ge, ["CT2"], ["CA"])
+    tt(SRN, T.CA[:, 0:128], GB, A.mult, ["CA", "GB"], ["SRN"])
+    ms(T.ONES[:], 1.0, ["ONES"])
+    ms(T.FBC[:], 16777215.0, ["FBC"])
+    ms(T.FB4C[:], 16777215.0, ["FB4C"])
+    ms(T.CA[:], 0.0, ["CA"])
+    ts(T.TB[:, W:WX], T.CA[:], I14, A.add, ["CA", "PC10"], ["TBx"])
+    ts(T.TA[:, W:WX], T.CA[:], I14, A.add, ["CA", "PC10"], ["TAx"])
+    ms(T.XC0[:, W:WX], 0.0, ["XC0x"])
+    ms(T.XC1[:, W:WX], 0.0, ["XC1x"])
+    wr["TB"] = deps(["TBd", "TBx"], [])
+    fill_table(T.TA, "TAd", T.PD[2], T.PD[3], "PD1")
+    wr["TA"] = deps(["TAd", "TAx"], [])
+
+    def row_to_list(src, lhsT, rows, out, okey, bank, bkey, fin):
+        op("p", mm(bank[:, 0:256], lhsT, src, True, True), rows, [bkey])
+        tt(T.DM[:], bank[:, 0:256], T.DIAG[:], A.mult, [bkey, "DIAG"], ["DM"])
+        scan(T.SC[:], T.RS16[:], T.DM[:], A.mult, A.add, ["RS16", "DM"], ["SC"])
+        fin(T.SC[:, 15:256:16])
+
+    cp(T.W1[:], T.PG4[:, 256:512:16], ["PG41"], ["W1"])
+    tt(T.E4[:], T.W1[:, 0:16].indirect(T.LX5[:]), T.DG2[:], A.mult, ["W1", "LX5", "DG2"], ["E4"])
+
+    def dead_done(t):
+        def fin(ap):
+            ts(T.DSND[:, 16 * t:16 * t + 16], ap, 1.0, A.min, ["SC"], ["DSND%d" % t], DEAD, A.mult)
+            send(nxt if t % 2 == 0 else prv, "e%d" % t, T.DLAND[:, 16 * t:16 * t + 16], T.DSND[:, 16 * t:16 * t + 16], ["DSND%d" % t])
+        return fin
+
+    row_to_list(T.E4[:], T.GBH[:], ["E4", "GBH"], None, None, T.G3, "G3", dead_done(0))
+
+    def near_back(t):
+        near, nk = (T.TA, "TA") if t % 2 == 0 else (T.TB, "TB")
+        landed(nxt if t % 2 == 0 else prv, "r%d" % t, ["RLAND%d" % t])
+        tt(T.E3[:], T.RLAND[:, 16 * t:16 * t + 16].indirect(T.LX4[:]), T.DIAG[:], A.mult, ["RLAND%d" % t, "LX4", "DIAG"], ["E3"])
+        op("p", mm(T.G4[:, 0:256], SRN, T.E3[:], True, True), ["SRN", "E3"], ["G4"])
+        tt(near[:, t:W:16], T.G4[:, 0:256], near[:, t:W:16], A.add, ["G4", nk], [nk])
+
+    BANKS = [T.G0, T.G1, T.G2, T.G3, T.G4, T.G5]
+    for t in range(NB):
+        frm, to = (prv, nxt) if t % 2 == 0 else (nxt, prv)
+        far, fk, near, nk = (T.TB, "TB", T.TA, "TA") if t % 2 == 0 else (T.TA, "TA", T.TB, "TB")
+        XC, xk = (T.XC0, "XC0") if t % 2 == 0 else (T.XC1, "XC1")
+        for d in range(ND):
+            m = t * ND + d
+            tail = d == ND - 1
+            if d == 0:
+                z, zk = T.SLAND[:, 256 * t:256 * t + 256], "SLAND%d" % t
+            else:
+                z, zk = T.Z[:], "Z"
+                pm = m - 1
+                msg = "%d%d" % (t, d - 1)
+                if d == 1:
+                    landed(frm, "b%d" % t, [xk + "b"])
+                    wr[xk] = deps([xk + "b", xk + "x"], [])
+                landed(frm, "n" + msg, ["NLAND%d" % pm])
+                landed(frm, "l" + msg, ["LLAND%d" % pm])
+                cp(XC[:, 0:WX].indirect(T.LLAND[:, 16 * pm:16 * pm + 16]), T.NLAND[:, 256 * pm:256 * pm + 256],
+                   ["NLAND%d" % pm, "LLAND%d" % pm], [xk])
+                cp(T.Z[:], XC[:, 0:WX].indirect(T.PU[:]), [xk, "PU"], ["Z"])
+            fs = []
+            zs = (lambda ll: T.SLAND[:, 256 * t + ll:256 * t + 256:4]) if d == 0 else (lambda ll: T.Z[:, ll:256:4])
+            for ll in range(4):
+                fs.append(mm(T.K6[:, 0:64], T.WH[:, 128 * ll:128 * ll + 128], zs(ll), ll == 0, False))
+                fs.append(mm(T.K6[:, 0:64], T.WL[:, 128 * ll:128 * ll + 128], zs(ll), False, ll == 3))
+            op("p", fs, ["WH", "WL", zk], ["K6"])
+            for cl in range(4):
+                cp(T.Z4[:, cl:1024:4], z, [zk] + (["Z4"] if cl == 9 else []), ["Z4_%d" % cl])
+            ts(T.NI[:], T.K6[:, 0:64], -0.5, A.add, ["K6"], ["NI"])
+            tt(T.UF[:], T.K6[:, 0:64], T.NI[:], A.subtract, ["K6", "NI"], ["UF"])
+            for ch in range(4):
+                act(T.SQ[:, 64 * ch:64 * ch + 64], T.UF[:], F.Square, ["UF", "SCOL"], ["SQ%d" % ch], bias=T.SCOL[:, ch:ch + 1], scale=4096.0)
+            for ch in range(4):
+                ts(T.FI[:, 64 * ch:64 * ch + 64], T.SQ[:, 64 * ch:64 * ch + 64], T.ACOL[:, ch:ch + 1], A.add, ["SQ%d" % ch, "ACOL"], ["FI%d" % ch], 1.0 / 32, A.mult)
+            ts(T.CI[:], T.FI[:], 4095, A.bitwise_and, ["FI0", "FI1", "FI2", "FI3"], ["CI"])
+            cp(T.OFF[:], T.CI[:], ["CI"], ["OFF"])
+            if d == 0:
+                act(T.SH[:], z, F.Copy, [zk], ["SH"], bias=-0.5)
+            pend = []
+
+            def gather(hc):
+                a = 512 * hc
+                tt(T.DF[:, a:a + 512], T.X[:, 0:WX].indirect(T.OFF[:, 32 * hc:32 * hc + 32]), T.Z4[:, 512 * (hc % 2):512 * (hc % 2) + 512], A.subtract,
+                   ["X", "OFF", "Z4_0", "Z4_1", "Z4_2", "Z4_3"], ["DF%d" % hc])
+                act(T.AB[:, a:a + 512], T.DF[:, a:a + 512], F.Abs, ["DF%d" % hc], ["AB%d" % hc])
+
+            def dsum(c0, n, p0, pr, keys, stop):
+                fs = []
+                for part in range(16):
+                    o = 2 * part + pr
+                    fs.append(mm(T.K6[p0:p0 + n, o:256:32], T.AB[:, 16 * c0 + part:16 * (c0 + n):16], T.OB[:], False, False))
+                if stop:
+                    fs.append(mm(T.K6[:, 0:256], T.ZB[:, 0:128], T.ZB[:], False, True))
+                op("p", fs, keys + ["OB"], ["K6"])
+
+            gather(0)
+            cp(T.CFL[:], T.CI[:], ["CI"], ["CFL"])
+            op("p", [mm(T.K6[:, 0:256], T.ZB[:, 0:128], T.ZB[:], True, False)] +
+               [mm(T.K6[:, pr:256:2], T.CFL[:, 128 * pr:128 * pr + 128], T.IDF[:], False, False) for pr in range(2)], ["ZB", "CFL", "IDF"], ["K6"])
+            if d > 0:
+                for ch in range(4):
+                    tt(T.EQ[:, 64 * ch:64 * ch + 64], T.CI[:, 64 * ch:64 * ch + 64], T.LAST[:], A.is_equal, ["CI", "LAST"], ["EQ%d" % ch])
+                op("p", [mm(T.K6[:, pr:256:2], T.EQ[:, 128 * pr:128 * pr + 128], T.PEN[:], False, False) for pr in range(2)], ["EQ0", "EQ1", "EQ2", "EQ3", "PEN"], ["K6"])
+            gather(1); gather(2); gather(3)
+            dsum(0, 128, 0, 0, ["AB0", "AB1", "AB2", "AB3"], False)
+            if d == 0:
+                landed(frm, "e%d" % t, ["DLAND%d" % t])
+                cp(T.DEADL[:], T.DLAND[:, 16 * t:16 * t + 16], ["DLAND%d" % t], ["DEADL"])
+                ms(T.RES[:], 0.0, ["RES"])
+                if t > 0:
+                    near_back(t - 1)
+                    ts(T.RC[:], T.RC[:], I15, A.add, ["RC", "PC11"], ["RC"])
+            gather(4); gather(5)
+            dsum(128, 64, 0, 1, ["AB4", "AB5"], False)
+            gather(6)
+            dsum(192, 32, 64, 1, ["AB6"], False)
+            gather(7)
+            dsum(224, 32, 96, 1, ["AB7"], True)
+            scan(T.R[:], T.RS8[:], T.K6[:, 0:256], A.max, A.min, ["RS8", "K6"], ["R"])
+            tt(T.E1[:], T.R[:, 0:256].indirect(T.LX1[:]), T.M1[:], A.mult, ["R", "LX1", "M1"], ["E1"])
+            op("p", mm(T.C7[:, 0:32], T.E1[:], T.RS1[:], True, True), ["E1", "RS1"], ["C7"])
+            fb, fbk = (T.FBC, "FBC") if d == 0 else (T.FB, "FB")
+            tt(T.MN[:], T.C7[:, 16:32], fb[:], A.min, ["C7", fbk], ["MN"])
+            tt(T.YI[:], T.C7[:, 0:16], T.MN[:], A.min, ["C7", "MN"], ["YI"])
+            ts(T.YA[:], T.YI[:], 4095, A.bitwise_and, ["YI"], ["YA"])
+            tt(T.YQ[:], T.YA[:], T.DEADL[:], A.max, ["YA", "DEADL"], ["YQ"])
+            cp(T.YU[:], T.YQ[:], ["YQ"], ["YU"])
+            tt(T.QL[:], far[:, 0:WX].indirect(T.YU[:]), T.CL[:], A.mult, [fk, "YU", "CL"], ["QL"])
+            act(T.QE[:], T.QL[:], F.Copy, ["QL", "WF6"], ["QE"], scale=ECOL)
+            tt(T.QR[:], far[:, 0:WX].indirect(T.YU[:]), T.CR[:], A.mult, [fk, "YU", "CR"], ["QR"])
+            ts(T.QO[:], T.QL[:], OCOL, A.mult, ["QL", "WF5"], ["QO"])
+            tt(T.TT[:], T.X[:, 0:WX].indirect(T.YU[:]), T.SH[:], A.add, ["X", "YU", "SH"], ["TT"])
+            act(T.T2[:], T.TT[:], F.Copy, ["TT"], ["T2"], scale=0.5, bias=8388608.0)
+            ns = T.NSND[:, 256 * m:256 * m + 256]
+            act(ns, T.T2[:], F.Copy, ["T2"], ["NSND%d" % m], bias=-8388608.0)
+            if not tail:
+                send(to, "n%d%d" % (t, d), T.NLAND[:, 256 * m:256 * m + 256], ns, ["NSND%d" % m])
+            for n, gr in enumerate((0, 4, 2, 6, 1, 5, 3, 7)):
+                b, bk = BANKS[n % 6], "G%d" % (n % 6)
+                qa, qk = (T.QE, "QE") if gr % 2 == 0 else (T.QO, "QO")
+                p0 = 32 * (gr // 2)
+                op("p", [mm(b[:, 0:128], qa[p0:p0 + 32, 0:128], T.QR[p0:p0 + 32, 0:128], True, True),
+                         mm(b[:, 128:384], qa[p0:p0 + 32, 128:256], T.QR[p0:p0 + 32, 0:256], True, True)], [qk, "QR"], [bk])
+                for h in range(2):
+                    src = b[:, 0:128] if h == 0 else b[:, 128:384]
+                    o = T.FL[:, 2 * gr + h:2 * gr + h + 1]
+                    if gr < 4:
+                        op("v", lambda: g.vector.tensor_reduce(o, src, AxisListType.X, A.max), [bk], ["FL%d_%d" % (gr, h)])
+                    else:
+                        act(T.JK[:, 0:(128 if h == 0 else 256)], src, F.Relu, [bk], ["JK", "FL%d_%d" % (gr, h)], bias=-1536.0, accum_out=o)
+            tt(T.E2[:], T.FL[:, 0:16].indirect(T.LX2[:]), T.TH2[:], A.is_gt, ["FL%d_%d" % (i, h) for i in range(8) for h in range(2)] + ["LX2", "TH2"], ["E2"])
+            fs = []
+            for h in range(2):
+                fs.append(mm(T.C7[:, 64 + 8 * h:72 + 8 * h], T.E2[:, 128 * h:128 * h + 128], RH, True, False))
+                fs.append(mm(T.C7[:, 64 + 8 * h:72 + 8 * h], T.E2[:, 128 * h:128 * h + 128], RL0 if h == 0 else RL1, False, True))
+            op("p", fs, ["E2", "RH", "RL0", "RL1"], ["C7"])
+            tt(T.LF[:], T.C7[:, 64:80], T.YQ[:], A.max, ["C7", "YQ"], ["LF"])
+            ls = T.LSND[:, 16 * m:16 * m + 16]
+            lk = "LSND%d" % m
+            cp(ls, T.LF[:], ["LF"], [lk])
+            if not tail:
+                send(to, "l%d%d" % (t, d), T.LLAND[:, 16 * m:16 * m + 16], ls, [lk])
+            if tail:
+                cp(T.X[:, 0:WX].indirect(ls), ns, [lk, "NSND%d" % m], ["X"])
+                if t + 1 < NB:
+                    start_batch(t + 1)
+            tt(T.UP[:], far[:, 0:WX].indirect(T.YU[:]), T.RC[:], A.max, [fk, "YU", "RC"], ["UP"])
+            cp(far[:, 0:WX].indirect(ls), T.UP[:], ["UP", lk], [fk])
+            if not tail:
+                act(T.PG[:], far[:, 0:WX].indirect(T.YU[:]), F.Copy, [fk, "YU"], ["PG"])
+            ts(T.WB[:], T.LF[:], float(DUM), A.is_lt, ["LF"], ["WB"])
+            op("p", mm(T.G0[:, 0:16], T.ONES[:], T.WB[:], True, True), ["ONES", "WB"], ["G0"])
+            ts(T.W3[:], T.YQ[:], 1.0, A.add, ["YQ"], ["W3"])
+            tt(T.W2[:], T.W3[:], T.WB[:], A.mult, ["W3", "WB"], ["W2"])
+            tt(T.RES[:], T.RES[:], T.W2[:], A.add, ["RES", "W2"], ["RES"])
+            if not tail:
+                row_to_list(T.PG[:], SR15, ["PG", "SR15"], None, None, T.G2, "G2",
+                            lambda ap: cp(T.PU[:], ap, ["SC"], ["PU"]))
+                ts(T.W1[:], T.WB[:], DEAD, A.mult, ["WB"], ["W1"])
+                tt(T.DEADL[:], T.DEADL[:], T.W1[:], A.max, ["DEADL", "W1"], ["DEADL"])
+                ts(T.FB[:], T.YA[:], BAR, A.add, ["YA"], ["FB"])
+                act(T.R4[:], T.R[:, 0:256].indirect(T.LX3[:]), F.Copy, ["R", "LX3"], ["R4"])
+                op("p", mm(T.G1[:, 0:128], T.R4[:], T.IDF[:], True, True), ["R4", "IDF"], ["G1"])
+                f4, f4k = (T.FB4C, "FB4C") if d == 0 else (T.FB4, "FB4")
+                tt(T.L1[:], T.G1[:, 64:128], f4[:], A.min, ["G1", f4k], ["L1"])
+                tt(T.L2[:], T.G1[:, 0:64], T.L1[:], A.min, ["G1", "L1"], ["L2"])
+                ts(T.LAST[:], T.L2[:], 4095, A.bitwise_and, ["L2"], ["LAST"])
+                if d == 0:
+                    ts(T.FB4[:], T.LAST[:], BAR, A.add, ["LAST"], ["FB4"])
+                cp(T.X[:, 0:WX].indirect(ls), ns, [lk, "NSND%d" % m], ["X"])
+            else:
+                cp(T.RSND[:, 16 * t:16 * t + 16], T.RES[:], ["RES"], ["RSND%d" % t])
+                send(frm, "r%d" % t, T.RLAND[:, 16 * t:16 * t + 16], T.RSND[:, 16 * t:16 * t + 16], ["RSND%d" % t])
+            if t + 1 < NB or not tail:
+                op("v", lambda: g.vector.tensor_reduce(T.KP[:, 0:1], T.G0[:, 0:16], AxisListType.X, A.add), ["G0"], ["KP0"])
+                cp(T.KI[:, 0:1], T.KP[:, 0:1], ["KP0"], ["KI0"])
+                ts(T.KI[:, 1:2], T.KI[:, 0:1], 31, A.bitwise_and, ["KI0"], ["KI1"])
+                ts(T.KP[:, 1:2], T.KI[:, 1:2], 32.0, A.mult, ["KI1"], ["KP1"])
+                ts(T.ACOL[:], T.ABASE[:], T.KP[:, 1:2], A.add, ["ABASE", "KP1"], ["ACOL"], 3104.0 * ((d + 1) % ND), A.add)
+            if tail and t + 1 < NB:
+                row_to_list(far[:, t + 1:W:16], SR14, [fk, "SR14"], None, None, T.G3, "G3", dead_done(t + 1))
+    dma("y", [(T.yx[:], T.X[:, 0:W])], ["X"], ["yx"])
+    dma("y", [(T.yb[:], T.TB[15:128:16, 0:W])], ["TB"], ["yb"])
+    near_back(NB - 1)
+    dma("y", [(T.ya[:], T.TA[15:128:16, 0:W])], ["TA"], ["ya"])
+    for sem in sorted(last):
+        q = "g"
+        if waited[q].get(sem, 0) < last[sem]:
+            need(q, {sem: last[sem]})

@@ -1,6 +1,4 @@
-from concourse.bass import DstId, RemoteDMATransfer
-from concourse.mybir import dt, AluOpType, AxisListType, ActivationFunctionType
-import numpy as np
+from concourse.mybir import AluOpType, AxisListType, ActivationFunctionType
 
 W = 4096
 WX = 4608
@@ -21,9 +19,9 @@ _sb("TA", WX, "float32"); _sb("TB", WX, "float32")
 _sb("PAI", 256, "int32"); _sb("PBI", 256, "int32"); _sb("PF", 512, "float32"); _sb("PG4", 512, "float32")
 _sb("BI", 384, "int32"); _sb("BF", 448, "float32")
 _sb("WI", 8, "int32"); _sb("WF2", 8, "float32")
-_sb("CI5", 512, "int32"); _sb("CT1", 512, "int32"); _sb("CT2", 512, "int32"); _sb("CA", 512, "float32"); _sb("CB", 512, "float32")
-_sb("PI", 8, "int32"); _sb("PT", 16, "int32"); _sb("PC", 16, "float32"); _sb("CF", 512, "float32")
-_sb("MW", 512, "bfloat16"); _sb("WH", 512, "bfloat16"); _sb("WL", 512, "bfloat16")
+_sb("CI5", 256, "int32"); _sb("CT1", 256, "int32"); _sb("CT2", 256, "int32"); _sb("CA", 512, "float32"); _sb("CB", 256, "float32")
+_sb("PI", 8, "int32"); _sb("PT", 16, "int32"); _sb("PC", 16, "float32"); _sb("CF", 256, "float32")
+_sb("WH", 512, "bfloat16"); _sb("WL", 512, "bfloat16")
 _sb("OB", 8, "bfloat16"); _sb("IDF", 128, "float32"); _sb("PEN", 128, "bfloat16"); _sb("ZB", 256, "bfloat16")
 _sb("DIAG", 256, "float32"); _sb("DG2", 256, "float32"); _sb("M1", 128, "float32"); _sb("RS1", 32, "float32")
 _sb("CL", 256, "float32"); _sb("CR", 256, "float32"); _sb("RC", 256, "float32"); _sb("TH2", 256, "float32")
@@ -64,7 +62,7 @@ for _t in range(NB):
     _MSG += ["s%d" % _t, "b%d" % _t, "e%d" % _t, "r%d" % _t]
     for _d in range(ND - 1):
         _MSG += ["n%d%d" % (_t, _d), "l%d%d" % (_t, _d)]
-SEMAPHORES = ["cv", "cs", "cp", "cg"] + ["rx" + m for m in _MSG] + ["tx" + m for m in _MSG] + ["dm%d" % i for i in range(24)]
+SEMAPHORES = ["cv", "cs", "cp", "cg"] + ["rx" + m for m in _MSG] + ["tx" + m for m in _MSG] + ["dm%d" % i for i in range(16)]
 
 
 def rank_program(g, core, T, topo):
@@ -76,6 +74,7 @@ def rank_program(g, core, T, topo):
     RH, RL0, RL1 = T.RHL[:, 0:8], T.RHL[:, 8:16], T.RHL[:, 16:24]
     GB, SR15, SR14, SRN = [T.SRM[:, 128 * i:128 * i + 128] for i in range(4)]
     n_ranks = len(T.cores)
+    nxt, prv = (rank + 1) % n_ranks, (rank - 1) % n_ranks
     Q = {"v": g.vector, "s": g.scalar, "p": g.tensor, "g": g, "y": g.sync}
     cnt = {"v": 0, "s": 0, "p": 0, "g": 0}
     waited = {q: {} for q in Q}
@@ -142,8 +141,7 @@ def rank_program(g, core, T, topo):
         note(reads, [], "tx" + msg, n)
 
     def landed(frm, msg, keys):
-        n = engs(T.cores[frm], core)[1]
-        note([], keys, "rx" + msg, n)
+        note([], keys, "rx" + msg, engs(T.cores[frm], core)[1])
 
     def ts(out, in0, s1, o0, r, w, s2=None, o1=None):
         if o1 is None:
@@ -169,32 +167,17 @@ def rank_program(g, core, T, topo):
     def mm(out, lhsT, rhs, start, stop):
         return lambda: g.tensor.matmul(out, lhsT, rhs, start, stop)
 
-    dma("y", [(T.X[:, 0:W], T.x[:])], [], ["X"])
-    dma("s", [(T.WI[:, 0:1], T.wt[:])], [], ["WI"])
-    dma("s", [(T.PBI[:], T.pb[:])], [], ["PBI"])
-    dma("s", [(T.PAI[:], T.pa[:])], [], ["PAI"])
-    op("g", lambda: g.iota(T.PI[:, 0:1], [[0, 1]], 0, 1), [], ["PI"])
-    op("g", lambda: g.iota(T.CI5[:], [[1, 512]], 0, 0), [], ["CI5"])
-    op("g", lambda: g.iota(T.BI[:, 0:32], [[1, 32]], 0, 32), [], ["BI0"])
-    PSH = [(0, "s", 4), (1, "a", 15), (2, "a", 3), (3, "s", 2), (5, "a", 1)]
-    for c, k, v in PSH:
-        ts(T.PT[:, c:c + 1], T.PI[:, 0:1], v, A.arith_shift_right if k == "s" else A.bitwise_and, ["PI"], ["PT%d" % c])
-    ts(T.PT[:, 4:5], T.PI[:, 0:1], 4, A.arith_shift_right, ["PI"], ["PT4"], 1, A.bitwise_and)
-    cp(T.PC[:, 0:4], T.PT[:, 0:4], ["PT0", "PT1", "PT2", "PT3"], ["PC0"])
-    cp(T.PC[:, 4:5], T.PI[:, 0:1], ["PI"], ["PC4"])
-    PGRP, PLOW, PL3, PS2, PP = T.PC[:, 0:1], T.PC[:, 1:2], T.PC[:, 2:3], T.PC[:, 3:4], T.PC[:, 4:5]
-    ts(T.WI[:, 2:3], T.WI[:, 0:1], 3840, A.bitwise_and, ["WI"], ["WI2"])
-    ts(T.WI[:, 3:4], T.WI[:, 0:1], 255, A.bitwise_and, ["WI"], ["WI3"])
-    ts(T.WF2[:, 0:2], T.WI[:, 2:4], 1.0 / 4096, A.mult, ["WI2", "WI3"], ["WF2"])
-    ts(T.CT1[:], T.CI5[:], 4, A.arith_shift_right, ["CI5"], ["CT1"], 7, A.bitwise_and)
-    ts(T.CA[:], T.CT1[:], PGRP, A.is_equal, ["CT1", "PC0"], ["CA"])
-    ts(T.CT1[:], T.CI5[:], 2, A.arith_shift_right, ["CI5"], ["CT1"], 3, A.bitwise_and)
-    ts(T.CT2[:], T.CI5[:], 7, A.arith_shift_right, ["CI5"], ["CT2"])
-    tt(T.CB[:], T.CT1[:], T.CT2[:], A.is_equal, ["CT1", "CT2"], ["CB"])
-    tt(T.MW[:], T.CA[:], T.CB[:], A.mult, ["CA", "CB"], ["MW"])
-    ts(T.WH[:], T.MW[:], T.WF2[:, 0:1], A.mult, ["MW", "WF2"], ["WH"])
-    ts(T.WL[:], T.MW[:], T.WF2[:, 1:2], A.mult, ["MW", "WF2"], ["WL"])
-    nxt, prv = (rank + 1) % n_ranks, (rank - 1) % n_ranks
+    def row_to_list(src, lhsT, rows, bank, bkey, fin):
+        op("p", mm(bank[:, 0:256], lhsT, src, True, True), rows, [bkey])
+        tt(T.DM[:], bank[:, 0:256], T.DIAG[:], A.mult, [bkey, "DIAG"], ["DM"])
+        scan(T.SC[:], T.RS16[:], T.DM[:], A.mult, A.add, ["RS16", "DM"], ["SC"])
+        fin(T.SC[:, 15:256:16])
+
+    def dead_done(t):
+        def fin(ap):
+            ts(T.DSND[:, 16 * t:16 * t + 16], ap, 1.0, A.min, ["SC"], ["DSND%d" % t], DEAD, A.mult)
+            send(nxt if t % 2 == 0 else prv, "e%d" % t, T.DLAND[:, 16 * t:16 * t + 16], T.DSND[:, 16 * t:16 * t + 16], ["DSND%d" % t])
+        return fin
 
     def start_batch(t):
         to = nxt if t % 2 == 0 else prv
@@ -202,25 +185,55 @@ def rank_program(g, core, T, topo):
         send(to, "s%d" % t, T.SLAND[:, 256 * t:256 * t + 256], T.SSND[:, 256 * t:256 * t + 256], ["SSND%d" % t])
         xc = T.XC0 if t % 2 == 0 else T.XC1
         send(to, "b%d" % t, xc[:, 0:W], T.X[:, 0:W], ["X"])
-        frm = prv if t % 2 == 0 else nxt
-        landed(frm, "s%d" % t, ["SLAND%d" % t])
+        landed(prv if t % 2 == 0 else nxt, "s%d" % t, ["SLAND%d" % t])
 
-    start_batch(0)
-    cp(T.CF[:], T.CI5[:], ["CI5"], ["CF"])
-    ts(T.PT[:, 8:9], T.PT[:, 2:3], 1, A.mult, ["PT2"], ["PT8"])
-    for ch in range(4):
-        ts(T.SCOL[:, ch:ch + 1], PL3, 32.0, A.mult, ["PC0"], ["SCOL"], 128.0 * ch + 16.0, A.add)
-    tt(T.ATMP[:], T.SCOL[:], T.SCOL[:], A.mult, ["SCOL"], ["ATMP"])
-    ts(T.ABASE[:], T.ATMP[:], -1.0, A.mult, ["ATMP"], ["ABASE"], 262144.0 - 12.0, A.add)
-    ts(T.ACOL[:], T.ABASE[:], 0.0, A.add, ["ABASE"], ["ACOL"])
-    ms(T.X[:, W:WX], 0.0, ["Xd"])
-    wr["X"] = deps(["X", "Xd"], [])
+    def near_send(t):
+        cp(T.RSND[:, 16 * t:16 * t + 16], T.RES[:], ["RES"], ["RSND%d" % t])
+        send(prv if t % 2 == 0 else nxt, "r%d" % t, T.RLAND[:, 16 * t:16 * t + 16], T.RSND[:, 16 * t:16 * t + 16], ["RSND%d" % t])
+
+    def near_rows(t):
+        landed(nxt if t % 2 == 0 else prv, "r%d" % t, ["RLAND%d" % t])
+        tt(T.E3[:], T.RLAND[:, 16 * t:16 * t + 16].indirect(T.LX4[:]), T.DIAG[:], A.mult, ["RLAND%d" % t, "LX4", "DIAG"], ["E3"])
+        op("p", mm(T.G4[:, 0:256], SRN, T.E3[:], True, True), ["SRN", "E3"], ["G4"])
+
+    def near_add(t):
+        near, nk = (T.TA, "TA") if t % 2 == 0 else (T.TB, "TB")
+        tt(near[:, t:W:16], T.G4[:, 0:256], near[:, t:W:16], A.add, ["G4", nk], [nk])
+
+    dma("s", [(T.PAI[:], T.pa[:])], [], ["PAI"])
+    dma("y", [(T.X[:, 0:W], T.x[:])], [], ["X"])
+    dma("s", [(T.PBI[:], T.pb[:])], [], ["PBI"])
+    dma("s", [(T.WI[:, 0:1], T.wt[:])], [], ["WI"])
+    op("g", lambda: g.iota(T.PI[:, 0:1], [[0, 1]], 0, 1), [], ["PI"])
+    op("g", lambda: g.iota(T.BI[:, 0:32], [[1, 32]], 0, 32), [], ["BI0"])
+    op("g", lambda: g.iota(T.CI5[:], [[1, 256]], 0, 0), [], ["CI5"])
+    op("g", lambda: g.iota(T.LXI[:, 0:8], [[32, 8]], 7, 0), [], ["LXI"])
+    for nm in ("X", "XC0", "XC1"):
+        op("g", lambda: g.iota(T[nm][:, W:WX], [[0, WX - W]], 0, 0, allow_small_or_imprecise_dtypes=True), [], [nm + "x"])
+    for c, k, v in [(0, "s", 4), (1, "a", 15), (2, "a", 3), (3, "s", 2)]:
+        ts(T.PT[:, c:c + 1], T.PI[:, 0:1], v, A.arith_shift_right if k == "s" else A.bitwise_and, ["PI"], ["PT%d" % c])
+    cp(T.PC[:, 0:4], T.PT[:, 0:4], ["PT0", "PT1", "PT2", "PT3"], ["PC0"])
+    cp(T.PC[:, 4:5], T.PI[:, 0:1], ["PI"], ["PC4"])
+    PGRP, PLOW, PL3, PS2, PP = T.PC[:, 0:1], T.PC[:, 1:2], T.PC[:, 2:3], T.PC[:, 3:4], T.PC[:, 4:5]
     for f in range(1, 12):
         ts(T.BI[:, 32 * f:32 * f + 32], T.BI[:, 0:32], f, A.arith_shift_right, ["BI0"], ["BI%d" % f], 1, A.bitwise_and)
     ts(T.BI[:, 0:32], T.BI[:, 0:32], 1, A.bitwise_and, ["BI0"], ["BI0"])
     ts(T.BF[:, 0:384], T.BI[:], 2.0, A.mult, ["BI%d" % f for f in range(12)], ["BFA"], -1.0, A.add)
     ms(T.BF[:, 384:448], 1.0, ["BFB"])
     dma("y", [(T.BD[f], T.BF[:, 32 * f:32 * f + 32]) for f in range(14)], ["BFA", "BFB"], ["BD"])
+    ts(T.CT1[:], T.CI5[:], 15, A.bitwise_and, ["CI5"], ["CT1"])
+    ts(T.CT2[:], T.CI5[:], 4, A.arith_shift_right, ["CI5"], ["CT2"])
+    ts(T.GBH[:], T.CT2[:, 0:128], PGRP, A.is_equal, ["CT2", "PC0"], ["GBH"])
+    ts(T.DG2[:], T.CT2[:], PLOW, A.is_equal, ["CT2", "PC0"], ["DG2"])
+    ms(T.CA[:, 0:16], 0.0, ["CA"])
+    ts(T.LX5[:], T.CA[:, 0:16], PLOW, A.add, ["CA", "PC0"], ["LX5"])
+    ts(T.W1[:], T.PAI[:, 0:256:16], 0.0, A.is_ge, ["PAI"], ["W1"])
+    tt(T.E4[:], T.W1[:, 0:16].indirect(T.LX5[:]), T.DG2[:], A.mult, ["W1", "LX5", "DG2"], ["E4"])
+    ts(T.RS16[:], T.CT1[:], 0.0, A.not_equal, ["CT1"], ["RS16"])
+    ts(T.DIAG[:], T.CT1[:], PLOW, A.is_equal, ["CT1", "PC0"], ["DIAG"])
+    row_to_list(T.E4[:], T.GBH[:], ["E4", "GBH"], T.G3, "G3", dead_done(0))
+    start_batch(0)
+    wr["X"] = deps(["X", "Xx"], [])
     cp(T.PF[:, 0:256], T.PBI[:], ["PBI"], ["PF0"])
     ts(T.PG4[:, 0:256], T.PBI[:], 0.0, A.is_ge, ["PBI"], ["PG40"])
     dma("y", [(T.PD[0], T.PF[:, 0:256]), (T.PD[1], T.PG4[:, 0:256])], ["PF0", "PG40"], ["PD0"])
@@ -234,110 +247,96 @@ def rank_program(g, core, T, topo):
         dma("y", pieces, ["BD", pk], [key])
 
     fill_table(T.TB, "TBd", T.PD[0], T.PD[1], "PD0")
+    fill_table(T.TA, "TAd", T.PD[2], T.PD[3], "PD1")
+    ts(T.WI[:, 2:3], T.WI[:, 0:1], 3840, A.bitwise_and, ["WI"], ["WI2"])
+    ts(T.WI[:, 3:4], T.WI[:, 0:1], 255, A.bitwise_and, ["WI"], ["WI3"])
+    ts(T.WF2[:, 0:2], T.WI[:, 2:4], 1.0 / 4096, A.mult, ["WI2", "WI3"], ["WF2"])
+    ts(T.CA[:, 0:128], T.CT2[:, 0:128], PGRP, A.is_equal, ["CT2", "PC0"], ["CA"], 100.0, A.mult)
+    ts(T.CT1[:, 0:128], T.CI5[:, 0:128], 2, A.arith_shift_right, ["CI5"], ["CT1"], 3, A.bitwise_and)
+    tt(T.CB[:, 0:128], T.CT1[:, 0:128], T.CA[:, 0:128], A.add, ["CT1", "CA"], ["CB"])
+    for ll in range(4):
+        for wm, wc in ((T.WH, 0), (T.WL, 1)):
+            ts(wm[:, 128 * ll:128 * ll + 128], T.CB[:, 0:128], 100.0 + ll, A.is_equal, ["CB", "WF2"], ["WHL%d%d" % (ll, wc)], T.WF2[:, wc:wc + 1], A.mult)
+    WHL = ["WHL%d%d" % (i, j) for i in range(4) for j in range(2)]
+    ts(T.M1[:], T.CT1[:, 0:128], PL3, A.is_equal, ["CT1", "PC0"], ["M1"])
+    for ch in range(4):
+        ts(T.SCOL[:, ch:ch + 1], PL3, 32.0, A.mult, ["PC0"], ["SCOL"], 128.0 * ch + 16.0, A.add)
+    tt(T.ATMP[:], T.SCOL[:], T.SCOL[:], A.mult, ["SCOL"], ["ATMP"])
+    ts(T.ABASE[:], T.ATMP[:], -1.0, A.mult, ["ATMP"], ["ABASE"], 262144.0 - 12.0, A.add)
+    ts(T.ACOL[:], T.ABASE[:], 0.0, A.add, ["ABASE"], ["ACOL"])
+    cp(T.CF[:], T.CI5[:], ["CI5"], ["CF"])
     ts(T.OB[:], T.CF[:, 0:8], PGRP, A.is_equal, ["CF", "PC0"], ["OB"], 4096.0, A.mult)
     ts(T.IDF[:], T.CF[:, 0:128], PP, A.is_equal, ["CF", "PC4"], ["IDF"])
     ts(T.PEN[:], T.IDF[:], float(2 ** 25), A.mult, ["IDF"], ["PEN"])
     ms(T.ZB[:], 0.0, ["ZB"])
-    ts(T.CT1[:, 0:256], T.CI5[:, 0:256], 7, A.bitwise_and, ["CI5"], ["CT1"])
-    ts(T.RS8[:], T.CT1[:, 0:256], 0.0, A.is_equal, ["CT1"], ["RS8"], float(2 ** 26), A.mult)
-    ts(T.CT1[:, 0:256], T.CI5[:, 0:256], 15, A.bitwise_and, ["CI5"], ["CT1"])
-    ts(T.RS16[:], T.CT1[:, 0:256], 0.0, A.not_equal, ["CT1"], ["RS16"])
-    ts(T.DIAG[:], T.CT1[:, 0:256], PLOW, A.is_equal, ["CT1", "PC0"], ["DIAG"])
-    ts(T.CT2[:, 0:256], T.CI5[:, 0:256], 4, A.arith_shift_right, ["CI5"], ["CT2"])
-    ts(T.DG2[:], T.CT2[:, 0:256], PLOW, A.is_equal, ["CT2", "PC0"], ["DG2"])
-    ts(T.CT2[:, 0:128], T.CI5[:, 0:128], 2, A.arith_shift_right, ["CI5", "DG2"], ["CT2"], 3, A.bitwise_and)
-    ts(T.M1[:], T.CT2[:, 0:128], PL3, A.is_equal, ["CT2", "PC0"], ["M1"])
+    ts(T.CT1[:], T.CI5[:], 7, A.bitwise_and, ["CI5"], ["CT1"])
+    ts(T.RS8[:], T.CT1[:], 0.0, A.is_equal, ["CT1"], ["RS8"], float(2 ** 26), A.mult)
     ts(T.RS1[:], T.CF[:, 0:32], PS2, A.is_equal, ["CF", "PC0"], ["RS1"])
-    op("g", lambda: g.iota(T.LXI[:, 0:8], [[32, 8]], 7, 0), [], ["LXI"])
-    ts(T.LXJ[:, 0:8], T.LXI[:, 0:8], 0, A.add, ["LXI"], ["LXJ"])
     ts(T.PC[:, 5:6], PL3, 8.0, A.mult, ["PC0"], ["PC5"])
     ts(T.LX1[:], T.LXI[:, 0:8], T.PC[:, 5:6], A.add, ["LXI", "PC5"], ["LX1"])
     ts(T.PT[:, 6:7], T.PI[:, 0:1], 2, A.arith_shift_right, ["PI"], ["PT6"], 3, A.bitwise_and)
     ts(T.PC[:, 6:7], T.PT[:, 6:7], 8.0, A.mult, ["PT6"], ["PC6"])
     ts(T.LX3[:], T.LXI[:, 0:8], T.PC[:, 6:7], A.add, ["LXI", "PC6"], ["LX3"])
-    ts(T.CT2[:, 0:16], T.CI5[:, 0:16], 7, A.bitwise_and, ["CI5", "M1"], ["CT2"])
-    ts(T.CT1[:, 0:16], T.CI5[:, 0:16], 3, A.arith_shift_right, ["CI5", "DIAG", "RS16"], ["CT1"])
-    ts(T.LXJ[:], T.CT2[:, 0:16], 2.0, A.mult, ["CT2"], ["LXJ"])
-    tt(T.LXI[:], T.LXJ[:], T.CT1[:, 0:16], A.add, ["LXJ", "CT1"], ["LXI"])
-    cp(T.LX2[:], T.LXI[:], ["LXI"], ["LX2"])
-    cp(T.LX4[:], T.CI5[:, 0:16], ["CI5"], ["LX4"])
-    ms(T.CA[:, 0:16], 0.0, ["CA"])
-    ts(T.LX5[:], T.CA[:, 0:16], PLOW, A.add, ["CA", "PC0"], ["LX5"])
     for i, r in enumerate((12, 13, 14, 15)):
         ts(T.PC[:, 8 + i:9 + i], PLOW, float(r), A.is_equal, ["PC0"], ["PC%d" % (8 + i)])
     I12, I13, I14, I15 = [T.PC[:, 8 + i:9 + i] for i in range(4)]
     ts(T.PC[:, 12:13], PLOW, 12.0, A.is_lt, ["PC0"], ["PC12"])
-    ts(T.CL[:], T.CF[:, 0:256], I13, A.mult, ["CF", "PC9"], ["CL"])
-    ts(T.PC[:, 13:14], T.PC[:, 12:13], 128.0, A.mult, ["PC12"], ["PC13"])
-    ts(T.PC[:, 14:15], I14, 2048.0, A.mult, ["PC10"], ["PC14"])
-    tt(T.PC[:, 13:14], T.PC[:, 13:14], I12, A.add, ["PC13", "PC8"], ["PC13"])
-    ts(T.CL[:], T.CL[:], T.PC[:, 13:14], A.add, ["CL", "PC13", "PC14"], ["CL"], T.PC[:, 14:15], A.add)
-    ts(T.CR[:], T.CF[:, 0:256], I12, A.mult, ["CF", "PC8"], ["CR"], -1.0, A.mult)
-    tt(T.PC[:, 15:16], T.PC[:, 12:13], I13, A.add, ["PC12", "PC9"], ["PC15"])
-    ts(T.CR[:], T.CR[:], T.PC[:, 15:16], A.add, ["CR", "PC15", "PC10"], ["CR"], I14, A.add)
-    ts(T.WF2[:, 4:5], PLOW, 14.0, A.is_lt, ["PC0"], ["WF4"], -2.0, A.mult)
-    tt(T.WF2[:, 4:5], T.WF2[:, 4:5], I14, A.add, ["WF4", "PC10"], ["WF4"])
-    ts(T.RC[:], T.CF[:, 0:256], 16.0, A.mult, ["CF"], ["RC"], I15, A.mult)
-    ts(T.RC[:], T.RC[:], T.WF2[:, 4:5], A.add, ["RC", "WF4"], ["RC"])
+    ts(T.PT[:, 4:5], T.PI[:, 0:1], 4, A.arith_shift_right, ["PI"], ["PT4"], 1, A.bitwise_and)
     cp(T.WF2[:, 5:6], T.PT[:, 4:5], ["PT4"], ["WF5"])
     ts(T.WF2[:, 6:7], T.WF2[:, 5:6], -1.0, A.mult, ["WF5"], ["WF6"], 1.0, A.add)
     ECOL, OCOL = T.WF2[:, 6:7], T.WF2[:, 5:6]
-    ts(T.CT1[:, 0:256], T.CI5[:, 0:256], 4, A.arith_shift_right, ["CI5", "LXI"], ["CT1"], 7, A.bitwise_and)
-    ts(T.CA[:, 0:256], T.CT1[:, 0:256], 4.0, A.is_lt, ["CT1"], ["CA"], 1536.0, A.mult)
-    ts(T.CB[:, 0:256], T.DIAG[:], 0.0, A.is_equal, ["DIAG"], ["CB"], 1e25, A.mult)
-    tt(T.TH2[:], T.CA[:, 0:256], T.CB[:, 0:256], A.max, ["CA", "CB"], ["TH2"])
-    ts(RH, T.CF[:, 0:8], PGRP, A.is_equal, ["CF", "PC0"], ["RH"], float(DUM), A.mult)
-    ts(RL0, T.CF[:, 0:8], PGRP, A.is_equal, ["CF", "PC0", "PC4"], ["RL0"], PP, A.mult)
-    ts(T.WF2[:, 7:8], PP, 128.0, A.add, ["PC4"], ["WF7"])
-    ts(RL1, T.CF[:, 0:8], PGRP, A.is_equal, ["CF", "PC0", "WF7"], ["RL1"], T.WF2[:, 7:8], A.mult)
-    ts(T.CT1[:, 0:128], T.CI5[:, 0:128], 4, A.arith_shift_right, ["CI5"], ["CT1"])
-    ts(GB, T.CT1[:, 0:128], PGRP, A.is_equal, ["CT1", "PC0"], ["GB"])
-    cp(T.GBH[:], GB, ["GB"], ["GBH"])
-    ts(SR15, GB, I15, A.mult, ["GB", "PC11"], ["SR15"])
-    ts(SR14, GB, I14, A.mult, ["GB", "PC10"], ["SR14"])
-    ts(T.CT2[:, 0:128], T.CI5[:, 0:128], 15, A.bitwise_and, ["CI5", "LXJ"], ["CT2"])
-    ts(T.CA[:, 0:128], T.CT2[:, 0:128], 14.0, A.is_ge, ["CT2"], ["CA"])
-    tt(SRN, T.CA[:, 0:128], GB, A.mult, ["CA", "GB"], ["SRN"])
-    ms(T.ONES[:], 1.0, ["ONES"])
     ms(T.FBC[:], 16777215.0, ["FBC"])
     ms(T.FB4C[:], 16777215.0, ["FB4C"])
-    ms(T.CA[:], 0.0, ["CA"])
-    ts(T.TB[:, W:WX], T.CA[:], I14, A.add, ["CA", "PC10"], ["TBx"])
-    ts(T.TA[:, W:WX], T.CA[:], I14, A.add, ["CA", "PC10"], ["TAx"])
-    ms(T.XC0[:, W:WX], 0.0, ["XC0x"])
-    ms(T.XC1[:, W:WX], 0.0, ["XC1x"])
-    wr["TB"] = deps(["TBd", "TBx"], [])
-    fill_table(T.TA, "TAd", T.PD[2], T.PD[3], "PD1")
-    wr["TA"] = deps(["TAd", "TAx"], [])
 
-    def row_to_list(src, lhsT, rows, out, okey, bank, bkey, fin):
-        op("p", mm(bank[:, 0:256], lhsT, src, True, True), rows, [bkey])
-        tt(T.DM[:], bank[:, 0:256], T.DIAG[:], A.mult, [bkey, "DIAG"], ["DM"])
-        scan(T.SC[:], T.RS16[:], T.DM[:], A.mult, A.add, ["RS16", "DM"], ["SC"])
-        fin(T.SC[:, 15:256:16])
+    def late_constants():
+        ts(T.CL[:], T.CF[:], I13, A.mult, ["CF", "PC9"], ["CL"])
+        ts(T.PC[:, 13:14], T.PC[:, 12:13], 128.0, A.mult, ["PC12"], ["PC13"])
+        ts(T.PC[:, 14:15], I14, 2048.0, A.mult, ["PC10"], ["PC14"])
+        tt(T.PC[:, 13:14], T.PC[:, 13:14], I12, A.add, ["PC13", "PC8"], ["PC13"])
+        ts(T.CL[:], T.CL[:], T.PC[:, 13:14], A.add, ["CL", "PC13", "PC14"], ["CL"], T.PC[:, 14:15], A.add)
+        ts(T.CR[:], T.CF[:], I12, A.mult, ["CF", "PC8"], ["CR"], -1.0, A.mult)
+        tt(T.PC[:, 15:16], T.PC[:, 12:13], I13, A.add, ["PC12", "PC9"], ["PC15"])
+        ts(T.CR[:], T.CR[:], T.PC[:, 15:16], A.add, ["CR", "PC15", "PC10"], ["CR"], I14, A.add)
+        ms(T.CA[:], 0.0, ["CA"])
+        ts(T.TB[:, W:WX], T.CA[:], I14, A.add, ["CA", "PC10"], ["TBx"])
+        wr["TB"] = deps(["TBd", "TBx"], [])
 
-    cp(T.W1[:], T.PG4[:, 256:512:16], ["PG41"], ["W1"])
-    tt(T.E4[:], T.W1[:, 0:16].indirect(T.LX5[:]), T.DG2[:], A.mult, ["W1", "LX5", "DG2"], ["E4"])
+    def later_constants():
+        ts(T.CT2[:, 0:16], T.CI5[:, 0:16], 7, A.bitwise_and, ["CI5"], ["CT2"])
+        ts(T.CT1[:, 0:16], T.CI5[:, 0:16], 3, A.arith_shift_right, ["CI5"], ["CT1"])
+        ts(T.LXJ[:], T.CT2[:, 0:16], 2.0, A.mult, ["CT2"], ["LXJ"])
+        tt(T.LXI[:], T.LXJ[:], T.CT1[:, 0:16], A.add, ["LXJ", "CT1"], ["LXI"])
+        cp(T.LX2[:], T.LXI[:], ["LXI"], ["LX2"])
+        ts(T.CT1[:], T.CI5[:], 4, A.arith_shift_right, ["CI5"], ["CT1"], 7, A.bitwise_and)
+        ts(T.CA[:, 0:256], T.CT1[:], 4.0, A.is_lt, ["CT1"], ["CA"], 1536.0, A.mult)
+        ts(T.CB[:], T.DIAG[:], 0.0, A.is_equal, ["DIAG"], ["CB"], 1e25, A.mult)
+        tt(T.TH2[:], T.CA[:, 0:256], T.CB[:], A.max, ["CA", "CB"], ["TH2"])
+        ts(RH, T.CF[:, 0:8], PGRP, A.is_equal, ["CF", "PC0"], ["RH"], float(DUM), A.mult)
+        ts(RL0, T.CF[:, 0:8], PGRP, A.is_equal, ["CF", "PC0", "PC4"], ["RL0"], PP, A.mult)
+        ts(T.WF2[:, 7:8], PP, 128.0, A.add, ["PC4"], ["WF7"])
+        ts(RL1, T.CF[:, 0:8], PGRP, A.is_equal, ["CF", "PC0", "WF7"], ["RL1"], T.WF2[:, 7:8], A.mult)
+        ts(T.WF2[:, 4:5], PLOW, 14.0, A.is_lt, ["PC0"], ["WF4"], -2.0, A.mult)
+        tt(T.WF2[:, 4:5], T.WF2[:, 4:5], I14, A.add, ["WF4", "PC10"], ["WF4"])
+        ts(T.RC[:], T.CF[:], 16.0, A.mult, ["CF"], ["RC"], I15, A.mult)
+        ts(T.RC[:], T.RC[:], T.WF2[:, 4:5], A.add, ["RC", "WF4"], ["RC"])
 
-    def dead_done(t):
-        def fin(ap):
-            ts(T.DSND[:, 16 * t:16 * t + 16], ap, 1.0, A.min, ["SC"], ["DSND%d" % t], DEAD, A.mult)
-            send(nxt if t % 2 == 0 else prv, "e%d" % t, T.DLAND[:, 16 * t:16 * t + 16], T.DSND[:, 16 * t:16 * t + 16], ["DSND%d" % t])
-        return fin
-
-    row_to_list(T.E4[:], T.GBH[:], ["E4", "GBH"], None, None, T.G3, "G3", dead_done(0))
-
-    def near_back(t):
-        near, nk = (T.TA, "TA") if t % 2 == 0 else (T.TB, "TB")
-        landed(nxt if t % 2 == 0 else prv, "r%d" % t, ["RLAND%d" % t])
-        tt(T.E3[:], T.RLAND[:, 16 * t:16 * t + 16].indirect(T.LX4[:]), T.DIAG[:], A.mult, ["RLAND%d" % t, "LX4", "DIAG"], ["E3"])
-        op("p", mm(T.G4[:, 0:256], SRN, T.E3[:], True, True), ["SRN", "E3"], ["G4"])
-        tt(near[:, t:W:16], T.G4[:, 0:256], near[:, t:W:16], A.add, ["G4", nk], [nk])
+    def last_constants():
+        ms(T.ONES[:], 1.0, ["ONES"])
+        cp(GB, T.GBH[:], ["GBH"], ["GB"])
+        ts(SR15, GB, I15, A.mult, ["GB", "PC11"], ["SR15"])
+        ts(SR14, GB, I14, A.mult, ["GB", "PC10"], ["SR14"])
+        ts(T.CT2[:, 0:128], T.CI5[:, 0:128], 15, A.bitwise_and, ["CI5"], ["CT2"])
+        ts(T.CA[:, 0:128], T.CT2[:, 0:128], 14.0, A.is_ge, ["CT2"], ["CA"])
+        tt(SRN, T.CA[:, 0:128], GB, A.mult, ["CA", "GB"], ["SRN"])
+        cp(T.LX4[:], T.CI5[:, 0:16], ["CI5"], ["LX4"])
+        ms(T.CA[:], 0.0, ["CA"])
+        ts(T.TA[:, W:WX], T.CA[:], I14, A.add, ["CA", "PC10"], ["TAx"])
+        wr["TA"] = deps(["TAd", "TAx"], [])
 
     BANKS = [T.G0, T.G1, T.G2, T.G3, T.G4, T.G5]
     for t in range(NB):
         frm, to = (prv, nxt) if t % 2 == 0 else (nxt, prv)
-        far, fk, near, nk = (T.TB, "TB", T.TA, "TA") if t % 2 == 0 else (T.TA, "TA", T.TB, "TB")
+        far, fk = (T.TB, "TB") if t % 2 == 0 else (T.TA, "TA")
         XC, xk = (T.XC0, "XC0") if t % 2 == 0 else (T.XC1, "XC1")
         for d in range(ND):
             m = t * ND + d
@@ -356,67 +355,95 @@ def rank_program(g, core, T, topo):
                 cp(XC[:, 0:WX].indirect(T.LLAND[:, 16 * pm:16 * pm + 16]), T.NLAND[:, 256 * pm:256 * pm + 256],
                    ["NLAND%d" % pm, "LLAND%d" % pm], [xk])
                 cp(T.Z[:], XC[:, 0:WX].indirect(T.PU[:]), [xk, "PU"], ["Z"])
+
+            def result():
+                ts(T.W3[:], T.YQ[:], 1.0, A.add, ["YQ"], ["W3"])
+                tt(T.W2[:], T.W3[:], T.WB[:], A.mult, ["W3", "WB"], ["W2"])
+                tt(T.RES[:], T.RES[:], T.W2[:], A.add, ["RES", "W2"], ["RES"])
+
             fs = []
-            zs = (lambda ll: T.SLAND[:, 256 * t + ll:256 * t + 256:4]) if d == 0 else (lambda ll: T.Z[:, ll:256:4])
             for ll in range(4):
-                fs.append(mm(T.K6[:, 0:64], T.WH[:, 128 * ll:128 * ll + 128], zs(ll), ll == 0, False))
-                fs.append(mm(T.K6[:, 0:64], T.WL[:, 128 * ll:128 * ll + 128], zs(ll), False, ll == 3))
-            op("p", fs, ["WH", "WL", zk], ["K6"])
+                zs = T.SLAND[:, 256 * t + ll:256 * t + 256:4] if d == 0 else T.Z[:, ll:256:4]
+                fs.append(mm(T.K6[:, 0:64], T.WH[:, 128 * ll:128 * ll + 128], zs, ll == 0, False))
+                fs.append(mm(T.K6[:, 0:64], T.WL[:, 128 * ll:128 * ll + 128], zs, False, ll == 3))
+            op("p", fs, WHL + [zk], ["K6"])
             for cl in range(4):
-                cp(T.Z4[:, cl:1024:4], z, [zk] + (["Z4"] if cl == 9 else []), ["Z4_%d" % cl])
+                cp(T.Z4[:, cl:1024:4], z, [zk], ["Z4_%d" % cl])
             ts(T.NI[:], T.K6[:, 0:64], -0.5, A.add, ["K6"], ["NI"])
             tt(T.UF[:], T.K6[:, 0:64], T.NI[:], A.subtract, ["K6", "NI"], ["UF"])
             for ch in range(4):
                 act(T.SQ[:, 64 * ch:64 * ch + 64], T.UF[:], F.Square, ["UF", "SCOL"], ["SQ%d" % ch], bias=T.SCOL[:, ch:ch + 1], scale=4096.0)
-            for ch in range(4):
-                ts(T.FI[:, 64 * ch:64 * ch + 64], T.SQ[:, 64 * ch:64 * ch + 64], T.ACOL[:, ch:ch + 1], A.add, ["SQ%d" % ch, "ACOL"], ["FI%d" % ch], 1.0 / 32, A.mult)
-            ts(T.CI[:], T.FI[:], 4095, A.bitwise_and, ["FI0", "FI1", "FI2", "FI3"], ["CI"])
-            cp(T.OFF[:], T.CI[:], ["CI"], ["OFF"])
+
+            def places(c0, c1):
+                for ch in range(c0, c1):
+                    ts(T.FI[:, 64 * ch:64 * ch + 64], T.SQ[:, 64 * ch:64 * ch + 64], T.ACOL[:, ch:ch + 1], A.add, ["SQ%d" % ch, "ACOL"], ["FI%d" % ch], 1.0 / 32, A.mult)
+                keys = [str(ch) for ch in range(c0, c1)]
+                ts(T.CI[:, 64 * c0:64 * c1], T.FI[:, 64 * c0:64 * c1], 4095, A.bitwise_and, ["FI" + c for c in keys], ["CI" + c for c in keys])
+                cp(T.OFF[:, 64 * c0:64 * c1], T.CI[:, 64 * c0:64 * c1], ["CI" + c for c in keys], ["OFF" + c for c in keys])
+
             if d == 0:
                 act(T.SH[:], z, F.Copy, [zk], ["SH"], bias=-0.5)
-            pend = []
 
-            def gather(hc):
-                a = 512 * hc
-                tt(T.DF[:, a:a + 512], T.X[:, 0:WX].indirect(T.OFF[:, 32 * hc:32 * hc + 32]), T.Z4[:, 512 * (hc % 2):512 * (hc % 2) + 512], A.subtract,
-                   ["X", "OFF", "Z4_0", "Z4_1", "Z4_2", "Z4_3"], ["DF%d" % hc])
-                act(T.AB[:, a:a + 512], T.DF[:, a:a + 512], F.Abs, ["DF%d" % hc], ["AB%d" % hc])
+            def gather(c0, n):
+                a, b, zo = 16 * c0, 16 * (c0 + n), 16 * (c0 % 64)
+                tt(T.DF[:, a:b], T.X[:, 0:WX].indirect(T.OFF[:, c0:c0 + n]), T.Z4[:, zo:zo + 16 * n], A.subtract,
+                   ["X", "OFF%d" % (c0 // 64), "Z4_0", "Z4_1", "Z4_2", "Z4_3"], ["DF%d" % c0])
+                act(T.AB[:, a:b], T.DF[:, a:b], F.Abs, ["DF%d" % c0], ["AB%d" % c0])
 
-            def dsum(c0, n, p0, pr, keys, stop):
+            def dsum(c0, n, p0, pr, keys):
                 fs = []
                 for part in range(16):
                     o = 2 * part + pr
                     fs.append(mm(T.K6[p0:p0 + n, o:256:32], T.AB[:, 16 * c0 + part:16 * (c0 + n):16], T.OB[:], False, False))
-                if stop:
-                    fs.append(mm(T.K6[:, 0:256], T.ZB[:, 0:128], T.ZB[:], False, True))
                 op("p", fs, keys + ["OB"], ["K6"])
 
-            gather(0)
-            cp(T.CFL[:], T.CI[:], ["CI"], ["CFL"])
+            places(0, 1)
+            gather(0, 32)
+            places(1, 4)
+            gather(32, 32)
+            cis = ["CI0", "CI1", "CI2", "CI3"]
+            cp(T.CFL[:], T.CI[:], cis, ["CFL"])
             op("p", [mm(T.K6[:, 0:256], T.ZB[:, 0:128], T.ZB[:], True, False)] +
                [mm(T.K6[:, pr:256:2], T.CFL[:, 128 * pr:128 * pr + 128], T.IDF[:], False, False) for pr in range(2)], ["ZB", "CFL", "IDF"], ["K6"])
+            gather(64, 32)
+            gather(96, 32)
+            dsum(0, 128, 0, 0, ["AB0", "AB32", "AB64", "AB96"])
+            gather(128, 32)
+            gather(160, 32)
+            dsum(128, 64, 0, 1, ["AB128", "AB160"])
+            if d == 0 and t > 0:
+                near_rows(t - 1)
+            gather(192, 32)
+            dsum(192, 32, 64, 1, ["AB192"])
+            gather(224, 16)
+            gather(240, 16)
             if d > 0:
                 for ch in range(4):
-                    tt(T.EQ[:, 64 * ch:64 * ch + 64], T.CI[:, 64 * ch:64 * ch + 64], T.LAST[:], A.is_equal, ["CI", "LAST"], ["EQ%d" % ch])
+                    tt(T.EQ[:, 64 * ch:64 * ch + 64], T.CI[:, 64 * ch:64 * ch + 64], T.LAST[:], A.is_equal, ["CI%d" % ch, "LAST"], ["EQ%d" % ch])
+            dsum(224, 32, 96, 1, ["AB224", "AB240"])
+            if d > 0:
                 op("p", [mm(T.K6[:, pr:256:2], T.EQ[:, 128 * pr:128 * pr + 128], T.PEN[:], False, False) for pr in range(2)], ["EQ0", "EQ1", "EQ2", "EQ3", "PEN"], ["K6"])
-            gather(1); gather(2); gather(3)
-            dsum(0, 128, 0, 0, ["AB0", "AB1", "AB2", "AB3"], False)
+            op("p", mm(T.K6[:, 0:256], T.ZB[:, 0:128], T.ZB[:], False, True), ["ZB"], ["K6"])
             if d == 0:
                 landed(frm, "e%d" % t, ["DLAND%d" % t])
                 cp(T.DEADL[:], T.DLAND[:, 16 * t:16 * t + 16], ["DLAND%d" % t], ["DEADL"])
                 ms(T.RES[:], 0.0, ["RES"])
                 if t > 0:
-                    near_back(t - 1)
+                    near_add(t - 1)
                     ts(T.RC[:], T.RC[:], I15, A.add, ["RC", "PC11"], ["RC"])
-            gather(4); gather(5)
-            dsum(128, 64, 0, 1, ["AB4", "AB5"], False)
-            gather(6)
-            dsum(192, 32, 64, 1, ["AB6"], False)
-            gather(7)
-            dsum(224, 32, 96, 1, ["AB7"], True)
+                else:
+                    late_constants()
+            else:
+                ts(T.W1[:], T.WB[:], DEAD, A.mult, ["WB"], ["W1"])
+                tt(T.DEADL[:], T.DEADL[:], T.W1[:], A.max, ["DEADL", "W1"], ["DEADL"])
+                ts(T.FB[:], T.YA[:], BAR, A.add, ["YA"], ["FB"])
+                result()
             scan(T.R[:], T.RS8[:], T.K6[:, 0:256], A.max, A.min, ["RS8", "K6"], ["R"])
             tt(T.E1[:], T.R[:, 0:256].indirect(T.LX1[:]), T.M1[:], A.mult, ["R", "LX1", "M1"], ["E1"])
             op("p", mm(T.C7[:, 0:32], T.E1[:], T.RS1[:], True, True), ["E1", "RS1"], ["C7"])
+            if not tail:
+                act(T.R4[:], T.R[:, 0:256].indirect(T.LX3[:]), F.Copy, ["R", "LX3"], ["R4"])
+                op("p", mm(T.K6[:, 0:128], T.R4[:], T.IDF[:], True, True), ["R4", "IDF"], ["K6"])
             fb, fbk = (T.FBC, "FBC") if d == 0 else (T.FB, "FB")
             tt(T.MN[:], T.C7[:, 16:32], fb[:], A.min, ["C7", fbk], ["MN"])
             tt(T.YI[:], T.C7[:, 0:16], T.MN[:], A.min, ["C7", "MN"], ["YI"])
@@ -433,19 +460,41 @@ def rank_program(g, core, T, topo):
             act(ns, T.T2[:], F.Copy, ["T2"], ["NSND%d" % m], bias=-8388608.0)
             if not tail:
                 send(to, "n%d%d" % (t, d), T.NLAND[:, 256 * m:256 * m + 256], ns, ["NSND%d" % m])
-            for n, gr in enumerate((0, 4, 2, 6, 1, 5, 3, 7)):
-                b, bk = BANKS[n % 6], "G%d" % (n % 6)
-                qa, qk = (T.QE, "QE") if gr % 2 == 0 else (T.QO, "QO")
-                p0 = 32 * (gr // 2)
-                op("p", [mm(b[:, 0:128], qa[p0:p0 + 32, 0:128], T.QR[p0:p0 + 32, 0:128], True, True),
-                         mm(b[:, 128:384], qa[p0:p0 + 32, 128:256], T.QR[p0:p0 + 32, 0:256], True, True)], [qk, "QR"], [bk])
-                for h in range(2):
-                    src = b[:, 0:128] if h == 0 else b[:, 128:384]
-                    o = T.FL[:, 2 * gr + h:2 * gr + h + 1]
-                    if gr < 4:
-                        op("v", lambda: g.vector.tensor_reduce(o, src, AxisListType.X, A.max), [bk], ["FL%d_%d" % (gr, h)])
-                    else:
-                        act(T.JK[:, 0:(128 if h == 0 else 256)], src, F.Relu, [bk], ["JK", "FL%d_%d" % (gr, h)], bias=-1536.0, accum_out=o)
+
+            def fill(n):
+                if n == 0:
+                    tt(T.UP[:], far[:, 0:WX].indirect(T.YU[:]), T.RC[:], A.max, [fk, "YU", "RC"], ["UP"])
+                if not tail:
+                    f4, f4k = (T.FB4C, "FB4C") if d == 0 else (T.FB4, "FB4")
+                    if n == 1:
+                        tt(T.L1[:], T.K6[:, 64:128], f4[:], A.min, ["K6", f4k], ["L1"])
+                        tt(T.L2[:], T.K6[:, 0:64], T.L1[:], A.min, ["K6", "L1"], ["L2"])
+                    if n == 2:
+                        ts(T.LAST[:], T.L2[:], 4095, A.bitwise_and, ["L2"], ["LAST"])
+                        if d == 0:
+                            ts(T.FB4[:], T.LAST[:], BAR, A.add, ["LAST"], ["FB4"])
+
+            if m == 0:
+                later_constants()
+            n = 0
+            for i, (gs, gv) in enumerate(((4, 0), (6, 2), (5, 1), (7, 3))):
+                for h in (1, 0):
+                    for gr in (gs, gv):
+                        b, bk = BANKS[n % 6], "G%d" % (n % 6)
+                        n += 1
+                        qa, qk = (T.QE, "QE") if gr % 2 == 0 else (T.QO, "QO")
+                        p0 = 32 * (gr // 2)
+                        w = 128 + 128 * h
+                        op("p", mm(b[:, 0:w], qa[p0:p0 + 32, 128 * h:128 * h + 128], T.QR[p0:p0 + 32, 0:w], True, True), [qk, "QR"], [bk])
+                        src = b[:, 0:w]
+                        o = T.FL[:, 2 * gr + h:2 * gr + h + 1]
+                        if gr < 4:
+                            op("v", lambda: g.vector.tensor_reduce(o, src, AxisListType.X, A.max), [bk], ["FL%d_%d" % (gr, h)])
+                        else:
+                            act(T.JK[:, 0:w], src, F.Relu, [bk], ["JK", "FL%d_%d" % (gr, h)], bias=-1536.0, accum_out=o)
+                fill(i)
+            if m == 0:
+                last_constants()
             tt(T.E2[:], T.FL[:, 0:16].indirect(T.LX2[:]), T.TH2[:], A.is_gt, ["FL%d_%d" % (i, h) for i in range(8) for h in range(2)] + ["LX2", "TH2"], ["E2"])
             fs = []
             for h in range(2):
@@ -462,46 +511,30 @@ def rank_program(g, core, T, topo):
                 cp(T.X[:, 0:WX].indirect(ls), ns, [lk, "NSND%d" % m], ["X"])
                 if t + 1 < NB:
                     start_batch(t + 1)
-            tt(T.UP[:], far[:, 0:WX].indirect(T.YU[:]), T.RC[:], A.max, [fk, "YU", "RC"], ["UP"])
+            ts(T.WB[:], T.LF[:], float(DUM), A.is_lt, ["LF"], ["WB"])
+            if not (tail and t + 1 == NB):
+                op("p", mm(T.G0[:, 0:16], T.ONES[:], T.WB[:], True, True), ["ONES", "WB"], ["G0"])
+            if tail:
+                result()
+                near_send(t)
             cp(far[:, 0:WX].indirect(ls), T.UP[:], ["UP", lk], [fk])
             if not tail:
                 act(T.PG[:], far[:, 0:WX].indirect(T.YU[:]), F.Copy, [fk, "YU"], ["PG"])
-            ts(T.WB[:], T.LF[:], float(DUM), A.is_lt, ["LF"], ["WB"])
-            op("p", mm(T.G0[:, 0:16], T.ONES[:], T.WB[:], True, True), ["ONES", "WB"], ["G0"])
-            ts(T.W3[:], T.YQ[:], 1.0, A.add, ["YQ"], ["W3"])
-            tt(T.W2[:], T.W3[:], T.WB[:], A.mult, ["W3", "WB"], ["W2"])
-            tt(T.RES[:], T.RES[:], T.W2[:], A.add, ["RES", "W2"], ["RES"])
-            if not tail:
-                row_to_list(T.PG[:], SR15, ["PG", "SR15"], None, None, T.G2, "G2",
-                            lambda ap: cp(T.PU[:], ap, ["SC"], ["PU"]))
-                ts(T.W1[:], T.WB[:], DEAD, A.mult, ["WB"], ["W1"])
-                tt(T.DEADL[:], T.DEADL[:], T.W1[:], A.max, ["DEADL", "W1"], ["DEADL"])
-                ts(T.FB[:], T.YA[:], BAR, A.add, ["YA"], ["FB"])
-                act(T.R4[:], T.R[:, 0:256].indirect(T.LX3[:]), F.Copy, ["R", "LX3"], ["R4"])
-                op("p", mm(T.G1[:, 0:128], T.R4[:], T.IDF[:], True, True), ["R4", "IDF"], ["G1"])
-                f4, f4k = (T.FB4C, "FB4C") if d == 0 else (T.FB4, "FB4")
-                tt(T.L1[:], T.G1[:, 64:128], f4[:], A.min, ["G1", f4k], ["L1"])
-                tt(T.L2[:], T.G1[:, 0:64], T.L1[:], A.min, ["G1", "L1"], ["L2"])
-                ts(T.LAST[:], T.L2[:], 4095, A.bitwise_and, ["L2"], ["LAST"])
-                if d == 0:
-                    ts(T.FB4[:], T.LAST[:], BAR, A.add, ["LAST"], ["FB4"])
                 cp(T.X[:, 0:WX].indirect(ls), ns, [lk, "NSND%d" % m], ["X"])
-            else:
-                cp(T.RSND[:, 16 * t:16 * t + 16], T.RES[:], ["RES"], ["RSND%d" % t])
-                send(frm, "r%d" % t, T.RLAND[:, 16 * t:16 * t + 16], T.RSND[:, 16 * t:16 * t + 16], ["RSND%d" % t])
-            if t + 1 < NB or not tail:
+            if not (tail and t + 1 == NB):
                 op("v", lambda: g.vector.tensor_reduce(T.KP[:, 0:1], T.G0[:, 0:16], AxisListType.X, A.add), ["G0"], ["KP0"])
                 cp(T.KI[:, 0:1], T.KP[:, 0:1], ["KP0"], ["KI0"])
                 ts(T.KI[:, 1:2], T.KI[:, 0:1], 31, A.bitwise_and, ["KI0"], ["KI1"])
                 ts(T.KP[:, 1:2], T.KI[:, 1:2], 32.0, A.mult, ["KI1"], ["KP1"])
                 ts(T.ACOL[:], T.ABASE[:], T.KP[:, 1:2], A.add, ["ABASE", "KP1"], ["ACOL"], 3104.0 * ((d + 1) % ND), A.add)
-            if tail and t + 1 < NB:
-                row_to_list(far[:, t + 1:W:16], SR14, [fk, "SR14"], None, None, T.G3, "G3", dead_done(t + 1))
+            if not tail:
+                row_to_list(T.PG[:], SR15, ["PG", "SR15"], T.G2, "G2", lambda ap: cp(T.PU[:], ap, ["SC"], ["PU"]))
+            elif t + 1 < NB:
+                row_to_list(far[:, t + 1:W:16], SR14, [fk, "SR14"], T.G3, "G3", dead_done(t + 1))
     dma("y", [(T.yx[:], T.X[:, 0:W])], ["X"], ["yx"])
     dma("y", [(T.yb[:], T.TB[15:128:16, 0:W])], ["TB"], ["yb"])
-    near_back(NB - 1)
+    near_rows(NB - 1)
+    near_add(NB - 1)
     dma("y", [(T.ya[:], T.TA[15:128:16, 0:W])], ["TA"], ["ya"])
     for sem in sorted(last):
-        q = "g"
-        if waited[q].get(sem, 0) < last[sem]:
-            need(q, {sem: last[sem]})
+        need("g", {sem: last[sem]})

@@ -26,7 +26,9 @@ _sb("OB", 8, "bfloat16"); _sb("IDF", 128, "float32"); _sb("PEN", 128, "bfloat16"
 _sb("DIAG", 256, "float32"); _sb("DG2", 256, "float32"); _sb("M1", 128, "float32"); _sb("RS1", 32, "float32")
 _sb("CL", 256, "float32"); _sb("CR", 256, "float32"); _sb("RC", 256, "float32"); _sb("TH2", 256, "float32")
 _sb("RHL", 24, "bfloat16")
-_sb("SRM", 512, "float32")
+_sb("SR14", 128, "float32")
+_sb("SRB", 384, "bfloat16")
+_sb("IBN", 256, "bfloat16")
 _sb("GBH", 128, "bfloat16"); _sb("ONES", 128, "bfloat16")
 _sb("RS8", 256, "float32"); _sb("RS16", 256, "float32")
 _sb("LX1", 8, "uint16"); _sb("LX2", 16, "uint16"); _sb("LX3", 8, "uint16"); _sb("LX4", 16, "uint16"); _sb("LX5", 16, "uint16")
@@ -37,7 +39,7 @@ _sb("SSND", 256 * NB, "bfloat16"); _sb("SLAND", 256 * NB, "bfloat16")
 _sb("DSND", 16 * NB, "float32"); _sb("DLAND", 16 * NB, "float32")
 _sb("NSND", 256 * NB * ND, "bfloat16"); _sb("NLAND", 256 * NB * ND, "bfloat16")
 _sb("LSND", 16 * NB * ND, "uint16"); _sb("LLAND", 16 * NB * ND, "uint16")
-_sb("RSND", 16 * NB, "float32"); _sb("RLAND", 16 * NB, "float32")
+_sb("RSND", 32 * NB, "float32"); _sb("RLAND", 32 * NB, "float32")
 _sb("Z", 256, "bfloat16"); _sb("Z4", 1024, "bfloat16"); _sb("SH", 256, "float32")
 _sb("NI", 64, "int32"); _sb("UF", 64, "float32"); _sb("SQ", 256, "float32"); _sb("FI", 256, "int32"); _sb("CI", 256, "int32")
 _sb("OFF", 256, "uint16"); _sb("CFL", 256, "float32"); _sb("EQ", 256, "bfloat16")
@@ -46,9 +48,9 @@ _sb("R", 256, "float32"); _sb("E1", 128, "float32"); _sb("R4", 128, "float32")
 _sb("MN", 16, "float32"); _sb("YI", 16, "int32"); _sb("YA", 16, "int32"); _sb("YQ", 16, "float32"); _sb("YU", 16, "uint16")
 _sb("FB", 16, "float32"); _sb("FB4", 64, "float32"); _sb("L1", 64, "float32"); _sb("L2", 64, "int32"); _sb("LAST", 64, "int32")
 _sb("QL", 256, "bfloat16"); _sb("QR", 256, "bfloat16"); _sb("QE", 256, "bfloat16"); _sb("QO", 256, "bfloat16")
-_sb("TT", 256, "float32"); _sb("T2", 256, "float32"); _sb("FL", 16, "float32"); _sb("JK", 256, "bfloat16")
-_sb("E2", 256, "bfloat16"); _sb("LF", 16, "float32"); _sb("UP", 256, "float32"); _sb("PG", 256, "float32")
-_sb("DM", 256, "float32"); _sb("SC", 256, "float32"); _sb("PU", 16, "uint16"); _sb("E3", 256, "float32"); _sb("E4", 256, "bfloat16")
+_sb("TT", 256, "float32"); _sb("T2", 256, "float32"); _sb("FL", 16, "float32"); _sb("JK", 1280, "bfloat16")
+_sb("E2", 256, "bfloat16"); _sb("LF", 16, "float32"); _sb("UP", 256, "float32"); _sb("PG", 256, "bfloat16")
+_sb("DM", 256, "float32"); _sb("SC", 256, "float32"); _sb("PU", 16, "uint16"); _sb("E3", 512, "bfloat16"); _sb("E4", 256, "bfloat16")
 _sb("W1", 16, "float32"); _sb("W2", 16, "float32"); _sb("W3", 16, "float32"); _sb("WB", 16, "bfloat16")
 _sb("DEADL", 16, "float32"); _sb("RES", 16, "float32"); _sb("KP", 8, "float32"); _sb("KI", 8, "int32")
 for _n in ["G0", "G1", "G2", "G3", "G4", "G5", "K6", "C7"]:
@@ -72,7 +74,7 @@ def rank_program(g, core, T, topo):
     A = AluOpType
     F = ActivationFunctionType
     RH, RL0, RL1 = T.RHL[:, 0:8], T.RHL[:, 8:16], T.RHL[:, 16:24]
-    GB, SR15, SR14, SRN = [T.SRM[:, 128 * i:128 * i + 128] for i in range(4)]
+    SRP, SRH, SRL = [T.SRB[:, 128 * i:128 * i + 128] for i in range(3)]
     n_ranks = len(T.cores)
     nxt, prv = (rank + 1) % n_ranks, (rank - 1) % n_ranks
     Q = {"v": g.vector, "s": g.scalar, "p": g.tensor, "g": g, "y": g.sync}
@@ -89,7 +91,7 @@ def rank_program(g, core, T, topo):
                 Q[q].wait_ge(T.sem[sem], toks[sem])
                 waited[q][sem] = toks[sem]
 
-    def deps(reads, writes):
+    def deps(reads, writes, own=None):
         toks = {}
         for k in reads:
             for s, v in wr.get(k, {}).items():
@@ -97,7 +99,8 @@ def rank_program(g, core, T, topo):
         for k in writes:
             for m in (wr, rd):
                 for s, v in m.get(k, {}).items():
-                    toks[s] = max(toks.get(s, 0), v)
+                    if s != own:
+                        toks[s] = max(toks.get(s, 0), v)
         return toks
 
     def note(reads, writes, sem, val):
@@ -110,8 +113,8 @@ def rank_program(g, core, T, topo):
                 m[sem] = max(m.get(sem, 0), val)
         last[sem] = max(last.get(sem, 0), val)
 
-    def op(q, fns, reads, writes):
-        need(q, deps(reads, writes))
+    def op(q, fns, reads, writes, acc=False):
+        need(q, deps(reads, writes, "c" + q if acc else None))
         for fn in (fns if isinstance(fns, list) else [fns]):
             cnt[q] += 1
             fn().then_inc(T.sem["c" + q], 1)
@@ -167,10 +170,14 @@ def rank_program(g, core, T, topo):
     def mm(out, lhsT, rhs, start, stop):
         return lambda: g.tensor.matmul(out, lhsT, rhs, start, stop)
 
-    def row_to_list(src, lhsT, rows, bank, bkey, fin):
+    def row_to_list(src, lhsT, rows, bank, bkey, fin, *between):
         op("p", mm(bank[:, 0:256], lhsT, src, True, True), rows, [bkey])
         tt(T.DM[:], bank[:, 0:256], T.DIAG[:], A.mult, [bkey, "DIAG"], ["DM"])
+        for f in between[0:1]:
+            f()
         scan(T.SC[:], T.RS16[:], T.DM[:], A.mult, A.add, ["RS16", "DM"], ["SC"])
+        for f in between[1:]:
+            f()
         fin(T.SC[:, 15:256:16])
 
     def dead_done(t):
@@ -188,13 +195,25 @@ def rank_program(g, core, T, topo):
         landed(prv if t % 2 == 0 else nxt, "s%d" % t, ["SLAND%d" % t])
 
     def near_send(t):
-        cp(T.RSND[:, 16 * t:16 * t + 16], T.RES[:], ["RES"], ["RSND%d" % t])
-        send(prv if t % 2 == 0 else nxt, "r%d" % t, T.RLAND[:, 16 * t:16 * t + 16], T.RSND[:, 16 * t:16 * t + 16], ["RSND%d" % t])
+        hi, lo = T.RSND[:, 32 * t:32 * t + 16], T.RSND[:, 32 * t + 16:32 * t + 32]
+        if t == NB - 1:
+            cp(hi, T.RES[:], ["RES"], ["RSH%d" % t])
+            send(prv if t % 2 == 0 else nxt, "r%d" % t, T.RLAND[:, 32 * t:32 * t + 16], hi, ["RSH%d" % t])
+            return
+        ts(T.LXJ[:], T.RES[:], -1.0, A.add, ["RES"], ["LXJ"])
+        ts(T.LXI[:], T.LXJ[:], 4, A.arith_shift_right, ["LXJ"], ["LXI"])
+        ts(hi, T.LXI[:], 0.0, A.max, ["LXI"], ["RSH%d" % t])
+        ts(T.W2[:], hi, -16.0, A.mult, ["RSH%d" % t], ["W2"])
+        tt(lo, T.RES[:], T.W2[:], A.add, ["RES", "W2"], ["RSL%d" % t])
+        send(prv if t % 2 == 0 else nxt, "r%d" % t, T.RLAND[:, 32 * t:32 * t + 32], T.RSND[:, 32 * t:32 * t + 32], ["RSH%d" % t, "RSL%d" % t])
 
     def near_rows(t):
         landed(nxt if t % 2 == 0 else prv, "r%d" % t, ["RLAND%d" % t])
-        tt(T.E3[:], T.RLAND[:, 16 * t:16 * t + 16].indirect(T.LX4[:]), T.DIAG[:], A.mult, ["RLAND%d" % t, "LX4", "DIAG"], ["E3"])
-        op("p", mm(T.G4[:, 0:256], SRN, T.E3[:], True, True), ["SRN", "E3"], ["G4"])
+        for i in range(2):
+            tt(T.E3[:, 256 * i:256 * i + 256], T.RLAND[:, 32 * t + 16 * i:32 * t + 16 * i + 16].indirect(T.LX4[:]), T.DIAG[:], A.mult,
+               ["RLAND%d" % t, "LX4", "DIAG"], ["E3_%d" % i])
+        op("p", [mm(T.G4[:, 0:256], SRH, T.E3[:, 0:256], True, False), mm(T.G4[:, 0:256], SRL, T.E3[:, 256:512], False, True)],
+           ["SRH", "SRL", "E3_0", "E3_1"], ["G4"])
 
     def near_add(t):
         near, nk = (T.TA, "TA") if t % 2 == 0 else (T.TB, "TB")
@@ -215,6 +234,11 @@ def rank_program(g, core, T, topo):
     cp(T.PC[:, 0:4], T.PT[:, 0:4], ["PT0", "PT1", "PT2", "PT3"], ["PC0"])
     cp(T.PC[:, 4:5], T.PI[:, 0:1], ["PI"], ["PC4"])
     PGRP, PLOW, PL3, PS2, PP = T.PC[:, 0:1], T.PC[:, 1:2], T.PC[:, 2:3], T.PC[:, 3:4], T.PC[:, 4:5]
+    for i, r in enumerate((12, 13, 14, 15)):
+        ts(T.PC[:, 8 + i:9 + i], PLOW, float(r), A.is_equal, ["PC0"], ["PC%d" % (8 + i)])
+    I12, I13, I14, I15 = [T.PC[:, 8 + i:9 + i] for i in range(4)]
+    ts(T.PT[:, 4:5], T.PI[:, 0:1], 4, A.arith_shift_right, ["PI"], ["PT4"], 1, A.bitwise_and)
+    ECOL, OCOL = T.WF2[:, 6:7], T.WF2[:, 5:6]
     for f in range(1, 12):
         ts(T.BI[:, 32 * f:32 * f + 32], T.BI[:, 0:32], f, A.arith_shift_right, ["BI0"], ["BI%d" % f], 1, A.bitwise_and)
     ts(T.BI[:, 0:32], T.BI[:, 0:32], 1, A.bitwise_and, ["BI0"], ["BI0"])
@@ -234,20 +258,21 @@ def rank_program(g, core, T, topo):
     row_to_list(T.E4[:], T.GBH[:], ["E4", "GBH"], T.G3, "G3", dead_done(0))
     start_batch(0)
     wr["X"] = deps(["X", "Xx"], [])
-    cp(T.PF[:, 0:256], T.PBI[:], ["PBI"], ["PF0"])
-    ts(T.PG4[:, 0:256], T.PBI[:], 0.0, A.is_ge, ["PBI"], ["PG40"])
-    dma("y", [(T.PD[0], T.PF[:, 0:256]), (T.PD[1], T.PG4[:, 0:256])], ["PF0", "PG40"], ["PD0"])
-    cp(T.PF[:, 256:512], T.PAI[:], ["PAI"], ["PF1"])
-    ts(T.PG4[:, 256:512], T.PAI[:], 0.0, A.is_ge, ["PAI"], ["PG41"])
-    dma("y", [(T.PD[2], T.PF[:, 256:512]), (T.PD[3], T.PG4[:, 256:512])], ["PF1", "PG41"], ["PD1"])
+    def table_rows(pin, pk, i):
+        hi, lo = T.PF[:, 256 * i:256 * i + 256], T.PG4[:, 256 * i:256 * i + 256]
+        ts(T.CT1[:], pin[:], 4, A.arith_shift_right, [pk], ["CT1"])
+        ts(hi, T.CT1[:], 0.0, A.max, ["CT1"], ["PF%d" % i])
+        ts(T.CB[:], hi, -16.0, A.mult, ["PF%d" % i], ["CB"], 1.0, A.add)
+        tt(lo, T.CB[:], pin[:], A.add, ["CB", pk], ["PG4%d" % i])
+        dma("y", [(T.PD[2 * i], hi), (T.PD[2 * i + 1], lo)], ["PF%d" % i, "PG4%d" % i], ["PD%d" % i])
 
     def fill_table(tab, key, pv, pf, pk):
         pieces = [(tab[16 * b:16 * b + 14, 0:W], T.BD[:]) for b in range(8)]
         pieces += [(tab[15:128:16, 0:W], pv), (tab[14:128:16, 0:W], pf)]
         dma("y", pieces, ["BD", pk], [key])
 
+    table_rows(T.PBI, "PBI", 0)
     fill_table(T.TB, "TBd", T.PD[0], T.PD[1], "PD0")
-    fill_table(T.TA, "TAd", T.PD[2], T.PD[3], "PD1")
     ts(T.WI[:, 2:3], T.WI[:, 0:1], 3840, A.bitwise_and, ["WI"], ["WI2"])
     ts(T.WI[:, 3:4], T.WI[:, 0:1], 255, A.bitwise_and, ["WI"], ["WI3"])
     ts(T.WF2[:, 0:2], T.WI[:, 2:4], 1.0 / 4096, A.mult, ["WI2", "WI3"], ["WF2"])
@@ -265,9 +290,19 @@ def rank_program(g, core, T, topo):
     ts(T.ABASE[:], T.ATMP[:], -1.0, A.mult, ["ATMP"], ["ABASE"], 262144.0 - 12.0, A.add)
     ts(T.ACOL[:], T.ABASE[:], 0.0, A.add, ["ABASE"], ["ACOL"])
     cp(T.CF[:], T.CI5[:], ["CI5"], ["CF"])
-    ts(T.OB[:], T.CF[:, 0:8], PGRP, A.is_equal, ["CF", "PC0"], ["OB"], 4096.0, A.mult)
     ts(T.IDF[:], T.CF[:, 0:128], PP, A.is_equal, ["CF", "PC4"], ["IDF"])
-    ts(T.PEN[:], T.IDF[:], float(2 ** 25), A.mult, ["IDF"], ["PEN"])
+    ts(T.PC[:, 12:13], PLOW, 12.0, A.is_lt, ["PC0"], ["PC12"])
+    ts(T.PC[:, 7:8], I12, -1.0, A.mult, ["PC8"], ["PC7"])
+    ts(T.PC[:, 13:14], T.PC[:, 12:13], 128.0, A.mult, ["PC12", "PC8"], ["PC13"], I12, A.add)
+    ts(T.PC[:, 14:15], I14, 2048.0, A.mult, ["PC10"], ["PC14"])
+    tt(T.PC[:, 13:14], T.PC[:, 13:14], T.PC[:, 14:15], A.add, ["PC13", "PC14"], ["PC13"])
+    ts(T.PC[:, 15:16], T.PC[:, 12:13], I13, A.add, ["PC12", "PC9", "PC10"], ["PC15"], I14, A.add)
+    ts(T.WF2[:, 4:5], PLOW, 14.0, A.is_lt, ["PC0", "PC10"], ["WF4"], -2.0, A.mult)
+    tt(T.WF2[:, 4:5], T.WF2[:, 4:5], I14, A.add, ["WF4", "PC10"], ["WF4"])
+    ts(T.WF2[:, 3:4], I15, 16.0, A.mult, ["PC11", "PC10"], ["WF3"], I14, A.add)
+    cp(T.WF2[:, 5:6], T.PT[:, 4:5], ["PT4"], ["WF5"])
+    ts(T.WF2[:, 6:7], T.WF2[:, 5:6], -1.0, A.mult, ["WF5"], ["WF6"], 1.0, A.add)
+    ts(T.OB[:], T.CF[:, 0:8], PGRP, A.is_equal, ["CF", "PC0"], ["OB"], 4096.0, A.mult)
     ms(T.ZB[:], 0.0, ["ZB"])
     ts(T.CT1[:], T.CI5[:], 7, A.bitwise_and, ["CI5"], ["CT1"])
     ts(T.RS8[:], T.CT1[:], 0.0, A.is_equal, ["CT1"], ["RS8"], float(2 ** 26), A.mult)
@@ -277,61 +312,47 @@ def rank_program(g, core, T, topo):
     ts(T.PT[:, 6:7], T.PI[:, 0:1], 2, A.arith_shift_right, ["PI"], ["PT6"], 3, A.bitwise_and)
     ts(T.PC[:, 6:7], T.PT[:, 6:7], 8.0, A.mult, ["PT6"], ["PC6"])
     ts(T.LX3[:], T.LXI[:, 0:8], T.PC[:, 6:7], A.add, ["LXI", "PC6"], ["LX3"])
-    for i, r in enumerate((12, 13, 14, 15)):
-        ts(T.PC[:, 8 + i:9 + i], PLOW, float(r), A.is_equal, ["PC0"], ["PC%d" % (8 + i)])
-    I12, I13, I14, I15 = [T.PC[:, 8 + i:9 + i] for i in range(4)]
-    ts(T.PC[:, 12:13], PLOW, 12.0, A.is_lt, ["PC0"], ["PC12"])
-    ts(T.PT[:, 4:5], T.PI[:, 0:1], 4, A.arith_shift_right, ["PI"], ["PT4"], 1, A.bitwise_and)
-    cp(T.WF2[:, 5:6], T.PT[:, 4:5], ["PT4"], ["WF5"])
-    ts(T.WF2[:, 6:7], T.WF2[:, 5:6], -1.0, A.mult, ["WF5"], ["WF6"], 1.0, A.add)
-    ECOL, OCOL = T.WF2[:, 6:7], T.WF2[:, 5:6]
     ms(T.FBC[:], 16777215.0, ["FBC"])
     ms(T.FB4C[:], 16777215.0, ["FB4C"])
+    act(T.IBN[:, 0:128], T.IDF[:], F.Identity, ["IDF"], ["IBN0"])
+    act(T.IBN[:, 128:256], T.IDF[:], F.Identity, ["IDF"], ["IBN1"], scale=-1.0)
+    act(T.CL[:], T.CF[:], F.Identity, ["CF", "PC9", "PC13"], ["CL"], scale=I13, bias=T.PC[:, 13:14])
+    act(T.CR[:], T.CF[:], F.Identity, ["CF", "PC7", "PC15"], ["CR"], scale=T.PC[:, 7:8], bias=T.PC[:, 15:16])
+    for i in range(2):
+        act(T.TB[:, W + 256 * i:W + 256 * i + 256], T.CF[:], F.Identity, ["CF", "PC10"], ["TBx%d" % i], scale=0.0, bias=I14)
+    wr["TB"] = deps(["TBd", "TBx0", "TBx1"], [])
 
-    def late_constants():
-        ts(T.CL[:], T.CF[:], I13, A.mult, ["CF", "PC9"], ["CL"])
-        ts(T.PC[:, 13:14], T.PC[:, 12:13], 128.0, A.mult, ["PC12"], ["PC13"])
-        ts(T.PC[:, 14:15], I14, 2048.0, A.mult, ["PC10"], ["PC14"])
-        tt(T.PC[:, 13:14], T.PC[:, 13:14], I12, A.add, ["PC13", "PC8"], ["PC13"])
-        ts(T.CL[:], T.CL[:], T.PC[:, 13:14], A.add, ["CL", "PC13", "PC14"], ["CL"], T.PC[:, 14:15], A.add)
-        ts(T.CR[:], T.CF[:], I12, A.mult, ["CF", "PC8"], ["CR"], -1.0, A.mult)
-        tt(T.PC[:, 15:16], T.PC[:, 12:13], I13, A.add, ["PC12", "PC9"], ["PC15"])
-        ts(T.CR[:], T.CR[:], T.PC[:, 15:16], A.add, ["CR", "PC15", "PC10"], ["CR"], I14, A.add)
-        ms(T.CA[:], 0.0, ["CA"])
-        ts(T.TB[:, W:WX], T.CA[:], I14, A.add, ["CA", "PC10"], ["TBx"])
-        wr["TB"] = deps(["TBd", "TBx"], [])
+    def scalar_constants():
+        act(T.PEN[:], T.IDF[:], F.Identity, ["IDF"], ["PEN"], scale=float(2 ** 25))
+        act(T.RC[:], T.CF[:], F.Identity, ["CF", "PC11", "WF4"], ["RC"], scale=I15, bias=T.WF2[:, 4:5])
+        act(SRP, T.GBH[:], F.Identity, ["GBH", "WF3"], ["SRP"], scale=T.WF2[:, 3:4])
+        act(T.SR14[:], T.GBH[:], F.Identity, ["GBH", "PC10"], ["SR14"], scale=I14)
+        for i in range(2):
+            act(T.TA[:, W + 256 * i:W + 256 * i + 256], T.CF[:], F.Identity, ["CF", "PC10"], ["TAx%d" % i], scale=0.0, bias=I14)
 
     def later_constants():
         ts(T.CT2[:, 0:16], T.CI5[:, 0:16], 7, A.bitwise_and, ["CI5"], ["CT2"])
-        ts(T.CT1[:, 0:16], T.CI5[:, 0:16], 3, A.arith_shift_right, ["CI5"], ["CT1"])
-        ts(T.LXJ[:], T.CT2[:, 0:16], 2.0, A.mult, ["CT2"], ["LXJ"])
-        tt(T.LXI[:], T.LXJ[:], T.CT1[:, 0:16], A.add, ["LXJ", "CT1"], ["LXI"])
-        cp(T.LX2[:], T.LXI[:], ["LXI"], ["LX2"])
+        cp(T.LX2[:], T.CT2[:, 0:16], ["CT2"], ["LX2"])
         ts(T.CT1[:], T.CI5[:], 4, A.arith_shift_right, ["CI5"], ["CT1"], 7, A.bitwise_and)
-        ts(T.CA[:, 0:256], T.CT1[:], 4.0, A.is_lt, ["CT1"], ["CA"], 1536.0, A.mult)
+        for h in range(2):
+            ts(T.CA[:, 128 * h:128 * h + 128], T.CT1[:, 128 * h:128 * h + 128], 4.0 + h, A.is_lt, ["CT1"], ["CA"], 1536.0, A.mult)
         ts(T.CB[:], T.DIAG[:], 0.0, A.is_equal, ["DIAG"], ["CB"], 1e25, A.mult)
         tt(T.TH2[:], T.CA[:, 0:256], T.CB[:], A.max, ["CA", "CB"], ["TH2"])
         ts(RH, T.CF[:, 0:8], PGRP, A.is_equal, ["CF", "PC0"], ["RH"], float(DUM), A.mult)
         ts(RL0, T.CF[:, 0:8], PGRP, A.is_equal, ["CF", "PC0", "PC4"], ["RL0"], PP, A.mult)
         ts(T.WF2[:, 7:8], PP, 128.0, A.add, ["PC4"], ["WF7"])
         ts(RL1, T.CF[:, 0:8], PGRP, A.is_equal, ["CF", "PC0", "WF7"], ["RL1"], T.WF2[:, 7:8], A.mult)
-        ts(T.WF2[:, 4:5], PLOW, 14.0, A.is_lt, ["PC0"], ["WF4"], -2.0, A.mult)
-        tt(T.WF2[:, 4:5], T.WF2[:, 4:5], I14, A.add, ["WF4", "PC10"], ["WF4"])
-        ts(T.RC[:], T.CF[:], 16.0, A.mult, ["CF"], ["RC"], I15, A.mult)
-        ts(T.RC[:], T.RC[:], T.WF2[:, 4:5], A.add, ["RC", "WF4"], ["RC"])
 
     def last_constants():
         ms(T.ONES[:], 1.0, ["ONES"])
-        cp(GB, T.GBH[:], ["GBH"], ["GB"])
-        ts(SR15, GB, I15, A.mult, ["GB", "PC11"], ["SR15"])
-        ts(SR14, GB, I14, A.mult, ["GB", "PC10"], ["SR14"])
         ts(T.CT2[:, 0:128], T.CI5[:, 0:128], 15, A.bitwise_and, ["CI5"], ["CT2"])
-        ts(T.CA[:, 0:128], T.CT2[:, 0:128], 14.0, A.is_ge, ["CT2"], ["CA"])
-        tt(SRN, T.CA[:, 0:128], GB, A.mult, ["CA", "GB"], ["SRN"])
+        for i, sel in ((15, SRH), (14, SRL)):
+            ts(T.CA[:, 0:128], T.CT2[:, 0:128], float(i), A.is_equal, ["CT2"], ["CA"])
+            tt(sel, T.CA[:, 0:128], T.GBH[:], A.mult, ["CA", "GBH"], ["SRH" if i == 15 else "SRL"])
         cp(T.LX4[:], T.CI5[:, 0:16], ["CI5"], ["LX4"])
-        ms(T.CA[:], 0.0, ["CA"])
-        ts(T.TA[:, W:WX], T.CA[:], I14, A.add, ["CA", "PC10"], ["TAx"])
-        wr["TA"] = deps(["TAd", "TAx"], [])
+        table_rows(T.PAI, "PAI", 1)
+        fill_table(T.TA, "TAd", T.PD[2], T.PD[3], "PD1")
+        wr["TA"] = deps(["TAd", "TAx0", "TAx1"], [])
 
     BANKS = [T.G0, T.G1, T.G2, T.G3, T.G4, T.G5]
     for t in range(NB):
@@ -356,10 +377,9 @@ def rank_program(g, core, T, topo):
                    ["NLAND%d" % pm, "LLAND%d" % pm], [xk])
                 cp(T.Z[:], XC[:, 0:WX].indirect(T.PU[:]), [xk, "PU"], ["Z"])
 
-            def result():
-                ts(T.W3[:], T.YQ[:], 1.0, A.add, ["YQ"], ["W3"])
-                tt(T.W2[:], T.W3[:], T.WB[:], A.mult, ["W3", "WB"], ["W2"])
-                tt(T.RES[:], T.RES[:], T.W2[:], A.add, ["RES", "W2"], ["RES"])
+            result = (lambda: ts(T.W3[:], T.YQ[:], 1.0, A.add, ["YQ"], ["W3"]),
+                      lambda: tt(T.W2[:], T.W3[:], T.WB[:], A.mult, ["W3", "WB"], ["W2"]),
+                      lambda: tt(T.RES[:], T.RES[:], T.W2[:], A.add, ["RES", "W2"], ["RES"]))
 
             fs = []
             for ll in range(4):
@@ -374,11 +394,18 @@ def rank_program(g, core, T, topo):
             for ch in range(4):
                 act(T.SQ[:, 64 * ch:64 * ch + 64], T.UF[:], F.Square, ["UF", "SCOL"], ["SQ%d" % ch], bias=T.SCOL[:, ch:ch + 1], scale=4096.0)
 
+            def floors(ch):
+                ts(T.FI[:, 64 * ch:64 * ch + 64], T.SQ[:, 64 * ch:64 * ch + 64], T.ACOL[:, ch:ch + 1], A.add, ["SQ%d" % ch, "ACOL"], ["FI%d" % ch], 1.0 / 32, A.mult)
+
             def places(c0, c1):
-                for ch in range(c0, c1):
-                    ts(T.FI[:, 64 * ch:64 * ch + 64], T.SQ[:, 64 * ch:64 * ch + 64], T.ACOL[:, ch:ch + 1], A.add, ["SQ%d" % ch, "ACOL"], ["FI%d" % ch], 1.0 / 32, A.mult)
                 keys = [str(ch) for ch in range(c0, c1)]
                 ts(T.CI[:, 64 * c0:64 * c1], T.FI[:, 64 * c0:64 * c1], 4095, A.bitwise_and, ["FI" + c for c in keys], ["CI" + c for c in keys])
+
+            def bars(ch):
+                tt(T.EQ[:, 64 * ch:64 * ch + 64], T.CI[:, 64 * ch:64 * ch + 64], T.LAST[:], A.is_equal, ["CI%d" % ch, "LAST"], ["EQ%d" % ch])
+
+            def lists(c0, c1):
+                keys = [str(ch) for ch in range(c0, c1)]
                 cp(T.OFF[:, 64 * c0:64 * c1], T.CI[:, 64 * c0:64 * c1], ["CI" + c for c in keys], ["OFF" + c for c in keys])
 
             if d == 0:
@@ -395,19 +422,29 @@ def rank_program(g, core, T, topo):
                 for part in range(16):
                     o = 2 * part + pr
                     fs.append(mm(T.K6[p0:p0 + n, o:256:32], T.AB[:, 16 * c0 + part:16 * (c0 + n):16], T.OB[:], False, False))
-                op("p", fs, keys + ["OB"], ["K6"])
+                op("p", fs, keys + ["OB"], ["K6"], True)
 
+            floors(0)
+            floors(1)
             places(0, 1)
+            floors(2)
+            lists(0, 1)
+            floors(3)
+            act(T.DF[:, 512:1024], T.X[:, 0:WX].indirect(T.OFF[:, 32:64]), F.Copy, ["X", "OFF0"], ["DF32"])
+            op("p", [mm(T.G0[:], T.IBN[:, 0:128], T.DF[:, 512:1024], True, False), mm(T.G0[:], T.IBN[:, 128:256], T.Z4[:, 512:1024], False, True)],
+               ["IBN0", "IBN1", "DF32", "Z4_0", "Z4_1", "Z4_2", "Z4_3"], ["G0"])
             gather(0, 32)
+            act(T.AB[:, 512:1024], T.G0[:], F.Abs, ["G0"], ["AB32"])
             places(1, 4)
-            gather(32, 32)
+            if d > 0:
+                bars(0)
+            lists(1, 4)
             cis = ["CI0", "CI1", "CI2", "CI3"]
             cp(T.CFL[:], T.CI[:], cis, ["CFL"])
             op("p", [mm(T.K6[:, 0:256], T.ZB[:, 0:128], T.ZB[:], True, False)] +
                [mm(T.K6[:, pr:256:2], T.CFL[:, 128 * pr:128 * pr + 128], T.IDF[:], False, False) for pr in range(2)], ["ZB", "CFL", "IDF"], ["K6"])
-            gather(64, 32)
-            gather(96, 32)
-            dsum(0, 128, 0, 0, ["AB0", "AB32", "AB64", "AB96"])
+            gather(64, 64)
+            dsum(0, 128, 0, 0, ["AB0", "AB32", "AB64"])
             gather(128, 32)
             gather(160, 32)
             dsum(128, 64, 0, 1, ["AB128", "AB160"])
@@ -418,26 +455,27 @@ def rank_program(g, core, T, topo):
             gather(224, 16)
             gather(240, 16)
             if d > 0:
-                for ch in range(4):
-                    tt(T.EQ[:, 64 * ch:64 * ch + 64], T.CI[:, 64 * ch:64 * ch + 64], T.LAST[:], A.is_equal, ["CI%d" % ch, "LAST"], ["EQ%d" % ch])
+                for ch in range(1, 4):
+                    bars(ch)
             dsum(224, 32, 96, 1, ["AB224", "AB240"])
             if d > 0:
-                op("p", [mm(T.K6[:, pr:256:2], T.EQ[:, 128 * pr:128 * pr + 128], T.PEN[:], False, False) for pr in range(2)], ["EQ0", "EQ1", "EQ2", "EQ3", "PEN"], ["K6"])
-            op("p", mm(T.K6[:, 0:256], T.ZB[:, 0:128], T.ZB[:], False, True), ["ZB"], ["K6"])
+                op("p", [mm(T.K6[:, pr:256:2], T.EQ[:, 128 * pr:128 * pr + 128], T.PEN[:], False, False) for pr in range(2)], ["EQ0", "EQ1", "EQ2", "EQ3", "PEN"], ["K6"], True)
+            op("p", mm(T.K6[:, 0:256], T.ZB[:, 0:128], T.ZB[:], False, True), ["ZB"], ["K6"], True)
             if d == 0:
                 landed(frm, "e%d" % t, ["DLAND%d" % t])
                 cp(T.DEADL[:], T.DLAND[:, 16 * t:16 * t + 16], ["DLAND%d" % t], ["DEADL"])
                 ms(T.RES[:], 0.0, ["RES"])
                 if t > 0:
                     near_add(t - 1)
-                    ts(T.RC[:], T.RC[:], I15, A.add, ["RC", "PC11"], ["RC"])
+                    ts(T.RC[:], T.RC[:], I14, A.add, ["RC", "PC10"], ["RC"])
                 else:
-                    late_constants()
+                    later_constants()
             else:
                 ts(T.W1[:], T.WB[:], DEAD, A.mult, ["WB"], ["W1"])
                 tt(T.DEADL[:], T.DEADL[:], T.W1[:], A.max, ["DEADL", "W1"], ["DEADL"])
                 ts(T.FB[:], T.YA[:], BAR, A.add, ["YA"], ["FB"])
-                result()
+            if m == 0:
+                scalar_constants()
             scan(T.R[:], T.RS8[:], T.K6[:, 0:256], A.max, A.min, ["RS8", "K6"], ["R"])
             tt(T.E1[:], T.R[:, 0:256].indirect(T.LX1[:]), T.M1[:], A.mult, ["R", "LX1", "M1"], ["E1"])
             op("p", mm(T.C7[:, 0:32], T.E1[:], T.RS1[:], True, True), ["E1", "RS1"], ["C7"])
@@ -445,62 +483,81 @@ def rank_program(g, core, T, topo):
                 act(T.R4[:], T.R[:, 0:256].indirect(T.LX3[:]), F.Copy, ["R", "LX3"], ["R4"])
                 op("p", mm(T.K6[:, 0:128], T.R4[:], T.IDF[:], True, True), ["R4", "IDF"], ["K6"])
             fb, fbk = (T.FBC, "FBC") if d == 0 else (T.FB, "FB")
+            rs = list(result) if d > 0 else [lambda: None] * 3
             tt(T.MN[:], T.C7[:, 16:32], fb[:], A.min, ["C7", fbk], ["MN"])
+            rs[0]()
             tt(T.YI[:], T.C7[:, 0:16], T.MN[:], A.min, ["C7", "MN"], ["YI"])
+            rs[1]()
             ts(T.YA[:], T.YI[:], 4095, A.bitwise_and, ["YI"], ["YA"])
+            rs[2]()
             tt(T.YQ[:], T.YA[:], T.DEADL[:], A.max, ["YA", "DEADL"], ["YQ"])
             cp(T.YU[:], T.YQ[:], ["YQ"], ["YU"])
-            tt(T.QL[:], far[:, 0:WX].indirect(T.YU[:]), T.CL[:], A.mult, [fk, "YU", "CL"], ["QL"])
-            act(T.QE[:], T.QL[:], F.Copy, ["QL", "WF6"], ["QE"], scale=ECOL)
-            tt(T.QR[:], far[:, 0:WX].indirect(T.YU[:]), T.CR[:], A.mult, [fk, "YU", "CR"], ["QR"])
-            ts(T.QO[:], T.QL[:], OCOL, A.mult, ["QL", "WF5"], ["QO"])
-            tt(T.TT[:], T.X[:, 0:WX].indirect(T.YU[:]), T.SH[:], A.add, ["X", "YU", "SH"], ["TT"])
-            act(T.T2[:], T.TT[:], F.Copy, ["TT"], ["T2"], scale=0.5, bias=8388608.0)
-            ns = T.NSND[:, 256 * m:256 * m + 256]
-            act(ns, T.T2[:], F.Copy, ["T2"], ["NSND%d" % m], bias=-8388608.0)
-            if not tail:
-                send(to, "n%d%d" % (t, d), T.NLAND[:, 256 * m:256 * m + 256], ns, ["NSND%d" % m])
-
-            def fill(n):
-                if n == 0:
-                    tt(T.UP[:], far[:, 0:WX].indirect(T.YU[:]), T.RC[:], A.max, [fk, "YU", "RC"], ["UP"])
-                if not tail:
-                    f4, f4k = (T.FB4C, "FB4C") if d == 0 else (T.FB4, "FB4")
-                    if n == 1:
-                        tt(T.L1[:], T.K6[:, 64:128], f4[:], A.min, ["K6", f4k], ["L1"])
-                        tt(T.L2[:], T.K6[:, 0:64], T.L1[:], A.min, ["K6", "L1"], ["L2"])
-                    if n == 2:
-                        ts(T.LAST[:], T.L2[:], 4095, A.bitwise_and, ["L2"], ["LAST"])
-                        if d == 0:
-                            ts(T.FB4[:], T.LAST[:], BAR, A.add, ["LAST"], ["FB4"])
-
-            if m == 0:
-                later_constants()
-            n = 0
-            for i, (gs, gv) in enumerate(((4, 0), (6, 2), (5, 1), (7, 3))):
-                for h in (1, 0):
-                    for gr in (gs, gv):
-                        b, bk = BANKS[n % 6], "G%d" % (n % 6)
-                        n += 1
-                        qa, qk = (T.QE, "QE") if gr % 2 == 0 else (T.QO, "QO")
-                        p0 = 32 * (gr // 2)
-                        w = 128 + 128 * h
-                        op("p", mm(b[:, 0:w], qa[p0:p0 + 32, 128 * h:128 * h + 128], T.QR[p0:p0 + 32, 0:w], True, True), [qk, "QR"], [bk])
-                        src = b[:, 0:w]
-                        o = T.FL[:, 2 * gr + h:2 * gr + h + 1]
-                        if gr < 4:
-                            op("v", lambda: g.vector.tensor_reduce(o, src, AxisListType.X, A.max), [bk], ["FL%d_%d" % (gr, h)])
-                        else:
-                            act(T.JK[:, 0:w], src, F.Relu, [bk], ["JK", "FL%d_%d" % (gr, h)], bias=-1536.0, accum_out=o)
-                fill(i)
+            for h in range(2):
+                a, b, yl = 128 * h, 128 * h + 128, T.YU[:, 8 * h:8 * h + 8]
+                tt(T.QL[:, a:b], far[:, 0:WX].indirect(yl), T.CL[:, a:b], A.mult, [fk, "YU", "CL"], ["QL%d" % h])
+                act(T.QE[:, a:b], T.QL[:, a:b], F.Copy, ["QL%d" % h, "WF6"], ["QE%d" % h], scale=ECOL)
+                tt(T.QR[:, a:b], far[:, 0:WX].indirect(yl), T.CR[:, a:b], A.mult, [fk, "YU", "CR"], ["QR%d" % h])
+                ts(T.QO[:, a:b], T.QL[:, a:b], OCOL, A.mult, ["QL%d" % h, "WF5"], ["QO%d" % h])
             if m == 0:
                 last_constants()
-            tt(T.E2[:], T.FL[:, 0:16].indirect(T.LX2[:]), T.TH2[:], A.is_gt, ["FL%d_%d" % (i, h) for i in range(8) for h in range(2)] + ["LX2", "TH2"], ["E2"])
+
+            def unit(gr, h, b, c):
+                qa, qk = (T.QE, "QE%d" % h) if gr % 2 == 0 else (T.QO, "QO%d" % h)
+                p0 = 32 * (gr // 2)
+                return mm(b[:, c:c + 128 + 128 * h], qa[p0:p0 + 32, 128 * h:128 * h + 128], T.QR[p0:p0 + 32, 0:128 + 128 * h], True, True)
+
+            def reduce(gr, h, b, bk, c, vec):
+                src = b[:, c:c + 128 + 128 * h]
+                o = T.FL[:, 8 * h + gr:8 * h + gr + 1]
+                if vec:
+                    op("v", lambda: g.vector.tensor_reduce(o, src, AxisListType.X, A.max), [bk], ["FL%d_%d" % (gr, h)])
+                else:
+                    j = 128 * (gr - 4) if h == 0 else 512 + 256 * (gr - 5)
+                    act(T.JK[:, j:j + 128 + 128 * h], src, F.Relu, [bk], ["JK%d_%d" % (gr, h), "FL%d_%d" % (gr, h)], bias=-1536.0, accum_out=o)
+
+            def unpaired(h):
+                tt(T.E2[:, 128 * h:128 * h + 128], T.FL[:, 8 * h:8 * h + 8].indirect(T.LX2[:, 8 * h:8 * h + 8]), T.TH2[:, 128 * h:128 * h + 128], A.is_gt,
+                   ["FL%d_%d" % (i, h) for i in range(8)] + ["LX2", "TH2"], ["E2_%d" % h])
+
+            for i, (ga, gb) in enumerate(((4, 5), (0, 1), (6, 7), (2, 3))):
+                b, bk = BANKS[i], "G%d" % i
+                op("p", [unit(ga, 0, b, 0), unit(gb, 0, b, 128)], ["QE0", "QO0", "QR0"], [bk])
+                reduce(ga, 0, b, bk, 0, ga < 4)
+                reduce(gb, 0, b, bk, 128, gb < 4)
+            tt(T.TT[:], T.X[:, 0:WX].indirect(T.YU[:]), T.SH[:], A.add, ["X", "YU", "SH"], ["TT"])
+            ns = T.NSND[:, 256 * m:256 * m + 256]
+            for n, gr in enumerate((5, 0, 6, 1, 7, 2, 3, 4)):
+                b, bk = BANKS[(4 + n) % 6], "G%d" % ((4 + n) % 6)
+                op("p", unit(gr, 1, b, 0), ["QE1" if gr % 2 == 0 else "QO1", "QR0", "QR1"], [bk])
+                reduce(gr, 1, b, bk, 0, gr < 5)
+                if n == 0:
+                    act(T.T2[:], T.TT[:], F.Copy, ["TT"], ["T2"], scale=0.5, bias=8388608.0)
+                    act(ns, T.T2[:], F.Copy, ["T2"], ["NSND%d" % m], bias=-8388608.0)
+                    if not tail:
+                        send(to, "n%d%d" % (t, d), T.NLAND[:, 256 * m:256 * m + 256], ns, ["NSND%d" % m])
+                if n == 1:
+                    unpaired(0)
+                if not tail:
+                    f4, f4k = (T.FB4C, "FB4C") if d == 0 else (T.FB4, "FB4")
+                    if n == 3:
+                        tt(T.L1[:], T.K6[:, 64:128], f4[:], A.min, ["K6", f4k], ["L1"])
+                    if n == 5:
+                        tt(T.L2[:], T.K6[:, 0:64], T.L1[:], A.min, ["K6", "L1"], ["L2"])
+                    if n == 6:
+                        ts(T.LAST[:], T.L2[:], 4095, A.bitwise_and, ["L2"], ["LAST"])
+                    if n == 7 and d == 0:
+                        ts(T.FB4[:], T.LAST[:], BAR, A.add, ["LAST"], ["FB4"])
+            unpaired(1)
             fs = []
             for h in range(2):
                 fs.append(mm(T.C7[:, 64 + 8 * h:72 + 8 * h], T.E2[:, 128 * h:128 * h + 128], RH, True, False))
                 fs.append(mm(T.C7[:, 64 + 8 * h:72 + 8 * h], T.E2[:, 128 * h:128 * h + 128], RL0 if h == 0 else RL1, False, True))
-            op("p", fs, ["E2", "RH", "RL0", "RL1"], ["C7"])
+            op("p", fs, ["E2_0", "E2_1", "RH", "RL0", "RL1"], ["C7"])
+            if m == ND * NB - 2:
+                dma("y", [(T.PG4[:, 0:256], T.TA[15:128:16, 0:W]), (T.PG4[:, 256:512], T.TA[14:128:16, 0:W])], ["TA"], ["PG4n"])
+                ts(T.CB[:], T.PG4[:, 0:256], 16.0, A.mult, ["PG4n"], ["CB"], -1.0, A.add)
+                tt(T.PF[:, 0:256], T.CB[:], T.PG4[:, 256:512], A.add, ["CB", "PG4n"], ["YA0"])
+            act(T.UP[:], far[:, 0:WX].indirect(T.YU[:]), F.Copy, [fk, "YU"], ["UP"])
             tt(T.LF[:], T.C7[:, 64:80], T.YQ[:], A.max, ["C7", "YQ"], ["LF"])
             ls = T.LSND[:, 16 * m:16 * m + 16]
             lk = "LSND%d" % m
@@ -515,26 +572,35 @@ def rank_program(g, core, T, topo):
             if not (tail and t + 1 == NB):
                 op("p", mm(T.G0[:, 0:16], T.ONES[:], T.WB[:], True, True), ["ONES", "WB"], ["G0"])
             if tail:
-                result()
+                for r in result:
+                    r()
                 near_send(t)
-            cp(far[:, 0:WX].indirect(ls), T.UP[:], ["UP", lk], [fk])
+            tt(far[:, 0:WX].indirect(ls), T.UP[:], T.RC[:], A.max, ["UP", "RC", lk], [fk])
             if not tail:
                 act(T.PG[:], far[:, 0:WX].indirect(T.YU[:]), F.Copy, [fk, "YU"], ["PG"])
                 cp(T.X[:, 0:WX].indirect(ls), ns, [lk, "NSND%d" % m], ["X"])
             if not (tail and t + 1 == NB):
                 op("v", lambda: g.vector.tensor_reduce(T.KP[:, 0:1], T.G0[:, 0:16], AxisListType.X, A.add), ["G0"], ["KP0"])
-                cp(T.KI[:, 0:1], T.KP[:, 0:1], ["KP0"], ["KI0"])
-                ts(T.KI[:, 1:2], T.KI[:, 0:1], 31, A.bitwise_and, ["KI0"], ["KI1"])
+                k1 = lambda: cp(T.KI[:, 0:1], T.KP[:, 0:1], ["KP0"], ["KI0"])
+                k2 = lambda: ts(T.KI[:, 1:2], T.KI[:, 0:1], 31, A.bitwise_and, ["KI0"], ["KI1"])
+                if not tail:
+                    row_to_list(T.PG[:], SRP, ["PG", "SRP"], T.G2, "G2",
+                                lambda ap: ts(T.PU[:], ap, -1.0, A.add, ["SC"], ["PU"]), k1, k2)
+                else:
+                    row_to_list(far[:, t + 1:W:16], T.SR14[:], [fk, "SR14"], T.G3, "G3", dead_done(t + 1), k1, k2)
                 ts(T.KP[:, 1:2], T.KI[:, 1:2], 32.0, A.mult, ["KI1"], ["KP1"])
                 ts(T.ACOL[:], T.ABASE[:], T.KP[:, 1:2], A.add, ["ABASE", "KP1"], ["ACOL"], 3104.0 * ((d + 1) % ND), A.add)
-            if not tail:
-                row_to_list(T.PG[:], SR15, ["PG", "SR15"], T.G2, "G2", lambda ap: cp(T.PU[:], ap, ["SC"], ["PU"]))
-            elif t + 1 < NB:
-                row_to_list(far[:, t + 1:W:16], SR14, [fk, "SR14"], T.G3, "G3", dead_done(t + 1))
     dma("y", [(T.yx[:], T.X[:, 0:W])], ["X"], ["yx"])
-    dma("y", [(T.yb[:], T.TB[15:128:16, 0:W])], ["TB"], ["yb"])
-    near_rows(NB - 1)
-    near_add(NB - 1)
-    dma("y", [(T.ya[:], T.TA[15:128:16, 0:W])], ["TA"], ["ya"])
+
+    dma("y", [(T.PG4[:, 0:256], T.TB[15:128:16, 0:W]), (T.PG4[:, 256:512], T.TB[14:128:16, 0:W])], ["TB", "YA0"], ["PG4f"])
+    t = NB - 1
+    landed(nxt if t % 2 == 0 else prv, "r%d" % t, ["RLAND%d" % t])
+    tt(T.E1[:], T.RLAND[:, 32 * t:32 * t + 16].indirect(T.LX5[:, 0:8]), T.GBH[:], A.mult, ["RLAND%d" % t, "LX5", "GBH"], ["E1"])
+    op("p", mm(T.G4[:, 0:16], T.E1[:], T.DIAG[:, 0:16], True, True), ["E1", "DIAG"], ["G4"])
+    ts(T.CB[:], T.PG4[:, 0:256], 16.0, A.mult, ["PG4f"], ["CB"], -1.0, A.add)
+    tt(T.PF[:, 256:512], T.CB[:], T.PG4[:, 256:512], A.add, ["CB", "PG4f"], ["YB0"])
+    tt(T.PF[:, t:256:16], T.G4[:, 0:16], T.PF[:, t:256:16], A.add, ["G4", "YA0"], ["YA0"])
+    dma("y", [(T.yb[:], T.PF[:, 256:512])], ["YB0"], ["yb"])
+    dma("y", [(T.ya[:], T.PF[:, 0:256])], ["YA0"], ["ya"])
     for sem in sorted(last):
         need("g", {sem: last[sem]})

from concourse.mybir import AluOpType, AxisListType, ActivationFunctionType

W = 4096
WX = 4608
DEAD = 4096.0
DUM = 4352
NB, ND = 3, 3
BAR = 4095.0 * 4096.0

_B = {}


def _sb(name, cols, dtype):
    _B[name] = ("sbuf", [128, cols], dtype)


_sb("X", WX, "bfloat16"); _sb("XC0", WX, "bfloat16"); _sb("XC1", WX, "bfloat16")
_sb("TA", WX, "float32"); _sb("TB", WX, "float32")
_sb("PAI", 256, "int32"); _sb("PBI", 256, "int32"); _sb("PF", 512, "float32"); _sb("PG4", 512, "float32")
_sb("BI", 384, "int32"); _sb("BF", 448, "float32")
_sb("WI", 8, "int32"); _sb("WF2", 8, "float32")
_sb("CI5", 256, "int32"); _sb("CT1", 256, "int32"); _sb("CT2", 256, "int32"); _sb("CA", 512, "float32"); _sb("CB", 256, "float32")
_sb("PI", 8, "int32"); _sb("PT", 16, "int32"); _sb("PC", 16, "float32"); _sb("CF", 256, "float32")
_sb("WH", 512, "bfloat16"); _sb("WL", 512, "bfloat16")
_sb("OB", 8, "bfloat16"); _sb("IDF", 128, "float32"); _sb("PEN", 128, "bfloat16"); _sb("ZB", 256, "bfloat16")
_sb("DIAG", 256, "float32"); _sb("DG2", 256, "float32"); _sb("M1", 128, "float32"); _sb("RS1", 32, "float32")
_sb("CL", 256, "float32"); _sb("CR", 256, "float32"); _sb("RC", 256, "float32"); _sb("TH2", 256, "float32")
_sb("RHL", 24, "bfloat16")
_sb("SR14", 128, "float32")
_sb("SRB", 384, "bfloat16")
_sb("IBN", 256, "bfloat16")
_sb("GBH", 128, "bfloat16"); _sb("ONES", 128, "bfloat16")
_sb("RS8", 256, "float32"); _sb("RS16", 256, "float32")
_sb("LX1", 8, "uint16"); _sb("LX2", 16, "uint16"); _sb("LX3", 8, "uint16"); _sb("LX4", 16, "uint16"); _sb("LX5", 16, "uint16")
_sb("LXI", 16, "int32"); _sb("LXJ", 16, "int32")
_sb("SCOL", 4, "float32"); _sb("ABASE", 4, "float32"); _sb("ACOL", 4, "float32"); _sb("ATMP", 4, "float32")
_sb("FBC", 16, "float32"); _sb("FB4C", 64, "float32")
_sb("SSND", 256 * NB, "bfloat16"); _sb("SLAND", 256 * NB, "bfloat16")
_sb("DSND", 16 * NB, "float32"); _sb("DLAND", 16 * NB, "float32")
_sb("NSND", 256 * NB * ND, "bfloat16"); _sb("NLAND", 256 * NB * ND, "bfloat16")
_sb("LSND", 16 * NB * ND, "uint16"); _sb("LLAND", 16 * NB * ND, "uint16")
_sb("RSND", 32 * NB, "float32"); _sb("RLAND", 32 * NB, "float32")
_sb("Z", 256, "bfloat16"); _sb("Z4", 1024, "bfloat16"); _sb("SH", 256, "float32")
_sb("NI", 64, "int32"); _sb("UF", 64, "float32"); _sb("SQ", 256, "float32"); _sb("FI", 256, "int32"); _sb("CI", 256, "int32")
_sb("OFF", 256, "uint16"); _sb("CFL", 256, "float32"); _sb("EQ", 256, "bfloat16")
_sb("DF", 4096, "bfloat16"); _sb("AB", 4096, "bfloat16")
_sb("R", 256, "float32"); _sb("E1", 128, "float32"); _sb("R4", 128, "float32")
_sb("MN", 16, "float32"); _sb("YI", 16, "int32"); _sb("YA", 16, "int32"); _sb("YQ", 16, "float32"); _sb("YU", 16, "uint16")
_sb("FB", 16, "float32"); _sb("FB4", 64, "float32"); _sb("L1", 64, "float32"); _sb("L2", 64, "int32"); _sb("LAST", 64, "int32")
_sb("QL", 256, "bfloat16"); _sb("QR", 256, "bfloat16"); _sb("QE", 256, "bfloat16"); _sb("QO", 256, "bfloat16")
_sb("TT", 256, "float32"); _sb("T2", 256, "float32"); _sb("FL", 16, "float32"); _sb("JK", 1280, "bfloat16")
_sb("E2", 256, "bfloat16"); _sb("LF", 16, "float32"); _sb("UP", 256, "float32"); _sb("PG", 256, "bfloat16")
_sb("DM", 256, "float32"); _sb("SC", 256, "float32"); _sb("PU", 16, "uint16"); _sb("E3", 512, "bfloat16"); _sb("E4", 256, "bfloat16")
_sb("W1", 16, "float32"); _sb("W2", 16, "float32"); _sb("W3", 16, "float32"); _sb("WB", 16, "bfloat16")
_sb("DEADL", 16, "float32"); _sb("RES", 16, "float32"); _sb("KP", 8, "float32"); _sb("KI", 8, "int32")
for _n in ["G0", "G1", "G2", "G3", "G4", "G5", "K6", "C7"]:
    _B[_n] = ("psum", [128, 512], "float32")
_B["BD"] = ("dram", [14, 128, 32], "float32")
_B["PD"] = ("dram", [4, 128, 256], "float32")
SCRATCH = _B

_MSG = []
for _t in range(NB):
    _MSG += ["s%d" % _t, "b%d" % _t, "e%d" % _t, "r%d" % _t]
    for _d in range(ND - 1):
        _MSG += ["n%d%d" % (_t, _d), "l%d%d" % (_t, _d)]
SEMAPHORES = ["cv", "cs", "cp", "cg"] + ["rx" + m for m in _MSG] + ["tx" + m for m in _MSG] + ["dm%d" % i for i in range(16)]


def rank_program(g, core, T, topo):
    rank = T.rank_of(core)
    if rank is None:
        return
    A = AluOpType
    F = ActivationFunctionType
    RH, RL0, RL1 = T.RHL[:, 0:8], T.RHL[:, 8:16], T.RHL[:, 16:24]
    SRP, SRH, SRL = [T.SRB[:, 128 * i:128 * i + 128] for i in range(3)]
    n_ranks = len(T.cores)
    nxt, prv = (rank + 1) % n_ranks, (rank - 1) % n_ranks
    Q = {"v": g.vector, "s": g.scalar, "p": g.tensor, "g": g, "y": g.sync}
    cnt = {"v": 0, "s": 0, "p": 0, "g": 0}
    waited = {q: {} for q in Q}
    wr = {}
    rd = {}
    nd = [0]
    last = {}

    def need(q, toks):
        for sem in sorted(toks):
            if waited[q].get(sem, 0) < toks[sem]:
                Q[q].wait_ge(T.sem[sem], toks[sem])
                waited[q][sem] = toks[sem]

    def deps(reads, writes, own=None):
        toks = {}
        for k in reads:
            for s, v in wr.get(k, {}).items():
                toks[s] = max(toks.get(s, 0), v)
        for k in writes:
            for m in (wr, rd):
                for s, v in m.get(k, {}).items():
                    if s != own:
                        toks[s] = max(toks.get(s, 0), v)
        return toks

    def note(reads, writes, sem, val):
        for k in writes:
            wr[k] = {sem: val}
            rd[k] = {}
        for k in reads:
            if k not in writes:
                m = rd.setdefault(k, {})
                m[sem] = max(m.get(sem, 0), val)
        last[sem] = max(last.get(sem, 0), val)

    def op(q, fns, reads, writes, acc=False):
        need(q, deps(reads, writes, "c" + q if acc else None))
        for fn in (fns if isinstance(fns, list) else [fns]):
            cnt[q] += 1
            fn().then_inc(T.sem["c" + q], 1)
        note(reads, writes, "c" + q, cnt[q])

    def dma(q, pieces, reads, writes):
        need(q, deps(reads, writes))
        sem = "dm%d" % nd[0]
        nd[0] += 1
        for out, in_ in pieces:
            Q[q].dma_start(out, in_).then_inc(T.sem[sem], 16)
        note(reads, writes, sem, 16 * len(pieces))

    def engs(src, dst):
        e = topo.engines(src, dst)
        m = 0
        for x in e:
            m |= 1 << x
        return m, len(e)

    def send(to, msg, out, in_, reads):
        need("g", deps(reads, []))
        dst = T.cores[to]
        rid, pid, _se = topo.addr(dst)
        m, n = engs(core, dst)
        g.remote_dma(out, in_, T.sem["rx" + msg], T.sem["tx" + msg], pid, rid, m)
        note(reads, [], "tx" + msg, n)

    def landed(frm, msg, keys):
        note([], keys, "rx" + msg, engs(T.cores[frm], core)[1])

    def ts(out, in0, s1, o0, r, w, s2=None, o1=None):
        if o1 is None:
            op("v", lambda: g.vector.tensor_scalar(out, in0, s1, None, o0), r, w)
        else:
            op("v", lambda: g.vector.tensor_scalar(out, in0, s1, s2, o0, o1), r, w)

    def tt(out, a, b, o, r, w):
        op("v", lambda: g.vector.tensor_tensor(out, a, b, o), r, w)

    def cp(out, a, r, w):
        op("v", lambda: g.vector.tensor_copy(out, a), r, w)

    def scan(out, d0, d1, o0, o1, r, w):
        op("v", lambda: g.vector.tensor_tensor_scan(out, d0, d1, 0.0, o0, o1), r, w)

    def ms(ap, c, w):
        op("v", lambda: g.vector.memset(ap, c), [], w)

    def act(out, in_, f, r, w, **kw):
        op("s", lambda: g.scalar.activation(out, in_, f, **kw), r, w)

    def mm(out, lhsT, rhs, start, stop):
        return lambda: g.tensor.matmul(out, lhsT, rhs, start, stop)

    def row_to_list(src, lhsT, rows, bank, bkey, fin, *between):
        op("p", mm(bank[:, 0:256], lhsT, src, True, True), rows, [bkey])
        tt(T.DM[:], bank[:, 0:256], T.DIAG[:], A.mult, [bkey, "DIAG"], ["DM"])
        for f in between[0:1]:
            f()
        scan(T.SC[:], T.RS16[:], T.DM[:], A.mult, A.add, ["RS16", "DM"], ["SC"])
        for f in between[1:]:
            f()
        fin(T.SC[:, 15:256:16])

    def dead_done(t):
        def fin(ap):
            ts(T.DSND[:, 16 * t:16 * t + 16], ap, 1.0, A.min, ["SC"], ["DSND%d" % t], DEAD, A.mult)
            send(nxt if t % 2 == 0 else prv, "e%d" % t, T.DLAND[:, 16 * t:16 * t + 16], T.DSND[:, 16 * t:16 * t + 16], ["DSND%d" % t])
        return fin

    def start_batch(t):
        to = nxt if t % 2 == 0 else prv
        act(T.SSND[:, 256 * t:256 * t + 256], T.X[:, t:W:16], F.Copy, ["X"], ["SSND%d" % t])
        send(to, "s%d" % t, T.SLAND[:, 256 * t:256 * t + 256], T.SSND[:, 256 * t:256 * t + 256], ["SSND%d" % t])
        xc = T.XC0 if t % 2 == 0 else T.XC1
        send(to, "b%d" % t, xc[:, 0:W], T.X[:, 0:W], ["X"])
        landed(prv if t % 2 == 0 else nxt, "s%d" % t, ["SLAND%d" % t])

    def near_send(t):
        hi, lo = T.RSND[:, 32 * t:32 * t + 16], T.RSND[:, 32 * t + 16:32 * t + 32]
        if t == NB - 1:
            cp(hi, T.RES[:], ["RES"], ["RSH%d" % t])
            send(prv if t % 2 == 0 else nxt, "r%d" % t, T.RLAND[:, 32 * t:32 * t + 16], hi, ["RSH%d" % t])
            return
        ts(T.LXJ[:], T.RES[:], -1.0, A.add, ["RES"], ["LXJ"])
        ts(T.LXI[:], T.LXJ[:], 4, A.arith_shift_right, ["LXJ"], ["LXI"])
        ts(hi, T.LXI[:], 0.0, A.max, ["LXI"], ["RSH%d" % t])
        ts(T.W2[:], hi, -16.0, A.mult, ["RSH%d" % t], ["W2"])
        tt(lo, T.RES[:], T.W2[:], A.add, ["RES", "W2"], ["RSL%d" % t])
        send(prv if t % 2 == 0 else nxt, "r%d" % t, T.RLAND[:, 32 * t:32 * t + 32], T.RSND[:, 32 * t:32 * t + 32], ["RSH%d" % t, "RSL%d" % t])

    def near_rows(t):
        landed(nxt if t % 2 == 0 else prv, "r%d" % t, ["RLAND%d" % t])
        for i in range(2):
            tt(T.E3[:, 256 * i:256 * i + 256], T.RLAND[:, 32 * t + 16 * i:32 * t + 16 * i + 16].indirect(T.LX4[:]), T.DIAG[:], A.mult,
               ["RLAND%d" % t, "LX4", "DIAG"], ["E3_%d" % i])
        op("p", [mm(T.G4[:, 0:256], SRH, T.E3[:, 0:256], True, False), mm(T.G4[:, 0:256], SRL, T.E3[:, 256:512], False, True)],
           ["SRH", "SRL", "E3_0", "E3_1"], ["G4"])

    def near_add(t):
        near, nk = (T.TA, "TA") if t % 2 == 0 else (T.TB, "TB")
        tt(near[:, t:W:16], T.G4[:, 0:256], near[:, t:W:16], A.add, ["G4", nk], [nk])

    dma("s", [(T.PAI[:], T.pa[:])], [], ["PAI"])
    dma("y", [(T.X[:, 0:W], T.x[:])], [], ["X"])
    dma("s", [(T.PBI[:], T.pb[:])], [], ["PBI"])
    dma("s", [(T.WI[:, 0:1], T.wt[:])], [], ["WI"])
    op("g", lambda: g.iota(T.PI[:, 0:1], [[0, 1]], 0, 1), [], ["PI"])
    op("g", lambda: g.iota(T.BI[:, 0:32], [[1, 32]], 0, 32), [], ["BI0"])
    op("g", lambda: g.iota(T.CI5[:], [[1, 256]], 0, 0), [], ["CI5"])
    op("g", lambda: g.iota(T.LXI[:, 0:8], [[32, 8]], 7, 0), [], ["LXI"])
    for nm in ("X", "XC0", "XC1"):
        op("g", lambda: g.iota(T[nm][:, W:WX], [[0, WX - W]], 0, 0, allow_small_or_imprecise_dtypes=True), [], [nm + "x"])
    for c, k, v in [(0, "s", 4), (1, "a", 15), (2, "a", 3), (3, "s", 2)]:
        ts(T.PT[:, c:c + 1], T.PI[:, 0:1], v, A.arith_shift_right if k == "s" else A.bitwise_and, ["PI"], ["PT%d" % c])
    cp(T.PC[:, 0:4], T.PT[:, 0:4], ["PT0", "PT1", "PT2", "PT3"], ["PC0"])
    cp(T.PC[:, 4:5], T.PI[:, 0:1], ["PI"], ["PC4"])
    PGRP, PLOW, PL3, PS2, PP = T.PC[:, 0:1], T.PC[:, 1:2], T.PC[:, 2:3], T.PC[:, 3:4], T.PC[:, 4:5]
    for i, r in enumerate((12, 13, 14, 15)):
        ts(T.PC[:, 8 + i:9 + i], PLOW, float(r), A.is_equal, ["PC0"], ["PC%d" % (8 + i)])
    I12, I13, I14, I15 = [T.PC[:, 8 + i:9 + i] for i in range(4)]
    ts(T.PT[:, 4:5], T.PI[:, 0:1], 4, A.arith_shift_right, ["PI"], ["PT4"], 1, A.bitwise_and)
    ECOL, OCOL = T.WF2[:, 6:7], T.WF2[:, 5:6]
    for f in range(1, 12):
        ts(T.BI[:, 32 * f:32 * f + 32], T.BI[:, 0:32], f, A.arith_shift_right, ["BI0"], ["BI%d" % f], 1, A.bitwise_and)
    ts(T.BI[:, 0:32], T.BI[:, 0:32], 1, A.bitwise_and, ["BI0"], ["BI0"])
    ts(T.BF[:, 0:384], T.BI[:], 2.0, A.mult, ["BI%d" % f for f in range(12)], ["BFA"], -1.0, A.add)
    ms(T.BF[:, 384:448], 1.0, ["BFB"])
    dma("y", [(T.BD[f], T.BF[:, 32 * f:32 * f + 32]) for f in range(14)], ["BFA", "BFB"], ["BD"])
    ts(T.CT1[:], T.CI5[:], 15, A.bitwise_and, ["CI5"], ["CT1"])
    ts(T.CT2[:], T.CI5[:], 4, A.arith_shift_right, ["CI5"], ["CT2"])
    ts(T.GBH[:], T.CT2[:, 0:128], PGRP, A.is_equal, ["CT2", "PC0"], ["GBH"])
    ts(T.DG2[:], T.CT2[:], PLOW, A.is_equal, ["CT2", "PC0"], ["DG2"])
    ms(T.CA[:, 0:16], 0.0, ["CA"])
    ts(T.LX5[:], T.CA[:, 0:16], PLOW, A.add, ["CA", "PC0"], ["LX5"])
    ts(T.W1[:], T.PAI[:, 0:256:16], 0.0, A.is_ge, ["PAI"], ["W1"])
    tt(T.E4[:], T.W1[:, 0:16].indirect(T.LX5[:]), T.DG2[:], A.mult, ["W1", "LX5", "DG2"], ["E4"])
    ts(T.RS16[:], T.CT1[:], 0.0, A.not_equal, ["CT1"], ["RS16"])
    ts(T.DIAG[:], T.CT1[:], PLOW, A.is_equal, ["CT1", "PC0"], ["DIAG"])
    row_to_list(T.E4[:], T.GBH[:], ["E4", "GBH"], T.G3, "G3", dead_done(0))
    start_batch(0)
    wr["X"] = deps(["X", "Xx"], [])
    def table_rows(pin, pk, i):
        hi, lo = T.PF[:, 256 * i:256 * i + 256], T.PG4[:, 256 * i:256 * i + 256]
        ts(T.CT1[:], pin[:], 4, A.arith_shift_right, [pk], ["CT1"])
        ts(hi, T.CT1[:], 0.0, A.max, ["CT1"], ["PF%d" % i])
        ts(T.CB[:], hi, -16.0, A.mult, ["PF%d" % i], ["CB"], 1.0, A.add)
        tt(lo, T.CB[:], pin[:], A.add, ["CB", pk], ["PG4%d" % i])
        dma("y", [(T.PD[2 * i], hi), (T.PD[2 * i + 1], lo)], ["PF%d" % i, "PG4%d" % i], ["PD%d" % i])

    def fill_table(tab, key, pv, pf, pk):
        pieces = [(tab[16 * b:16 * b + 14, 0:W], T.BD[:]) for b in range(8)]
        pieces += [(tab[15:128:16, 0:W], pv), (tab[14:128:16, 0:W], pf)]
        dma("y", pieces, ["BD", pk], [key])

    table_rows(T.PBI, "PBI", 0)
    fill_table(T.TB, "TBd", T.PD[0], T.PD[1], "PD0")
    ts(T.WI[:, 2:3], T.WI[:, 0:1], 3840, A.bitwise_and, ["WI"], ["WI2"])
    ts(T.WI[:, 3:4], T.WI[:, 0:1], 255, A.bitwise_and, ["WI"], ["WI3"])
    ts(T.WF2[:, 0:2], T.WI[:, 2:4], 1.0 / 4096, A.mult, ["WI2", "WI3"], ["WF2"])
    ts(T.CA[:, 0:128], T.CT2[:, 0:128], PGRP, A.is_equal, ["CT2", "PC0"], ["CA"], 100.0, A.mult)
    ts(T.CT1[:, 0:128], T.CI5[:, 0:128], 2, A.arith_shift_right, ["CI5"], ["CT1"], 3, A.bitwise_and)
    tt(T.CB[:, 0:128], T.CT1[:, 0:128], T.CA[:, 0:128], A.add, ["CT1", "CA"], ["CB"])
    for ll in range(4):
        for wm, wc in ((T.WH, 0), (T.WL, 1)):
            ts(wm[:, 128 * ll:128 * ll + 128], T.CB[:, 0:128], 100.0 + ll, A.is_equal, ["CB", "WF2"], ["WHL%d%d" % (ll, wc)], T.WF2[:, wc:wc + 1], A.mult)
    WHL = ["WHL%d%d" % (i, j) for i in range(4) for j in range(2)]
    ts(T.M1[:], T.CT1[:, 0:128], PL3, A.is_equal, ["CT1", "PC0"], ["M1"])
    for ch in range(4):
        ts(T.SCOL[:, ch:ch + 1], PL3, 32.0, A.mult, ["PC0"], ["SCOL"], 128.0 * ch + 16.0, A.add)
    tt(T.ATMP[:], T.SCOL[:], T.SCOL[:], A.mult, ["SCOL"], ["ATMP"])
    ts(T.ABASE[:], T.ATMP[:], -1.0, A.mult, ["ATMP"], ["ABASE"], 262144.0 - 12.0, A.add)
    ts(T.ACOL[:], T.ABASE[:], 0.0, A.add, ["ABASE"], ["ACOL"])
    cp(T.CF[:], T.CI5[:], ["CI5"], ["CF"])
    ts(T.IDF[:], T.CF[:, 0:128], PP, A.is_equal, ["CF", "PC4"], ["IDF"])
    ts(T.PC[:, 12:13], PLOW, 12.0, A.is_lt, ["PC0"], ["PC12"])
    ts(T.PC[:, 7:8], I12, -1.0, A.mult, ["PC8"], ["PC7"])
    ts(T.PC[:, 13:14], T.PC[:, 12:13], 128.0, A.mult, ["PC12", "PC8"], ["PC13"], I12, A.add)
    ts(T.PC[:, 14:15], I14, 2048.0, A.mult, ["PC10"], ["PC14"])
    tt(T.PC[:, 13:14], T.PC[:, 13:14], T.PC[:, 14:15], A.add, ["PC13", "PC14"], ["PC13"])
    ts(T.PC[:, 15:16], T.PC[:, 12:13], I13, A.add, ["PC12", "PC9", "PC10"], ["PC15"], I14, A.add)
    ts(T.WF2[:, 4:5], PLOW, 14.0, A.is_lt, ["PC0", "PC10"], ["WF4"], -2.0, A.mult)
    tt(T.WF2[:, 4:5], T.WF2[:, 4:5], I14, A.add, ["WF4", "PC10"], ["WF4"])
    ts(T.WF2[:, 3:4], I15, 16.0, A.mult, ["PC11", "PC10"], ["WF3"], I14, A.add)
    cp(T.WF2[:, 5:6], T.PT[:, 4:5], ["PT4"], ["WF5"])
    ts(T.WF2[:, 6:7], T.WF2[:, 5:6], -1.0, A.mult, ["WF5"], ["WF6"], 1.0, A.add)
    ts(T.OB[:], T.CF[:, 0:8], PGRP, A.is_equal, ["CF", "PC0"], ["OB"], 4096.0, A.mult)
    ms(T.ZB[:], 0.0, ["ZB"])
    ts(T.CT1[:], T.CI5[:], 7, A.bitwise_and, ["CI5"], ["CT1"])
    ts(T.RS8[:], T.CT1[:], 0.0, A.is_equal, ["CT1"], ["RS8"], float(2 ** 26), A.mult)
    ts(T.RS1[:], T.CF[:, 0:32], PS2, A.is_equal, ["CF", "PC0"], ["RS1"])
    ts(T.PC[:, 5:6], PL3, 8.0, A.mult, ["PC0"], ["PC5"])
    ts(T.LX1[:], T.LXI[:, 0:8], T.PC[:, 5:6], A.add, ["LXI", "PC5"], ["LX1"])
    ts(T.PT[:, 6:7], T.PI[:, 0:1], 2, A.arith_shift_right, ["PI"], ["PT6"], 3, A.bitwise_and)
    ts(T.PC[:, 6:7], T.PT[:, 6:7], 8.0, A.mult, ["PT6"], ["PC6"])
    ts(T.LX3[:], T.LXI[:, 0:8], T.PC[:, 6:7], A.add, ["LXI", "PC6"], ["LX3"])
    ms(T.FBC[:], 16777215.0, ["FBC"])
    ms(T.FB4C[:], 16777215.0, ["FB4C"])
    act(T.IBN[:, 0:128], T.IDF[:], F.Identity, ["IDF"], ["IBN0"])
    act(T.IBN[:, 128:256], T.IDF[:], F.Identity, ["IDF"], ["IBN1"], scale=-1.0)
    act(T.CL[:], T.CF[:], F.Identity, ["CF", "PC9", "PC13"], ["CL"], scale=I13, bias=T.PC[:, 13:14])
    act(T.CR[:], T.CF[:], F.Identity, ["CF", "PC7", "PC15"], ["CR"], scale=T.PC[:, 7:8], bias=T.PC[:, 15:16])
    for i in range(2):
        act(T.TB[:, W + 256 * i:W + 256 * i + 256], T.CF[:], F.Identity, ["CF", "PC10"], ["TBx%d" % i], scale=0.0, bias=I14)
    wr["TB"] = deps(["TBd", "TBx0", "TBx1"], [])

    def scalar_constants():
        act(T.PEN[:], T.IDF[:], F.Identity, ["IDF"], ["PEN"], scale=float(2 ** 25))
        act(T.RC[:], T.CF[:], F.Identity, ["CF", "PC11", "WF4"], ["RC"], scale=I15, bias=T.WF2[:, 4:5])
        act(SRP, T.GBH[:], F.Identity, ["GBH", "WF3"], ["SRP"], scale=T.WF2[:, 3:4])
        act(T.SR14[:], T.GBH[:], F.Identity, ["GBH", "PC10"], ["SR14"], scale=I14)
        for i in range(2):
            act(T.TA[:, W + 256 * i:W + 256 * i + 256], T.CF[:], F.Identity, ["CF", "PC10"], ["TAx%d" % i], scale=0.0, bias=I14)

    def later_constants():
        ts(T.CT2[:, 0:16], T.CI5[:, 0:16], 7, A.bitwise_and, ["CI5"], ["CT2"])
        cp(T.LX2[:], T.CT2[:, 0:16], ["CT2"], ["LX2"])
        ts(T.CT1[:], T.CI5[:], 4, A.arith_shift_right, ["CI5"], ["CT1"], 7, A.bitwise_and)
        for h in range(2):
            ts(T.CA[:, 128 * h:128 * h + 128], T.CT1[:, 128 * h:128 * h + 128], 4.0 + h, A.is_lt, ["CT1"], ["CA"], 1536.0, A.mult)
        ts(T.CB[:], T.DIAG[:], 0.0, A.is_equal, ["DIAG"], ["CB"], 1e25, A.mult)
        tt(T.TH2[:], T.CA[:, 0:256], T.CB[:], A.max, ["CA", "CB"], ["TH2"])
        ts(RH, T.CF[:, 0:8], PGRP, A.is_equal, ["CF", "PC0"], ["RH"], float(DUM), A.mult)
        ts(RL0, T.CF[:, 0:8], PGRP, A.is_equal, ["CF", "PC0", "PC4"], ["RL0"], PP, A.mult)
        ts(T.WF2[:, 7:8], PP, 128.0, A.add, ["PC4"], ["WF7"])
        ts(RL1, T.CF[:, 0:8], PGRP, A.is_equal, ["CF", "PC0", "WF7"], ["RL1"], T.WF2[:, 7:8], A.mult)

    def last_constants():
        ms(T.ONES[:], 1.0, ["ONES"])
        ts(T.CT2[:, 0:128], T.CI5[:, 0:128], 15, A.bitwise_and, ["CI5"], ["CT2"])
        for i, sel in ((15, SRH), (14, SRL)):
            ts(T.CA[:, 0:128], T.CT2[:, 0:128], float(i), A.is_equal, ["CT2"], ["CA"])
            tt(sel, T.CA[:, 0:128], T.GBH[:], A.mult, ["CA", "GBH"], ["SRH" if i == 15 else "SRL"])
        cp(T.LX4[:], T.CI5[:, 0:16], ["CI5"], ["LX4"])
        table_rows(T.PAI, "PAI", 1)
        fill_table(T.TA, "TAd", T.PD[2], T.PD[3], "PD1")
        wr["TA"] = deps(["TAd", "TAx0", "TAx1"], [])

    BANKS = [T.G0, T.G1, T.G2, T.G3, T.G4, T.G5]
    for t in range(NB):
        frm, to = (prv, nxt) if t % 2 == 0 else (nxt, prv)
        far, fk = (T.TB, "TB") if t % 2 == 0 else (T.TA, "TA")
        XC, xk = (T.XC0, "XC0") if t % 2 == 0 else (T.XC1, "XC1")
        for d in range(ND):
            m = t * ND + d
            tail = d == ND - 1
            if d == 0:
                z, zk = T.SLAND[:, 256 * t:256 * t + 256], "SLAND%d" % t
            else:
                z, zk = T.Z[:], "Z"
                pm = m - 1
                msg = "%d%d" % (t, d - 1)
                if d == 1:
                    landed(frm, "b%d" % t, [xk + "b"])
                    wr[xk] = deps([xk + "b", xk + "x"], [])
                landed(frm, "n" + msg, ["NLAND%d" % pm])
                landed(frm, "l" + msg, ["LLAND%d" % pm])
                cp(XC[:, 0:WX].indirect(T.LLAND[:, 16 * pm:16 * pm + 16]), T.NLAND[:, 256 * pm:256 * pm + 256],
                   ["NLAND%d" % pm, "LLAND%d" % pm], [xk])
                cp(T.Z[:], XC[:, 0:WX].indirect(T.PU[:]), [xk, "PU"], ["Z"])

            result = (lambda: ts(T.W3[:], T.YQ[:], 1.0, A.add, ["YQ"], ["W3"]),
                      lambda: tt(T.W2[:], T.W3[:], T.WB[:], A.mult, ["W3", "WB"], ["W2"]),
                      lambda: tt(T.RES[:], T.RES[:], T.W2[:], A.add, ["RES", "W2"], ["RES"]))

            fs = []
            for ll in range(4):
                zs = T.SLAND[:, 256 * t + ll:256 * t + 256:4] if d == 0 else T.Z[:, ll:256:4]
                fs.append(mm(T.K6[:, 0:64], T.WH[:, 128 * ll:128 * ll + 128], zs, ll == 0, False))
                fs.append(mm(T.K6[:, 0:64], T.WL[:, 128 * ll:128 * ll + 128], zs, False, ll == 3))
            op("p", fs, WHL + [zk], ["K6"])
            for cl in range(4):
                cp(T.Z4[:, cl:1024:4], z, [zk], ["Z4_%d" % cl])
            ts(T.NI[:], T.K6[:, 0:64], -0.5, A.add, ["K6"], ["NI"])
            tt(T.UF[:], T.K6[:, 0:64], T.NI[:], A.subtract, ["K6", "NI"], ["UF"])
            for ch in range(4):
                act(T.SQ[:, 64 * ch:64 * ch + 64], T.UF[:], F.Square, ["UF", "SCOL"], ["SQ%d" % ch], bias=T.SCOL[:, ch:ch + 1], scale=4096.0)

            def floors(ch):
                ts(T.FI[:, 64 * ch:64 * ch + 64], T.SQ[:, 64 * ch:64 * ch + 64], T.ACOL[:, ch:ch + 1], A.add, ["SQ%d" % ch, "ACOL"], ["FI%d" % ch], 1.0 / 32, A.mult)

            def places(c0, c1):
                keys = [str(ch) for ch in range(c0, c1)]
                ts(T.CI[:, 64 * c0:64 * c1], T.FI[:, 64 * c0:64 * c1], 4095, A.bitwise_and, ["FI" + c for c in keys], ["CI" + c for c in keys])

            def bars(ch):
                tt(T.EQ[:, 64 * ch:64 * ch + 64], T.CI[:, 64 * ch:64 * ch + 64], T.LAST[:], A.is_equal, ["CI%d" % ch, "LAST"], ["EQ%d" % ch])

            def lists(c0, c1):
                keys = [str(ch) for ch in range(c0, c1)]
                cp(T.OFF[:, 64 * c0:64 * c1], T.CI[:, 64 * c0:64 * c1], ["CI" + c for c in keys], ["OFF" + c for c in keys])

            if d == 0:
                act(T.SH[:], z, F.Copy, [zk], ["SH"], bias=-0.5)

            def gather(c0, n):
                a, b, zo = 16 * c0, 16 * (c0 + n), 16 * (c0 % 64)
                tt(T.DF[:, a:b], T.X[:, 0:WX].indirect(T.OFF[:, c0:c0 + n]), T.Z4[:, zo:zo + 16 * n], A.subtract,
                   ["X", "OFF%d" % (c0 // 64), "Z4_0", "Z4_1", "Z4_2", "Z4_3"], ["DF%d" % c0])
                act(T.AB[:, a:b], T.DF[:, a:b], F.Abs, ["DF%d" % c0], ["AB%d" % c0])

            def dsum(c0, n, p0, pr, keys):
                fs = []
                for part in range(16):
                    o = 2 * part + pr
                    fs.append(mm(T.K6[p0:p0 + n, o:256:32], T.AB[:, 16 * c0 + part:16 * (c0 + n):16], T.OB[:], False, False))
                op("p", fs, keys + ["OB"], ["K6"], True)

            floors(0)
            floors(1)
            places(0, 1)
            floors(2)
            lists(0, 1)
            floors(3)
            act(T.DF[:, 512:1024], T.X[:, 0:WX].indirect(T.OFF[:, 32:64]), F.Copy, ["X", "OFF0"], ["DF32"])
            op("p", [mm(T.G0[:], T.IBN[:, 0:128], T.DF[:, 512:1024], True, False), mm(T.G0[:], T.IBN[:, 128:256], T.Z4[:, 512:1024], False, True)],
               ["IBN0", "IBN1", "DF32", "Z4_0", "Z4_1", "Z4_2", "Z4_3"], ["G0"])
            gather(0, 32)
            act(T.AB[:, 512:1024], T.G0[:], F.Abs, ["G0"], ["AB32"])
            places(1, 4)
            if d > 0:
                bars(0)
            lists(1, 4)
            cis = ["CI0", "CI1", "CI2", "CI3"]
            cp(T.CFL[:], T.CI[:], cis, ["CFL"])
            op("p", [mm(T.K6[:, 0:256], T.ZB[:, 0:128], T.ZB[:], True, False)] +
               [mm(T.K6[:, pr:256:2], T.CFL[:, 128 * pr:128 * pr + 128], T.IDF[:], False, False) for pr in range(2)], ["ZB", "CFL", "IDF"], ["K6"])
            gather(64, 64)
            dsum(0, 128, 0, 0, ["AB0", "AB32", "AB64"])
            gather(128, 32)
            gather(160, 32)
            dsum(128, 64, 0, 1, ["AB128", "AB160"])
            if d == 0 and t > 0:
                near_rows(t - 1)
            gather(192, 32)
            dsum(192, 32, 64, 1, ["AB192"])
            gather(224, 16)
            gather(240, 16)
            if d > 0:
                for ch in range(1, 4):
                    bars(ch)
            dsum(224, 32, 96, 1, ["AB224", "AB240"])
            if d > 0:
                op("p", [mm(T.K6[:, pr:256:2], T.EQ[:, 128 * pr:128 * pr + 128], T.PEN[:], False, False) for pr in range(2)], ["EQ0", "EQ1", "EQ2", "EQ3", "PEN"], ["K6"], True)
            op("p", mm(T.K6[:, 0:256], T.ZB[:, 0:128], T.ZB[:], False, True), ["ZB"], ["K6"], True)
            if d == 0:
                landed(frm, "e%d" % t, ["DLAND%d" % t])
                cp(T.DEADL[:], T.DLAND[:, 16 * t:16 * t + 16], ["DLAND%d" % t], ["DEADL"])
                ms(T.RES[:], 0.0, ["RES"])
                if t > 0:
                    near_add(t - 1)
                    ts(T.RC[:], T.RC[:], I14, A.add, ["RC", "PC10"], ["RC"])
                else:
                    later_constants()
            else:
                ts(T.W1[:], T.WB[:], DEAD, A.mult, ["WB"], ["W1"])
                tt(T.DEADL[:], T.DEADL[:], T.W1[:], A.max, ["DEADL", "W1"], ["DEADL"])
                ts(T.FB[:], T.YA[:], BAR, A.add, ["YA"], ["FB"])
            if m == 0:
                scalar_constants()
            scan(T.R[:], T.RS8[:], T.K6[:, 0:256], A.max, A.min, ["RS8", "K6"], ["R"])
            tt(T.E1[:], T.R[:, 0:256].indirect(T.LX1[:]), T.M1[:], A.mult, ["R", "LX1", "M1"], ["E1"])
            op("p", mm(T.C7[:, 0:32], T.E1[:], T.RS1[:], True, True), ["E1", "RS1"], ["C7"])
            if not tail:
                act(T.R4[:], T.R[:, 0:256].indirect(T.LX3[:]), F.Copy, ["R", "LX3"], ["R4"])
                op("p", mm(T.K6[:, 0:128], T.R4[:], T.IDF[:], True, True), ["R4", "IDF"], ["K6"])
            fb, fbk = (T.FBC, "FBC") if d == 0 else (T.FB, "FB")
            rs = list(result) if d > 0 else [lambda: None] * 3
            tt(T.MN[:], T.C7[:, 16:32], fb[:], A.min, ["C7", fbk], ["MN"])
            rs[0]()
            tt(T.YI[:], T.C7[:, 0:16], T.MN[:], A.min, ["C7", "MN"], ["YI"])
            rs[1]()
            ts(T.YA[:], T.YI[:], 4095, A.bitwise_and, ["YI"], ["YA"])
            rs[2]()
            tt(T.YQ[:], T.YA[:], T.DEADL[:], A.max, ["YA", "DEADL"], ["YQ"])
            cp(T.YU[:], T.YQ[:], ["YQ"], ["YU"])
            for h in range(2):
                a, b, yl = 128 * h, 128 * h + 128, T.YU[:, 8 * h:8 * h + 8]
                tt(T.QL[:, a:b], far[:, 0:WX].indirect(yl), T.CL[:, a:b], A.mult, [fk, "YU", "CL"], ["QL%d" % h])
                act(T.QE[:, a:b], T.QL[:, a:b], F.Copy, ["QL%d" % h, "WF6"], ["QE%d" % h], scale=ECOL)
                tt(T.QR[:, a:b], far[:, 0:WX].indirect(yl), T.CR[:, a:b], A.mult, [fk, "YU", "CR"], ["QR%d" % h])
                ts(T.QO[:, a:b], T.QL[:, a:b], OCOL, A.mult, ["QL%d" % h, "WF5"], ["QO%d" % h])
            if m == 0:
                last_constants()

            def unit(gr, h, b, c):
                qa, qk = (T.QE, "QE%d" % h) if gr % 2 == 0 else (T.QO, "QO%d" % h)
                p0 = 32 * (gr // 2)
                return mm(b[:, c:c + 128 + 128 * h], qa[p0:p0 + 32, 128 * h:128 * h + 128], T.QR[p0:p0 + 32, 0:128 + 128 * h], True, True)

            def reduce(gr, h, b, bk, c, vec):
                src = b[:, c:c + 128 + 128 * h]
                o = T.FL[:, 8 * h + gr:8 * h + gr + 1]
                if vec:
                    op("v", lambda: g.vector.tensor_reduce(o, src, AxisListType.X, A.max), [bk], ["FL%d_%d" % (gr, h)])
                else:
                    j = 128 * (gr - 4) if h == 0 else 512 + 256 * (gr - 5)
                    act(T.JK[:, j:j + 128 + 128 * h], src, F.Relu, [bk], ["JK%d_%d" % (gr, h), "FL%d_%d" % (gr, h)], bias=-1536.0, accum_out=o)

            def unpaired(h):
                tt(T.E2[:, 128 * h:128 * h + 128], T.FL[:, 8 * h:8 * h + 8].indirect(T.LX2[:, 8 * h:8 * h + 8]), T.TH2[:, 128 * h:128 * h + 128], A.is_gt,
                   ["FL%d_%d" % (i, h) for i in range(8)] + ["LX2", "TH2"], ["E2_%d" % h])

            for i, (ga, gb) in enumerate(((4, 5), (0, 1), (6, 7), (2, 3))):
                b, bk = BANKS[i], "G%d" % i
                op("p", [unit(ga, 0, b, 0), unit(gb, 0, b, 128)], ["QE0", "QO0", "QR0"], [bk])
                reduce(ga, 0, b, bk, 0, ga < 4)
                reduce(gb, 0, b, bk, 128, gb < 4)
            tt(T.TT[:], T.X[:, 0:WX].indirect(T.YU[:]), T.SH[:], A.add, ["X", "YU", "SH"], ["TT"])
            ns = T.NSND[:, 256 * m:256 * m + 256]
            for n, gr in enumerate((5, 0, 6, 1, 7, 2, 3, 4)):
                b, bk = BANKS[(4 + n) % 6], "G%d" % ((4 + n) % 6)
                op("p", unit(gr, 1, b, 0), ["QE1" if gr % 2 == 0 else "QO1", "QR0", "QR1"], [bk])
                reduce(gr, 1, b, bk, 0, gr < 5)
                if n == 0:
                    act(T.T2[:], T.TT[:], F.Copy, ["TT"], ["T2"], scale=0.5, bias=8388608.0)
                    act(ns, T.T2[:], F.Copy, ["T2"], ["NSND%d" % m], bias=-8388608.0)
                    if not tail:
                        send(to, "n%d%d" % (t, d), T.NLAND[:, 256 * m:256 * m + 256], ns, ["NSND%d" % m])
                if n == 1:
                    unpaired(0)
                if not tail:
                    f4, f4k = (T.FB4C, "FB4C") if d == 0 else (T.FB4, "FB4")
                    if n == 3:
                        tt(T.L1[:], T.K6[:, 64:128], f4[:], A.min, ["K6", f4k], ["L1"])
                    if n == 5:
                        tt(T.L2[:], T.K6[:, 0:64], T.L1[:], A.min, ["K6", "L1"], ["L2"])
                    if n == 6:
                        ts(T.LAST[:], T.L2[:], 4095, A.bitwise_and, ["L2"], ["LAST"])
                    if n == 7 and d == 0:
                        ts(T.FB4[:], T.LAST[:], BAR, A.add, ["LAST"], ["FB4"])
            unpaired(1)
            fs = []
            for h in range(2):
                fs.append(mm(T.C7[:, 64 + 8 * h:72 + 8 * h], T.E2[:, 128 * h:128 * h + 128], RH, True, False))
                fs.append(mm(T.C7[:, 64 + 8 * h:72 + 8 * h], T.E2[:, 128 * h:128 * h + 128], RL0 if h == 0 else RL1, False, True))
            op("p", fs, ["E2_0", "E2_1", "RH", "RL0", "RL1"], ["C7"])
            if m == ND * NB - 2:
                dma("y", [(T.PG4[:, 0:256], T.TA[15:128:16, 0:W]), (T.PG4[:, 256:512], T.TA[14:128:16, 0:W])], ["TA"], ["PG4n"])
                ts(T.CB[:], T.PG4[:, 0:256], 16.0, A.mult, ["PG4n"], ["CB"], -1.0, A.add)
                tt(T.PF[:, 0:256], T.CB[:], T.PG4[:, 256:512], A.add, ["CB", "PG4n"], ["YA0"])
            act(T.UP[:], far[:, 0:WX].indirect(T.YU[:]), F.Copy, [fk, "YU"], ["UP"])
            tt(T.LF[:], T.C7[:, 64:80], T.YQ[:], A.max, ["C7", "YQ"], ["LF"])
            ls = T.LSND[:, 16 * m:16 * m + 16]
            lk = "LSND%d" % m
            cp(ls, T.LF[:], ["LF"], [lk])
            if not tail:
                send(to, "l%d%d" % (t, d), T.LLAND[:, 16 * m:16 * m + 16], ls, [lk])
            if tail:
                cp(T.X[:, 0:WX].indirect(ls), ns, [lk, "NSND%d" % m], ["X"])
                if t + 1 < NB:
                    start_batch(t + 1)
            ts(T.WB[:], T.LF[:], float(DUM), A.is_lt, ["LF"], ["WB"])
            if not (tail and t + 1 == NB):
                op("p", mm(T.G0[:, 0:16], T.ONES[:], T.WB[:], True, True), ["ONES", "WB"], ["G0"])
            if tail:
                for r in result:
                    r()
                near_send(t)
            tt(far[:, 0:WX].indirect(ls), T.UP[:], T.RC[:], A.max, ["UP", "RC", lk], [fk])
            if not tail:
                act(T.PG[:], far[:, 0:WX].indirect(T.YU[:]), F.Copy, [fk, "YU"], ["PG"])
                cp(T.X[:, 0:WX].indirect(ls), ns, [lk, "NSND%d" % m], ["X"])
            if not (tail and t + 1 == NB):
                op("v", lambda: g.vector.tensor_reduce(T.KP[:, 0:1], T.G0[:, 0:16], AxisListType.X, A.add), ["G0"], ["KP0"])
                k1 = lambda: cp(T.KI[:, 0:1], T.KP[:, 0:1], ["KP0"], ["KI0"])
                k2 = lambda: ts(T.KI[:, 1:2], T.KI[:, 0:1], 31, A.bitwise_and, ["KI0"], ["KI1"])
                if not tail:
                    row_to_list(T.PG[:], SRP, ["PG", "SRP"], T.G2, "G2",
                                lambda ap: ts(T.PU[:], ap, -1.0, A.add, ["SC"], ["PU"]), k1, k2)
                else:
                    row_to_list(far[:, t + 1:W:16], T.SR14[:], [fk, "SR14"], T.G3, "G3", dead_done(t + 1), k1, k2)
                ts(T.KP[:, 1:2], T.KI[:, 1:2], 32.0, A.mult, ["KI1"], ["KP1"])
                ts(T.ACOL[:], T.ABASE[:], T.KP[:, 1:2], A.add, ["ABASE", "KP1"], ["ACOL"], 3104.0 * ((d + 1) % ND), A.add)
    dma("y", [(T.yx[:], T.X[:, 0:W])], ["X"], ["yx"])

    dma("y", [(T.PG4[:, 0:256], T.TB[15:128:16, 0:W]), (T.PG4[:, 256:512], T.TB[14:128:16, 0:W])], ["TB", "YA0"], ["PG4f"])
    t = NB - 1
    landed(nxt if t % 2 == 0 else prv, "r%d" % t, ["RLAND%d" % t])
    tt(T.E1[:], T.RLAND[:, 32 * t:32 * t + 16].indirect(T.LX5[:, 0:8]), T.GBH[:], A.mult, ["RLAND%d" % t, "LX5", "GBH"], ["E1"])
    op("p", mm(T.G4[:, 0:16], T.E1[:], T.DIAG[:, 0:16], True, True), ["E1", "DIAG"], ["G4"])
    ts(T.CB[:], T.PG4[:, 0:256], 16.0, A.mult, ["PG4f"], ["CB"], -1.0, A.add)
    tt(T.PF[:, 256:512], T.CB[:], T.PG4[:, 256:512], A.add, ["CB", "PG4f"], ["YB0"])
    tt(T.PF[:, t:256:16], T.G4[:, 0:16], T.PF[:, t:256:16], A.add, ["G4", "YA0"], ["YA0"])
    dma("y", [(T.yb[:], T.PF[:, 256:512])], ["YB0"], ["yb"])
    dma("y", [(T.ya[:], T.PF[:, 0:256])], ["YA0"], ["ya"])
    for sem in sorted(last):
        need("g", {sem: last[sem]})
